import numpy as np, ml_dtypes
CORES = [6,15,38,47]
N = 4
BF = ml_dtypes.bfloat16
W, U, SH, B, T, DEL, LIM = 4096, 1024, 2, 256, 8, 4, 16
def parts(rng):
    return (rng.integers(0, 64, (N, 8, 16, W)), rng.integers(0, W, (N, 8, 16, U)), rng.integers(0, W, (N, 8, 16, B)), rng.integers(0, W, (N, 8, B)), rng.integers(0, 64, (N, 8, 16, B)))
def pack(x, canal, trail, cut, z):
    return {"x": x.reshape(N, 128, W).astype(np.float32).astype(BF), "canal": np.ascontiguousarray(canal.reshape(N, 128, U)).astype(np.int32), "trail": np.ascontiguousarray(trail.reshape(N, 128, B)).astype(np.int32),
            "cut": np.ascontiguousarray(cut).astype(np.int32), "z": z.reshape(N, 128, B).astype(np.float32).astype(BF)}
def setup_inputs(rng):
    return pack(*parts(rng))
def setup_inputs_spread(rng):
    def low(*shape): return np.minimum((W * rng.random(shape) ** 3).astype(np.int64), W - 1)
    def size(n): return np.minimum((64.0 ** rng.random((N, 8, 1, n)) * rng.random((N, 8, 16, n))).astype(np.int64), 63)
    return pack(size(W), low(N, 8, 16, U), low(N, 8, 16, B), low(N, 8, B), size(B))
def tips(rng, *shape):
    q = rng.random(shape)
    return np.where(q < 0.36, 0, np.where(q < 0.72, W - 1, rng.integers(0, W, shape)))
def setup_inputs_ends(rng):
    k = rng.random((N, 8, 1, W)); x = np.where(k < 0.2, 0, np.where(k < 0.4, 63, 63 * rng.integers(0, 2, (N, 8, 16, W))))
    one = (np.arange(16).reshape(1, 1, 16, 1) == rng.integers(0, 16, (N, 8, 1, W))) & (rng.random((N, 8, 1, W)) < 0.15)
    x = np.where(one, np.where(x == 63, 62, 1), x)
    for q in (1, N - 1): x[q] = np.where(rng.random((8, 1, W)) < 0.3, 32 + LIM + rng.integers(0, 3, (8, 1, W)), x[q])
    k = rng.random((N, 8, 1, B)); z = np.where(k < 0.3, 0, np.where(k < 0.45, 63, 63 * rng.integers(0, 2, (N, 8, 16, B))))
    for q in (0, 1, N - 1): z[q] = np.repeat(63 * rng.integers(0, 2, (8, 1, B)), 16, axis=1)
    z[:, :, :, B - 1] = 0
    canal, trail, cut = tips(rng, N, 8, 16, U), tips(rng, N, 8, 16, B), tips(rng, N, 8, B); cut[:, :, B - 1] = W - 1
    for r in range(N):
        for g in range(8):
            a = 2 * int(rng.integers(W // 8, W // 4)); b = a - 1; rows = rng.permutation(15)[:2]
            x[r, g, :, 0] = 0 if r in (0, 1, N - 1) else 63 * ((r + g) % 2)
            x[r, g, :, W - 1] = 63; x[r, g, :, a] = 63; x[r, g, :, b] = 63; x[r, g, int(rng.integers(0, 16)), b] = 62
            canal[r, g, :, U - 1] = W - 1; canal[r, g, rows[0], U - 1] = a; canal[r, g, rows[1], U - 1] = b
    w = 16 - DEL
    for q in (1, N - 1): trail[q, :, w] = np.where(z[q, :, 0] == 0, W - 1, 0)
    trail[1, 0, w, 0] = W - 1 - trail[1, 0, w, 0]
    trail[0, :, w] = np.where(z[0, :, 0] == 0, 0, W - 1)
    for q in range(2, N - 1):
        trail[q, 7, w] = np.where((trail[q, 7, w] >> SH) == U - 1, 0, trail[q, 7, w]); trail[q, 7, w, B - 1] = W - 1
    return pack(x, canal, trail, cut, z)
def setup_inputs_corners(rng):
    x, canal, trail, cut, z = parts(rng); s = int(rng.integers(0, 8)); H = 1 << SH
    for r in range(N):
        for g in range(8):
            kind = (r + g + s) % 8
            if kind == 0: cut[r, g] = (0, W - 1, int(rng.integers(0, W)))[r % 3]
            if kind == 1:
                u = rng.integers(0, U, (16, 1)); u[16 - DEL] = U - 1; u[17 - DEL if DEL > 1 else 0] = 0
                trail[r, g] = (u << SH) + rng.integers(0, H, (16, B))
            if kind == 2: trail[r, g] = (np.argsort(rng.random((16, U)), axis=1)[:, :B] << SH) + rng.integers(0, H, (16, B))
            if kind == 3:
                canal[r, g] = (np.arange(U)[None, :] << SH) + rng.integers(0, H, (16, U))
                cut[r, g] = rng.permutation(W)[:B]; trail[r, g] = cut[r, g][None, :]
            if kind == 4: x[r, g] = 30 + rng.integers(0, 4, (16, W)); z[r, g] = 30 + rng.integers(0, 4, (16, B))
            if kind == 5: x[r, g] = rng.integers(0, 4, (16, W)); z[r, g] = rng.integers(60, 64, (16, B))
            if kind == 6:
                at = np.argsort(rng.random((16, W)), axis=0); n = rng.integers(8, 10, (1, W)); sg = 2 * rng.integers(0, 2, (16, W)) - 1
                x[r, g] = 24 + sg * np.where(at < n, LIM + 1, LIM); z[r, g] = 24
            if kind == 7:
                x[r, g] = rng.integers(60, 64, (16, 4))[:, rng.integers(0, 4, W)]
                canal[r, g] = -np.sort(-canal[r, g], axis=0); canal[r, g, :, ::5] = canal[r, g, :1, ::5]
    return pack(x, canal, trail, cut, z)
def setup_inputs_full(rng):
    x, canal, trail, cut, z = parts(rng); w = 16 - DEL; w1 = (17 - DEL) % 16; H = 1 << SH; q = B // 4
    for r in range(N):
        for g in range(8):
            v = rng.integers(0, 64, W); y = np.full(B, 16); l = canal[r, g]; h = trail[r, g]
            if r == 0:
                h[w] = (rng.permutation(U)[:B] << SH) + rng.integers(0, H, B); v[h[w]] = rng.integers(40, 59, B)
            elif r == 1:
                o = rng.permutation(W - H); best = o[:B]; low = o[B:]
                v = rng.integers(0, 21, W); v[best] = rng.integers(25, 33, B)
                u = rng.permutation(U)[:B]; cut[r, g] = (u << SH) + rng.integers(0, H, B)
                l[:] = low[rng.integers(0, len(low), (16, U))]; l[rng.integers(0, 16, B), u] = best
                h[:] = rng.integers(0, W - H, (16, B))
                h[w, :B - 1] = (rng.permutation(U - 1)[:B - 1] << SH) + rng.integers(0, H, B - 1); h[w, B - 1] = W - 1
            elif r == 2:
                a = np.flatnonzero((v >= 16) & (v <= 32)); h[w] = a[rng.integers(0, len(a), B)]; h[w1] = a[rng.integers(0, len(a), B)]
                if g in (0, 3, 7):
                    far = np.flatnonzero(v >= 40); i = 0 if g == 0 else B - 1 if g == 7 else int(rng.integers(0, B))
                    h[w, i] = far[int(rng.integers(0, len(far)))]
            else:
                v = rng.integers(0, 63, W); v[0] = 63; v[W - 1] = 63
                y = rng.integers(0, 64, B); i = rng.permutation(B); u = rng.permutation(U - 1)[:2 * q]
                y[i[:q]] = 63; y[i[q:2 * q]] = 0; cut[r, g, i[:2 * q]] = (u << SH) + rng.integers(0, H, 2 * q)
                l[:, u[:q]] = W - 1; l[:, u[q:]] = rng.integers(1, W - 1, (16, q))
                l[rng.integers(0, 2, q), u[q:]] = 0; l[rng.integers(13, 16, q), u[q:]] = W - 1
            x[r, g] = v; z[r, g] = y
            if r > 2: x[r, g, int(rng.integers(0, 16)), 0] = 62
    return pack(x, canal, trail, cut, z)
def setup_inputs_meet(rng):
    x, canal, trail, cut, z = parts(rng)
    for r in range(N):
        for g in range(8):
            s = rng.permutation(W)[:64]; s[0] = W - 1
            canal[r, g] = s[rng.integers(0, 64, (16, U))]; trail[r, g] = s[rng.integers(0, 64, (16, B))]; cut[r, g] = s[rng.integers(0, 64, B)]
    return pack(x, canal, trail, cut, z)
def check_inputs(d):
    bad = []
    for k, hi in (("x", 63), ("canal", W - 1), ("trail", W - 1), ("cut", W - 1), ("z", 63)):
        a = np.asarray(d[k]).astype(np.float64)
        if not (np.min(a) >= 0 and np.max(a) <= hi): bad.append("range of " + k)
        if not np.all(a == np.floor(a)): bad.append("whole numbers in " + k)
    return bad
def reference(x, canal, trail, cut, z):
    X = x.astype(np.float32).astype(np.int64).reshape(N, 8, 16, W); C = canal.astype(np.int64).reshape(N, 8, 16, U); G = trail.astype(np.int64).reshape(N, 8, 16, B)
    V = cut.astype(np.int64).reshape(N, 8, B); Z = z.astype(np.float32).astype(np.int64).reshape(N, 8, 16, B); skips = np.zeros(N, np.int64)
    for t in range(T):
        lim = LIM + (skips & 3); skips = np.zeros(N, np.int64); come = np.zeros_like(Z); row = (t + 16 - DEL) % 16
        for r in range(N):
            for g in range(8):
                a, l, h, q = X[r, g], C[r, g], G[r, g], Z[r, g]
                k = l[:, V[r, g] >> SH]
                score = np.add.reduce(np.maximum(a[:, k] - q[:, None, :], 0), axis=0)
                c = np.min(np.where(score == np.max(score, axis=0), k, W), axis=0)
                cut_off = np.sum(np.abs(a[:, h] - q[:, None, :]) > lim[r], axis=0) >= 9
                w = h[row] + 0; skip = cut_off[row]; xw = a[:, w]; xc = a[:, c]
                first = np.zeros(B, bool); first[np.unique(w >> SH, return_index=True)[1]] = True
                new = np.where(skip, np.minimum(xw + 4, 63), (xw + q) >> 1)
                a[:, w[first]] = new[:, first]
                m = first & ~skip; u = w[m] >> SH
                l[:, u] = np.where(cut_off[:, m], l[:, u], h[:, m])
                h[:] = np.where(cut_off, k, h); h[t] = c
                a[:, c] = xc >> 1
                V[r, g] = c; skips[r] += np.sum(skip)
                come[(r + 1 + t % (N - 1)) % N, g] = (q + xc) >> 1
        Z = come
    return {"yx": X.reshape(N, 128, W).astype(np.float32).astype(BF), "yl": C.reshape(N, 128, U).astype(np.float32), "yg": G.reshape(N, 128, B).astype(np.float32)}

@@ -1,0 +1,510 @@
+from concourse.mybir import AluOpType, AxisListType, ActivationFunctionType
+
+A = AluOpType
+AF = ActivationFunctionType
+NT = 8
+BIAS = 160.0
+XW = 6144
+CW = 1536
+
+F4, BF, HF, I4, U2 = "float32", "bfloat16", "float16", "int32", "uint16"
+SCRATCH = {}
+for _n, _s, _d in (
+        ("X", XW, BF), ("CAN", CW, F4), ("cin", 1024, I4), ("tin", 256, I4), ("vin", 256, I4),
+        ("xg0", 4096, BF), ("xg1", 4096, BF), ("ab", 4096, BF), ("th", 4096, BF), ("zrep", 4096, BF), ("sc", 4096, BF),
+        ("lo", 1024, F4), ("go", 256, F4), ("eqw", 3072, BF), ("eqc", 3072, BF), ("df", 3072, BF), ("wrow", 2048, HF), ("wall", 2048, HF),
+        ("sco", 256, F4), ("q1", 16, I4), ("q2", 16, I4), ("UW", 256, HF), ("SPs", 256, HF), ("LwU", 32, F4),
+        ("nw", 16, F4), ("n1w", 16, F4), ("nc", 16, F4), ("n1c", 16, F4), ("A1", 256, HF), ("A2c", 256, HF), ("A2w", 256, HF),
+        ("ufw", 16, HF), ("uf", 16, HF), ("xs", 256, HF), ("xw", 256, BF), ("r2", 256, BF), ("r2m", 256, BF),
+        ("rn", 256, BF), ("cw", 256, F4), ("cm", 256, F4), ("cn", 256, F4), ("gm", 256, HF), ("sevL", 256, BF), ("sevT", 256, BF),
+        ("skrep", 256, BF), ("sf", 1, F4), ("si", 1, HF), ("sj", 16, F4), ("lim", 8, F4),
+        ("Z", 256 * NT, BF), ("ZS", 256 * NT, BF),
+        ("i128", 128, F4), ("pc", 1, F4), ("pci", 1, I4), ("pg", 1, F4), ("pk", 1, F4), ("p16", 1, F4),
+        ("rc", 1, F4), ("k272", 272, F4), ("w144", 144, F4), ("v1", 256, F4), ("zli", 256, I4),
+        ("skli", 128, I4), ("zl", 256, U2), ("skl", 128, U2), ("RM", 16, F4), ("RM1", 16, F4), ("RM2", 16, F4), ("RMn", 16, F4),
+        ("I16", 128, HF), ("I8n", 128, BF), ("I8p", 128, BF), ("Ib", 128, BF), ("Ibn", 128, BF), ("Ih", 128, BF), ("I5n", 128, BF),
+        ("It", 1024, HF), ("blkf", 8, F4), ("blk1", 8, HF), ("blkb", 8, BF), ("blkS", 8, BF), ("onesg", 1024, HF), ("ones16", 256, HF),
+        ("onesb", 128, BF), ("qtr", 128, HF), ("dmask", 256, HF), ("in1c", 256, HF), ("selk", 64, HF), ("wide", 144, HF),
+        ("thrk", 272, F4), ("resetv", 256, F4), ("wtf", 1, F4), ("wt", 1, BF), ("wbig", 1, BF), ("thr", 1, F4)):
+    SCRATCH[_n] = ("sbuf", [128, _s], _d)
+for _k in range(2):
+    for _n, _s, _d in (("Kn", 256, HF), ("Ku", 256, U2), ("Gn", 256, HF), ("Gu", 256, U2), ("cutv", 256, BF), ("Lc", 16, F4),
+                       ("cu", 16, U2), ("vl", 16, U2), ("dwu", 16, U2), ("dwl", 16, U2), ("dcu", 16, U2)):
+        SCRATCH["%s%d" % (_n, _k)] = ("sbuf", [128, _s], _d)
+for _k in range(8):
+    SCRATCH["ps%d" % _k] = ("psum", [128, 512], F4)
+
+SEMAPHORES = (["qv", "qs", "qt", "qg"] + ["ld_" + n for n in ("cut", "z", "trail", "canal", "x0", "x1", "x2", "x3")]
+              + ["st_" + n for n in ("o0", "o1", "o2", "o3", "ol", "og")] + ["row%d" % k for k in range(NT)]
+              + ["arr%d" % k for k in range(1, NT)] + ["snt%d" % k for k in range(1, NT)])
+
+CY, GA, PEC, SYNC = 0.00083, 1.5, 0.0006, 0.1
+BONUS = {'cn_v': 1.5, 'dwu_v': 3, 'cnt_t': -1.5, 'zs_v': -1.5, 'nw_v': -0.7, 'SPs_v': 0.7, 'BCc_t': -6, 'sevL_v': 3, 'Aw_v': -1.5,
+         'd_t': -3, 'X_v': -6, 'gm_v': -3, 'eqc_v': -3, 'N_t': -6, 'vl_v': -1.5, 'UW_v': -1.5, 'wrow_y': 1.5, 'th_v': -0.7, 'lim_v': 6,
+         'A_v': 6, 'Gu_v': -3, 'sc_v': 3, 'sco_v': 3, 'ab_s': 3, 'eqw_v': 3, 'xw_s': -0.7, 'Ku_v': 3, 'cw_v': 3, 'r_v': -3,
+         'zrep_s': -1.5, 'si_v': -6, 'uf_v': -0.7, 'Ibn_v': 6, 'SP_t': 3, 'cm_v': 1.5, 'cw_s': 0.7, 'rn_v': 6, 'lo_v': 3, 'CAN_v': -3,
+         'R_t': -3, 'xg_s': -3, 'Ww_t': 3, 'Ac_v': -3, 'Lc_v': 0.7, 'nc_v': 6, 'Z_x': -0.7, 'S_t': -3, 'sf_s': -1.5, 'cu_v': -0.7,
+         'wall_g': -3, 'Gn_v': -3, 'key_t': 0.7, 'dwl_v': 1.5, 'Wc_t': 0.7, 'cutv_s': -3, 'Z_v': -3, 'q_v': -1.5, 'EQw_t': 3,
+         'EQc_t': -1.5, 'cW_t': 6, 'rm_v': 1.5, 'df_s': 0.7, 'sevT_v': 3, 'way_g': -3, 'xs_v': 0.7, 'G_t': -3}
+EA = (0, 1, 2)
+
+
+def dv(n): return 0.06 + n * CY
+def dh(n): return 0.06 + max(n * 0.5, 64) * CY
+def dg(n): return 0.05 + n * GA * CY
+def ds(n): return 0.05 + n * 3.5 * CY
+def sg(n): return 0.065 + n * GA * CY
+def sa(n): return 0.065 + n * CY
+def pe(*ns): return sum(max(64, n) for n in ns) * PEC + 0.02
+
+
+def rank_program(g, core, T, topo):
+    rank = T.rank_of(core)
+    if rank is None:
+        return
+    V, S, PE, Y = g.vector, g.scalar, g.tensor, g.sync
+    ops = []
+
+    def op(eng, cost, calls, R=(), W=(), tile=None, lat=0.0, sem=None, cnt=0):
+        ops.append({"e": eng, "c": cost, "f": calls, "R": list(R), "W": list(W), "tile": tile, "lat": lat,
+                    "sem": sem, "cnt": cnt, "i": len(ops)})
+
+    def v(cost, f, R, W): op("v", cost, [f], R, W)
+    def s(cost, f, R, W): op("s", cost, [f], R, W)
+    def vp(cost, f, tile, R, W): op("v", cost, lambda B: [lambda: f(B)], R, W, tile=tile)
+    mm = PE.matmul
+
+    def ts(out, i0, s1, s2, o0, o1=None):
+        if o1 is None:
+            return V.tensor_scalar(out, i0, s1, None, o0)
+        return V.tensor_scalar(out, i0, s1, s2, o0, o1)
+
+    def load(name, out, src, W, lat, R=()):
+        op("y", 0.1, [lambda: Y.dma_start(out, src)], R, W, lat=lat, sem="ld_" + name, cnt=16)
+
+    v(dv(256), lambda: V.memset(T.vin[:], 0), [], ["vin"])
+    v(dh(2048), lambda: V.memset(T.X[:, 4096:XW], BIAS), [], ["Xd"])
+    v(dv(512), lambda: V.memset(T.CAN[:, 1024:CW], 0.0), [], ["CANd"])
+    load("z", T.xw[:], T.z[:], ["xw"], 2.0)
+    load("trail", T.tin[:], T.trail[:], ["tin"], 2.2)
+    load("canal", T.cin[:], T.canal[:], ["cin"], 4.0)
+    for q in range(4):
+        load("x%d" % q, T.X[:, 1024 * q:1024 * q + 1024], T.x[:, 1024 * q:1024 * q + 1024], ["X%d" % q], 4.0 + q)
+    load("cut", T.vin[0:128:16, :], T.cut[:], ["vin2"], 2.0, ["vin"])
+    XC = ["X0", "X1", "X2", "X3"]
+    XR = XC + ["Xd"]
+
+    def iota(name, out, pat, base, cm, f=True):
+        n = 1
+        for a, b in pat:
+            n *= b
+        kw = {"allow_small_or_imprecise_dtypes": True} if f else {}
+        op("g", 0.13 + 2 * n * CY, [lambda: g.iota(out, pat, base, cm, **kw)], [], [name])
+
+    iota("pci", T.pci[:], [[0, 1]], 0, 1, False)
+    iota("pc", T.pc[:], [[0, 1]], 0, 1)
+    iota("i128", T.i128[:], [[1, 128]], 0, 0)
+    iota("k272", T.k272[:], [[0, 17], [1, 16]], 0, 0)
+    iota("zli", T.zli[:], [[1, 256]], 0, 0, False)
+    iota("v1", T.v1[:], [[-1024, 2], [0, 128]], -2052, -8)
+    iota("w144", T.w144[:], [[1, 144]], -15, 0)
+    iota("sklia", T.skli[:, 0:64], [[1, 4], [16, 16]], 12, 0, False)
+    iota("sklib", T.skli[:, 64:128], [[1, 4], [16, 16]], 0, 0, False)
+    one = dv(64)
+    v(one, lambda: ts(T.q1[:, 0:1], T.pci[:], 4, None, A.arith_shift_right), ["pci"], ["q1"])
+    v(one, lambda: ts(T.q2[:, 0:1], T.pci[:], 15, None, A.bitwise_and), ["pci"], ["q2"])
+    v(one, lambda: V.tensor_copy(T.pg[:], T.q1[:, 0:1]), ["q1"], ["pg"])
+    v(one, lambda: V.tensor_copy(T.pk[:], T.q2[:, 0:1]), ["q2"], ["pk"])
+    v(one, lambda: ts(T.p16[:], T.pg[:], 16.0, None, A.mult), ["pg"], ["p16"])
+    v(one, lambda: ts(T.rc[:], T.pk[:], 0.0, 2048.0, A.is_equal, A.mult), ["pk"], ["rc"])
+    v(one, lambda: ts(T.RM[:], T.i128[:, 0:16], T.pk[:], None, A.is_equal), ["i128", "pk"], ["RM"])
+    v(one, lambda: ts(T.RM1[:], T.RM[:], 0.25, None, A.mult), ["RM"], ["RM1"])
+    v(one, lambda: ts(T.RM2[:], T.RM[:], 1536.375, None, A.mult), ["RM"], ["RM2"])
+    v(one, lambda: ts(T.RMn[:], T.RM[:], -1.0, 1.0, A.mult, A.add), ["RM"], ["RMn"])
+    for name, val in (("I16", 1.0), ("Ib", 1.0), ("Ibn", -1.0), ("I8n", -8192.0), ("I8p", 8192.0), ("Ih", 0.5), ("I5n", -512.0)):
+        v(dv(128), lambda name=name, val=val: ts(T[name][:], T.i128[:], T.pc[:], val, A.is_equal, A.mult), ["i128", "pc"], [name])
+    for name, val in (("blkf", 1.0), ("blk1", 1.0), ("blkb", 1.0), ("blkS", 4096.0)):
+        v(one, lambda name=name, val=val: ts(T[name][:], T.i128[:, 0:8], T.pg[:], val, A.is_equal, A.mult), ["i128", "pg"], [name])
+    v(dv(256), lambda: ts(T.ones16[:], T.k272[:, 0:256], 0.0, 1.0, A.mult, A.add), ["k272"], ["ones16"])
+    v(dh(128), lambda: V.memset(T.onesb[:], 1.0), [], ["onesb"])
+    v(dh(128), lambda: ts(T.qtr[:], T.ones16[:, 0:128], -0.25 / 128, None, A.mult), ["ones16"], ["qtr"])
+    v(one, lambda: V.memset(T.wbig[:], float(2.0 ** 90)), [], ["wbig"])
+    v(one, lambda: V.memset(T.lim[:, 0:1], 16.0), [], ["lim0"])
+    op("v", 8 * dh(128), [lambda k=k: ts(T.onesg[:, 128 * k:128 * k + 128], T.ones16[:, 0:128], T.blkf[:, k:k + 1], None, A.mult)
+                          for k in range(8)], ["ones16", "blkf"], ["onesg"])
+    v(dv(256), lambda: ts(T.dmask[:], T.k272[:, 0:256], T.pk[:], None, A.is_equal), ["k272", "pk"], ["dmask"])
+    v(dv(256), lambda: ts(T.resetv[:], T.k272[:, 0:256], 0.0, -2.0e7, A.is_equal, A.mult), ["k272"], ["resetv"])
+    v(dv(272), lambda: ts(T.sco[:], T.v1[:], -4096.0, None, A.add), ["v1"], ["sco"])
+    v(dv(512), lambda: V.tensor_tensor(T.go[:], T.sco[:], T.dmask[:], A.mult), ["sco", "dmask"], ["go"])
+    v(dv(256), lambda: ts(T.in1c[:], T.go[:], 4096.0, None, A.add), ["go"], ["in1c"])
+    v(dv(272), lambda: ts(T.thrk[:], T.k272[:], 15.0, 100.0, A.is_equal, A.mult), ["k272"], ["thrk0"])
+    v(dv(272), lambda: ts(T.thrk[:], T.thrk[:], 8.5, None, A.add), ["thrk0"], ["thrk"])
+    v(dv(144), lambda: ts(T.wide[:], T.w144[:], T.p16[:], None, A.is_equal), ["w144", "p16"], ["wide"])
+    v(dv(256), lambda: V.tensor_copy(T.zl[:], T.zli[:]), ["zli"], ["zl"])
+    v(dv(128), lambda: V.tensor_copy(T.skl[:], T.skli[:]), ["sklia", "sklib"], ["skl"])
+    op("v", 8 * one, [lambda t=t: ts(T.selk[:, 8 * t:8 * t + 8], T.blkf[:], T.RM[:, (t + 12) % 16:(t + 12) % 16 + 1], None, A.mult)
+                      for t in range(NT)], ["blkf", "RM"], ["selk"])
+    op("v", 8 * dh(128), [lambda t=t: ts(T.It[:, 128 * t:128 * t + 128], T.I16[:], T.RMn[:, t:t + 1], None, A.mult)
+                          for t in range(NT)], ["I16", "RMn"], ["It"])
+    v(dv(128), lambda: V.memset(T.cm[:, 0:128], 0.5), [], ["cm"])
+    v(dv(128), lambda: V.memset(T.cn[:, 0:128], 0.0), [], ["cn"])
+    v(dv(128), lambda: V.tensor_tensor_scan(T.cw[:, 0:128], T.cm[:, 0:128], T.cn[:, 0:128], float(2.0 ** 64), A.mult, A.add), ["cm", "cn"], ["cw"])
+    v(dv(256), lambda: V.tensor_tensor(T.lo[:, 0:128], T.cw[:, 0:128], T.I16[:], A.mult), ["cw", "I16"], ["lo"])
+    v(dv(128), lambda: V.tensor_reduce(T.wtf[:], T.lo[:, 0:128], AxisListType.X, A.add), ["lo"], ["wtf"])
+    v(one, lambda: V.tensor_copy(T.wt[:], T.wtf[:]), ["wtf"], ["wt"])
+    v(one, lambda: ts(T.thr[:], T.wtf[:], 2.5, None, A.mult), ["wtf"], ["thr"])
+
+    v(dv(256), lambda: ts(T.UW[:], T.vin[:], -1.0, T.rc[:], A.mult, A.add), ["vin", "vin2", "rc"], ["UW"])
+    v(dv(256), lambda: ts(T.Gn0[:], T.tin[:], -1.0, 2048.0, A.mult, A.add), ["tin"], ["Gn0"])
+    v(dv(256), lambda: V.tensor_copy(T.Gu0[:], T.tin[:]), ["tin"], ["Gu0"])
+    v(dh(256), lambda: ts(T.Z[:, 0:256], T.xw[:], BIAS, None, A.add), ["xw"], ["Z0"])
+    v(dv(1024), lambda: ts(T.CAN[:, 0:1024], T.cin[:], -1.0, 2048.0, A.mult, A.add), ["cin"], ["CAN"])
+    for q in range(4):
+        v(dh(1024), lambda q=q: ts(T.X[:, 1024 * q:1024 * q + 1024], T.X[:, 1024 * q:1024 * q + 1024], BIAS, None, A.add),
+          ["X%d" % q], ["X%d" % q])
+
+    def halves(src, rhs):
+        return lambda B: [lambda h=h: mm(B[:, 8 * h:8 * h + 8], T[src][:, 128 * h:128 * h + 128], rhs, True, True) for h in range(2)]
+
+    def spread_lists(key, tname):
+        op("t", pe(64, 64), halves(key, T.blk1[:]), [key, "blk1"], [], tile=tname)
+
+    def same(t, tag, src, col0, Lname, eq, pb):
+        k0 = (t + 12) % 16
+        if pb:
+            op("y", 0.1, [lambda: Y.dma_start(T.wrow[0:1, :], T[src][k0:128:16, :])], [src], ["wrow"], lat=2.0, sem="row%d" % t, cnt=16)
+            op("g", 0.14 + 4 * 2048 * CY, [lambda: g.partition_broadcast(T.wall[:], T.wrow[0:1, :], 128)], ["wrow"], ["wall"])
+        for b in range(4):
+            ks = (2 * b, 2 * b + 1)
+
+            def cmp(W, off, k, h):
+                return lambda: ts(T[eq][:, 384 * k + 256 * h:384 * k + 256 + 128 * h], W[:, off + 128 * h:off + 256],
+                                  T[Lname][:, col0 + 8 * h + k:col0 + 8 * h + k + 1], None, A.is_equal)
+
+            def dist(B, k, h):
+                return lambda: S.activation(T.df[:, 384 * k + 256 * h:384 * k + 256 + 128 * h], B[:, 256 * (k % 2) + 128 * h:256 * (k % 2) + 256],
+                                            AF.Abs, bias=T[Lname][:, col0 + 8 * h + k:col0 + 8 * h + k + 1], scale=-1.0)
+            if pb:
+                op("v", 2 * dh(256) + 2 * dh(128), [cmp(T.wall, 256 * k, k, h) for k in ks for h in range(2)], [Lname, "wall"], ["%s_%d" % (eq, b)])
+                continue
+            tn = "BC%s%d_%d" % (tag, t, b)
+            op("t", pe(256, 256), lambda B, ks=ks: [lambda k=k: mm(B[:, 256 * (k % 2):256 * (k % 2) + 256], T.onesg[:, 128 * k:128 * k + 128],
+               T[src][:], True, True) for k in ks], [src, "onesg"], [], tile=tn)
+            if b in EA:
+                op("s", 2 * sa(256) + 2 * sa(128), lambda B, ks=ks, dist=dist: [dist(B, k, h) for k in ks for h in range(2)],
+                   [Lname], ["df_%d" % b], tile=tn)
+                v(dh(768), lambda b=b: ts(T[eq][:, 768 * b:768 * b + 768], T.df[:, 768 * b:768 * b + 768], 0.0, None, A.is_equal),
+                  ["df_%d" % b], ["%s_%d" % (eq, b)])
+            else:
+                op("v", 2 * dv(256) + 2 * dv(128), lambda B, ks=ks, cmp=cmp: [cmp(B, 256 * (k % 2), k, h) for k in ks for h in range(2)],
+                   [Lname], ["%s_%d" % (eq, b)], tile=tn)
+        tn = "EQ%s%d" % (tag, t)
+        for b in range(4):
+            def sums(B, b=b):
+                r = []
+                for k in (2 * b, 2 * b + 1):
+                    o = 384 * k
+                    r.append(lambda k=k, o=o: mm(B[:, k:k + 1], T[eq][:, o:o + 128], T.wt[:], True, True))
+                    r.append(lambda k=k, o=o: mm(B[:, 8 + k:9 + k], T[eq][:, o + 128:o + 256], T.wbig[:], True, False))
+                    r.append(lambda k=k, o=o: mm(B[:, 8 + k:9 + k], T[eq][:, o + 256:o + 384], T.wt[:], False, True))
+                return r
+            op("t", pe(64, 64, 64, 64, 64, 64), sums, ["%s_%d" % (eq, b), "wt", "wbig"], [], tile=tn)
+        return tn
+
+    def place(t, par, first):
+        v(dg(256), lambda: V.tensor_tensor(T.A1[:], T["Lc%d" % par][:, 0:16].indirect(T.zl[:, 0:16]), T.dmask[:], A.mult),
+          ["Lc%d" % par, "zl", "dmask"], ["A1"])
+        tn = "cW%d" % t
+        spread_lists("A1", tn)
+        if not first:
+            vp(one, lambda B: ts(T["cu%d" % par][:], B[:, 0:16], -1.0, 2048.0, A.mult, A.add), tn, [], ["cu%d" % par])
+        if t < NT - 1:
+            vp(one, lambda B: ts(T.uf[:], B[:, 0:16], 0.25, 1536.375, A.mult, A.add), tn, [], ["uf"])
+            v(one, lambda: ts(T["vl%d" % par][:], T.uf[:], -1.0, 2048.0, A.mult, A.add), ["uf"], ["vl%d" % par])
+
+    op("t", pe(64, 64), halves("UW", T.blk1[:]), ["UW", "blk1"], [], tile="cut0")
+    vp(one, lambda B: V.tensor_copy(T.Lc1[:], B[:, 0:16]), "cut0", [], ["Lc1"])
+    place(-1, 1, True)
+
+    def step(t):
+        p, q = t % 2, 1 - t % 2
+        last = t == NT - 1
+        k0 = (t + 12) % 16
+        Z, Kn, Ku, Gn, Gu, xg = "Z%d" % t, "Kn%d" % p, "Ku%d" % p, "Gn%d" % p, "Gu%d" % p, "xg%d" % p
+        Lc, cu, dcu, dwu, dwl, cutv = "Lc%d" % p, "cu%d" % p, "dcu%d" % p, "dwu%d" % p, "dwl%d" % p, "cutv%d" % p
+        Gn1, Gu1, vl = "Gn%d" % q, "Gu%d" % q, "vl%d" % q
+        z0, z1 = 256 * t, 256 * t + 256
+        v(dg(256), lambda: V.tensor_copy(T[Kn][:], T.CAN[:, 0:1024].indirect(T[vl][:])), ["CAN", vl], [Kn])
+        v(dh(256), lambda: ts(T[Ku][:], T[Kn][:], -1.0, 2048.0, A.mult, A.add), [Kn], [Ku])
+        for c in range(4):
+            s(sg(1024), lambda c=c: S.activation(T[xg][:, 1024 * c:1024 * c + 1024],
+              T.X[:, 0:4096].indirect(T[Gu][:, 64 * c:64 * c + 64]), AF.Copy), XC + [Gu], ["%s_%d" % (xg, c)])
+        v(dh(256), lambda: ts(T.UW[:], T[Gn][:], T.RM1[:, k0:k0 + 1], T.RM2[:, k0:k0 + 1], A.mult, A.add), [Gn, "RM1", "RM2"], ["UW"])
+
+        def callsL(B):
+            r = []
+            for h in range(2):
+                r.append(lambda h=h: mm(B[:, 8 * h:8 * h + 8], T[Gn][:, 128 * h:128 * h + 128], T.selk[:, 8 * t:8 * t + 8], True, True))
+                r.append(lambda h=h: mm(B[:, 16 + 8 * h:24 + 8 * h], T.UW[:, 128 * h:128 * h + 128], T.blk1[:], True, True))
+            return r
+        op("t", pe(64, 64, 64, 64), callsL, [Gn, "UW", "selk", "blk1"], [], tile="LwU%d" % t)
+        op("s", sa(32), lambda B: [lambda: S.activation(T.LwU[:], B[:, 0:32], AF.Copy)], [], ["LwU"], tile="LwU%d" % t)
+        tn = same(t, "w", "UW", 16, "LwU", "eqw", True)
+        vp(one, lambda B: ts(T.nw[:], B[:, 0:16], T.thr[:], -10000.0, A.is_gt, A.mult), tn, ["thr"], ["nw"])
+        v(one, lambda: V.tensor_tensor(T.n1w[:], T.nw[:], T.LwU[:, 0:16], A.add), ["nw", "LwU"], ["n1w"])
+        v(dg(256), lambda: V.tensor_tensor(T.A2w[:], T.n1w[:, 0:16].indirect(T.zl[:, 0:16]), T.in1c[:], A.max), ["n1w", "zl", "in1c"], ["A2w"])
+        spread_lists("A2w", "W2w%d" % t)
+        vp(one, lambda B: ts(T[dwu][:], B[:, 0:16], -1.0, 63488.0, A.mult, A.add), "W2w%d" % t, [], [dwu])
+        vp(one, lambda B: ts(T.ufw[:], B[:, 0:16], -0.25, 16896.625, A.mult, A.add), "W2w%d" % t, [], ["ufw"])
+        v(one, lambda: ts(T[dwl][:], T.ufw[:], -1025.0, None, A.add), ["ufw"], [dwl])
+        s(sg(256), lambda: S.activation(T.xw[:], T.X[:].indirect(T[dwu][:]), AF.Copy), XR + [dwu], ["xw"])
+        s(sg(256), lambda: S.activation(T.cw[:], T.CAN[:].indirect(T[dwl][:]), AF.Copy), ["CAN", "CANd", dwl], ["cw"])
+        v(dh(256), lambda: ts(T.r2[:], T.xw[:], 4.0, BIAS + 63.0, A.add, A.min), ["xw"], ["r2"])
+        for h in range(2):
+            s(sg(2048), lambda h=h: S.activation(T.zrep[:, 2048 * h:2048 * h + 2048], T.Z[:, z0:z1].indirect(T.zl[:, 128 * h:128 * h + 128]), AF.Copy),
+              [Z, "zl"], ["zrep%d" % h])
+        for h in range(2):
+            v(dg(2048), lambda h=h: V.tensor_tensor(T.sc[:, 2048 * h:2048 * h + 2048], T.X[:, 0:4096].indirect(T[Ku][:, 128 * h:128 * h + 128]),
+              T.zrep[:, 2048 * h:2048 * h + 2048], A.max), XC + [Ku, "zrep%d" % h], ["sc%d" % h])
+
+            def callsK(B, h=h):
+                r = [lambda: mm(B[:, 128 * h:128 * h + 128], T[Kn][:, 128 * h:128 * h + 128], T.I16[:], True, False)]
+                for k in range(16):
+                    r.append(lambda k=k: mm(B[:, 128 * h + k:128 * h + 128:16], T.sc[:, 2048 * h + k:2048 * h + 2048:16], T.blkS[:], False, k == 15))
+                return r
+            op("t", pe(128, *([64] * 16)), callsK, [Kn, "I16", "blkS", "sc%d" % h], [], tile="key%d" % t)
+        vp(dv(256), lambda B: V.tensor_tensor_scan(T.sco[:], T.resetv[:], B[:, 0:256], 0.0, A.add, A.max), "key%d" % t, ["resetv"], ["sco"])
+        v(one, lambda: ts(T.q1[:], T.sco[:, 15:256:16], 2047.0, None, A.add), ["sco"], ["q1"])
+        v(one, lambda: ts(T.q2[:], T.q1[:], 4095, None, A.bitwise_and), ["q1"], ["q2"])
+        v(one, lambda: ts(T[Lc][:], T.q2[:], -2047.0, None, A.add), ["q2"], [Lc])
+        place(t, p, False)
+        if not last:
+            snt, arr = "snt%d" % (t + 1), "arr%d" % (t + 1)
+            v(dg(256), lambda: V.tensor_tensor(T.xs[:], T.X[:, 0:4096].indirect(T[cu][:]), T.Z[:, z0:z1], A.add), XC + [cu, Z], ["xs"])
+            v(dh(256), lambda: ts(T.ZS[:, z0:z1], T.xs[:], 0.5, -0.25, A.mult, A.add), ["xs"], ["zs%d" % t])
+            dst = T.cores[(rank + 1 + t % 3) % len(T.cores)]
+            rid, pid = topo.addr(dst)[0], topo.addr(dst)[1]
+            ne = len(topo.engines(core, dst))
+            op("g", 1.0, [lambda: g.remote_dma(T.Z[:, z1:z1 + 256], T.ZS[:, z0:z1], T.sem[arr], T.sem[snt], pid=pid, routing_id=rid,
+                                               dma_engine_mask=topo.mask(core, dst))], ["zs%d" % t], ["way%d" % t], sem=snt, cnt=ne)
+            op("x", 0.0, [], ["way%d" % t], ["Z%d" % (t + 1)], lat=2.5, sem=arr, cnt=ne)
+        s(sg(256), lambda: S.activation(T[cutv][:], T.X[:, 0:4096].indirect(T[cu][:]), AF.Identity, bias=BIAS / 2 - 0.25, scale=0.5), XC + [cu], [cutv])
+        op("t", pe(128, 128), lambda B: [lambda h=h: mm(B[:, 128 * h:128 * h + 128], T.A1[:, 128 * h:128 * h + 128], T.I16[:], True, True)
+                                         for h in range(2)], ["A1", "I16"], [], tile="SP%d" % t)
+        vp(dv(256), lambda B: V.tensor_copy(T.SPs[:], B[:, 0:256]), "SP%d" % t, [], ["SPs"])
+        tn = same(t, "c", "SPs", 0, Lc, "eqc", False)
+        vp(one, lambda B: ts(T.nc[:], B[:, 0:16], T.thr[:], -10000.0, A.is_gt, A.mult), tn, ["thr"], ["nc"])
+        v(one, lambda: V.tensor_tensor(T.n1c[:], T.nc[:], T[Lc][:], A.add), ["nc", Lc], ["n1c"])
+        v(dg(256), lambda: V.tensor_tensor(T.A2c[:], T.n1c[:, 0:16].indirect(T.zl[:, 0:16]), T.in1c[:], A.max), ["n1c", "zl", "in1c"], ["A2c"])
+        spread_lists("A2c", "W2c%d" % t)
+        vp(one, lambda B: ts(T[dcu][:], B[:, 0:16], -1.0, 63488.0, A.mult, A.add), "W2c%d" % t, [], [dcu])
+        for b in range(8):
+            tn = "d%d_%d" % (t, b)
+            h, kb = b // 4, 4 * (b % 4)
+
+            def callsD(B, h=h, kb=kb):
+                r = []
+                for j in range(4):
+                    r.append(lambda j=j: mm(B[:, 128 * j:128 * j + 128], T.Ib[:], T[xg][:, 2048 * h + kb + j:2048 * h + 2048:16], True, False))
+                    r.append(lambda j=j: mm(B[:, 128 * j:128 * j + 128], T.Ibn[:], T.Z[:, z0 + 128 * h:z0 + 128 * h + 128], False, True))
+                return r
+            op("t", pe(*([128] * 8)), callsD, ["Ib", "Ibn", Z] + ["%s_%d" % (xg, c) for c in (2 * h, 2 * h + 1)], [], tile=tn)
+            op("s", sa(512), lambda B, b=b: [lambda: S.activation(T.ab[:, 512 * b:512 * b + 512], B[:], AF.Abs)], [], ["ab%d" % b], tile=tn)
+            if b % 2 == 1:
+                c = b // 2
+                v(dh(1024), lambda c=c: ts(T.th[:, 1024 * c:1024 * c + 1024], T.ab[:, 1024 * c:1024 * c + 1024], T.lim[:, t:t + 1], None, A.is_gt),
+                  ["ab%d" % (b - 1), "ab%d" % b, "lim%d" % t], ["th%d" % c])
+        for c in range(4):
+            h = c // 2
+            op("t", pe(*([64] * 8)), lambda B, c=c, h=h: [
+                lambda k=k: mm(B[:, 128 * h + k:128 * h + 128:16], T.th[:, 2048 * h + 128 * k:2048 * h + 128 * k + 128], T.blkb[:], True, True)
+                for k in range(8 * (c % 2), 8 * (c % 2) + 8)], ["th%d" % c, "blkb"], [], tile="cnt%d" % t)
+        vp(dv(256), lambda B: ts(T.sevL[:], B[:, 0:256], 8.5, None, A.is_gt), "cnt%d" % t, [], ["sevL"])
+        vp(dv(256), lambda B: V.tensor_tensor(T.sevT[:], B[:, 0:256], T.thrk[:, 15 - t:271 - t], A.is_gt), "cnt%d" % t, ["thrk"], ["sevT"])
+        s(sg(256), lambda: S.activation(T.skrep[:], T.sevL[:].indirect(T.skl[:, 16 * t:16 * t + 16]), AF.Copy), ["sevL", "skl"], ["skrep"])
+        if not last:
+            op("t", pe(64), lambda B: [lambda: mm(B[:, 0:16], T.onesb[:], T.sevL[:, k0:256:16], True, True)], ["onesb", "sevL"], [], tile="S%d" % t)
+            op("s", sa(16) + 0.14, lambda B: [lambda: S.activation(T.sj[:], B[:, 0:16], AF.Identity, bias=385.0, accum_out=T.sf[:])],
+               [], ["sf"], tile="S%d" % t)
+            v(one, lambda: ts(T.si[:], T.sf[:], 0.25, -4.375, A.mult, A.add), ["sf"], ["si"])
+            v(one, lambda: ts(T.lim[:, t + 1:t + 2], T.si[:], -4.0, T.sf[:], A.mult, A.add), ["si", "sf"], ["lim%d" % (t + 1)])
+
+        def blend(ident, extra, sevs):
+            def calls(B):
+                r = []
+                for o, m in ((0, "I8n"), (256, "I8p")):
+                    r.append(lambda o=o: mm(B[:, o:o + 256], ident, T[Gn][:], True, False))
+                    if extra:
+                        r.append(lambda o=o: mm(B[:, o:o + 256], T.wide[:, 15 - t:143 - t], T.SPs[:], False, False))
+                    for n in sevs:
+                        for h in range(2):
+                            r.append(lambda o=o, m=m, h=h, n=n: mm(B[:, o + 128 * h:o + 128 * h + 128], T[n][:, 128 * h:128 * h + 128], T[m][:],
+                                                                   False, h == 1 and n == sevs[-1]))
+                return r
+            return calls
+        op("t", pe(*([256] * 6)), blend(T.It[:, 128 * t:128 * t + 128], True, ["sevT"]),
+           ["It", Gn, "wide", "SPs", "sevT", "I8n", "I8p"], [], tile="G%d" % t)
+        vp(dv(256), lambda B: V.tensor_tensor(T.gm[:], T[Kn][:], B[:, 0:256], A.max), "G%d" % t, [Kn], ["gm"])
+        vp(dv(256), lambda B: V.tensor_tensor(T[Gn1][:], T.gm[:], B[:, 256:512], A.min), "G%d" % t, ["gm"], [Gn1])
+        if not last:
+            v(dh(256), lambda: ts(T[Gu1][:], T[Gn1][:], -1.0, 2048.0, A.mult, A.add), [Gn1], [Gu1])
+        op("t", pe(*([256] * 6)), blend(T.I16[:], False, ["sevL", "skrep"]), ["I16", Gn, "sevL", "skrep", "I8n", "I8p"], [], tile="N%d" % t)
+        vp(dv(256), lambda B: V.tensor_tensor(T.cm[:], T.cw[:], B[:, 0:256], A.max), "N%d" % t, ["cw"], ["cm"])
+        vp(dv(256), lambda B: V.tensor_tensor(T.cn[:], T.cm[:], B[:, 256:512], A.min), "N%d" % t, ["cm"], ["cn"])
+        v(ds(256), lambda: V.tensor_copy(T.CAN[:].indirect(T[dwl][:]), T.cn[:]), ["cn", dwl], ["CAN", "CANd"])
+
+        def callsR(B):
+            r = [lambda: mm(B[:, 0:256], T.Ih[:], T.xw[:], True, False),
+                 lambda: mm(B[:, 0:256], T.Ih[:], T.Z[:, z0:z1], False, False),
+                 lambda: mm(B[:, 0:256], T.qtr[:], T.ones16[:], False, False)]
+            for h in range(2):
+                r.append(lambda h=h: mm(B[:, 128 * h:128 * h + 128], T.skrep[:, 128 * h:128 * h + 128], T.I5n[:], False, h == 1))
+            for h in range(2):
+                r.append(lambda h=h: mm(B[:, 256 + 128 * h:384 + 128 * h], T.skrep[:, 128 * h:128 * h + 128], T.Ib[:], True, True))
+            return r
+        op("t", pe(256, 256, 256, 128, 128, 128, 128), callsR, ["Ih", "xw", Z, "qtr", "ones16", "skrep", "I5n", "Ib"], [], tile="R%d" % t)
+        vp(dv(256), lambda B: V.tensor_tensor(T.r2m[:], T.r2[:], B[:, 256:512], A.mult), "R%d" % t, ["r2"], ["r2m"])
+        vp(dv(256), lambda B: V.tensor_tensor(T.rn[:], T.r2m[:], B[:, 0:256], A.max), "R%d" % t, ["r2m"], ["rn"])
+        v(ds(256), lambda: V.tensor_copy(T.X[:].indirect(T[dwu][:]), T.rn[:]), ["rn", dwu], XR)
+        v(ds(256), lambda: V.tensor_copy(T.X[:].indirect(T[dcu][:]), T[cutv][:]), [cutv, dcu], XR)
+
+    for t in range(NT):
+        step(t)
+
+    def store(name, out, src, R):
+        op("y", 0.1, [lambda: Y.dma_start(out, src)], R, ["y" + name], lat=3.0, sem="st_" + name, cnt=16)
+
+    s(sa(1024), lambda: S.activation(T.lo[:], T.CAN[:, 0:1024], AF.Identity, bias=2048.0, scale=-1.0), ["CAN"], ["lo"])
+    store("ol", T.yl[:], T.lo[:], ["lo"])
+    v(dv(256), lambda: ts(T.go[:], T["Gn%d" % (NT % 2)][:], -1.0, 2048.0, A.mult, A.add), ["Gn%d" % (NT % 2)], ["go"])
+    store("og", T.yg[:], T.go[:], ["go"])
+    for c in range(4):
+        a, b = 1024 * c, 1024 * c + 1024
+        if c < 3:
+            v(dh(1024), lambda a=a, b=b: ts(T.th[:, a:b], T.X[:, a:b], -BIAS, None, A.add), ["X%d" % c], ["th%d" % c])
+        else:
+            s(sa(1024), lambda a=a, b=b: S.activation(T.th[:, a:b], T.X[:, a:b], AF.Identity, bias=-BIAS), ["X%d" % c], ["th%d" % c])
+        store("o%d" % c, T.yx[:, a:b], T.th[:, a:b], ["th%d" % c])
+    emit(g, T, ops, schedule(ops))
+
+
+def depend(ops):
+    last, readers, tiles = {}, {}, {}
+    for o in ops:
+        d = set()
+        for r in o["R"]:
+            d.update(last.get(r, ()))
+        for w in o["W"]:
+            d.update(last.get(w, ()))
+            d.update(readers.get(w, ()))
+        for r in o["R"]:
+            readers.setdefault(r, []).append(o["i"])
+        for w in o["W"]:
+            last[w] = [o["i"]]
+            readers[w] = []
+        if o["tile"]:
+            tl = tiles.setdefault(o["tile"], [None, [], []])
+            if tl[0] != o["e"]:
+                tl[0], tl[1], tl[2] = o["e"], tl[2], []
+            d.update(tl[1])
+            tl[2].append(o["i"])
+        d.discard(o["i"])
+        o["d"] = d
+
+
+def schedule(ops):
+    depend(ops)
+    n = len(ops)
+    succ = [[] for _ in range(n)]
+    for o in ops:
+        for j in o["d"]:
+            succ[j].append(o["i"])
+    prio = [0.0] * n
+    for i in range(n - 1, -1, -1):
+        prio[i] = ops[i]["c"] + ops[i]["lat"] + SYNC + max([prio[j] for j in succ[i]] or [0.0])
+    for o in ops:
+        prio[o["i"]] += BONUS.get("".join(c for c in (o["W"] or [o["tile"]])[0] if c.isalpha()) + "_" + o["e"], 0.0)
+    users = {}
+    for o in ops:
+        if o["tile"]:
+            users.setdefault(o["tile"], []).append(o["i"])
+    left = {k: len(u) for k, u in users.items()}
+    bank = {}
+    free = {k: [] for k in range(8)}
+    need = [len(o["d"]) for o in ops]
+    rt, fin = [0.0] * n, [0.0] * n
+    ready = [i for i in range(n) if need[i] == 0]
+    et = {"v": 0.0, "s": 0.0, "t": 0.0, "g": 0.0, "y": 0.0, "x": 0.0}
+    order = []
+    while ready:
+        cand = []
+        for i in ready:
+            o = ops[i]
+            st = max(rt[i], et[o["e"]] if o["e"] != "x" else 0.0)
+            bk = None
+            if o["tile"] and o["tile"] not in bank:
+                if not free:
+                    continue
+                a, bk = min((max([fin[u] for u in us] or [0.0]), k) for k, us in free.items())
+                st = max(st, a + SYNC)
+            cand.append((st, -prio[i], i, bk))
+        if not cand:
+            raise ValueError("no bank for any ready op")
+        st, _, i, bk = min(cand, key=lambda c: c[:3])
+        ready.remove(i)
+        o = ops[i]
+        if bk is not None:
+            bank[o["tile"]] = bk
+            o["d"] = set(o["d"]) | set(free.pop(bk))
+        if o["tile"]:
+            o["b"] = bank[o["tile"]]
+            left[o["tile"]] -= 1
+            if left[o["tile"]] == 0:
+                free[o["b"]] = users[o["tile"]]
+        et[o["e"]] = st + o["c"]
+        fin[i] = st + o["c"] + o["lat"]
+        o["t0"] = st
+        order.append(i)
+        for j in succ[i]:
+            need[j] -= 1
+            rt[j] = max(rt[j], fin[i] + SYNC)
+            if need[j] == 0:
+                ready.append(j)
+    if len(order) != n:
+        raise ValueError("schedule stuck")
+    return order
+
+
+def emit(g, T, ops, order):
+    Q = {"v": g.vector, "s": g.scalar, "t": g.tensor, "g": g, "y": g.sync}
+    known = {e: {} for e in Q}
+    count, done = {}, {}
+    for i in order:
+        o = ops[i]
+        e = o["e"]
+        if e == "x":
+            done[i] = (o["sem"], o["cnt"], {})
+            continue
+        kn = known[e]
+        for _, j in sorted(((ops[j]["t0"], j) for j in o["d"]), reverse=True):
+            sm, c, snap = done[j]
+            if c > kn.get(sm, 0):
+                Q[e].wait_ge(T.sem[sm], c)
+                kn[sm] = c
+                for a, b in snap.items():
+                    if b > kn.get(a, 0):
+                        kn[a] = b
+        calls = o["f"](T["ps%d" % o["b"]]) if o["tile"] else o["f"]
+        for f in calls:
+            r = f()
+            if o["sem"] is None:
+                count["q" + e] = count.get("q" + e, 0) + 1
+                r.then_inc(T.sem["q" + e], 1)
+            elif not o["sem"].startswith("snt"):
+                r.then_inc(T.sem[o["sem"]], 16)
+        done[i] = (o["sem"] or "q" + e, o["cnt"] or count.get("q" + e, 0), dict(kn))
+    for sm in sorted(count):
+        g.wait_ge(T.sem[sm], count[sm])
+    for o in ops:
+        if o["sem"] is not None:
+            g.wait_ge(T.sem[o["sem"]], o["cnt"])

@@ -4,58 +4,54 @@ A = AluOpType
 AF = ActivationFunctionType
 NT = 8
 BIAS = 160.0
-XW = 6144
-CW = 1536
+XW = 5120
+CW = 1280
+BIG = 8192.0
+GRID = 402653184.0
+EQN = [256 - 16 * a for a in range(16)]
+EQO = [sum(EQN[:a]) for a in range(17)]
 
 F4, BF, HF, I4, U2 = "float32", "bfloat16", "float16", "int32", "uint16"
 SCRATCH = {}
 for _n, _s, _d in (
-        ("X", XW, BF), ("CAN", CW, F4), ("cin", 1024, I4), ("tin", 256, I4), ("vin", 256, I4),
-        ("xg0", 4096, BF), ("xg1", 4096, BF), ("ab", 4096, BF), ("th", 4096, BF), ("zrep", 4096, BF), ("sc", 4096, BF),
-        ("lo", 1024, F4), ("go", 256, F4), ("eqw", 3072, BF), ("eqc", 3072, BF), ("df", 3072, BF), ("wrow", 2048, HF), ("wall", 2048, HF),
-        ("sco", 256, F4), ("q1", 16, I4), ("q2", 16, I4), ("UW", 256, HF), ("SPs", 256, HF), ("LwU", 32, F4),
-        ("nw", 16, F4), ("n1w", 16, F4), ("nc", 16, F4), ("n1c", 16, F4), ("A1", 256, HF), ("A2c", 256, HF), ("A2w", 256, HF),
-        ("ufw", 16, HF), ("uf", 16, HF), ("xs", 256, HF), ("xw", 256, BF), ("r2", 256, BF), ("r2m", 256, BF),
-        ("rn", 256, BF), ("cw", 256, F4), ("cm", 256, F4), ("cn", 256, F4), ("gm", 256, HF), ("sevL", 256, BF), ("sevT", 256, BF),
-        ("skrep", 256, BF), ("sf", 1, F4), ("si", 1, HF), ("sj", 16, F4), ("lim", 8, F4),
-        ("Z", 256 * NT, BF), ("ZS", 256 * NT, BF),
-        ("i128", 128, F4), ("pc", 1, F4), ("pci", 1, I4), ("pg", 1, F4), ("pk", 1, F4), ("p16", 1, F4),
-        ("rc", 1, F4), ("k272", 272, F4), ("w144", 144, F4), ("v1", 256, F4), ("zli", 256, I4),
-        ("skli", 128, I4), ("zl", 256, U2), ("skl", 128, U2), ("RM", 16, F4), ("RM1", 16, F4), ("RM2", 16, F4), ("RMn", 16, F4),
-        ("I16", 128, HF), ("I8n", 128, BF), ("I8p", 128, BF), ("Ib", 128, BF), ("Ibn", 128, BF), ("Ih", 128, BF), ("I5n", 128, BF),
-        ("It", 1024, HF), ("blkf", 8, F4), ("blk1", 8, HF), ("blkb", 8, BF), ("blkS", 8, BF), ("onesg", 1024, HF), ("ones16", 256, HF),
-        ("onesb", 128, BF), ("qtr", 128, HF), ("dmask", 256, HF), ("in1c", 256, HF), ("selk", 64, HF), ("wide", 144, HF),
-        ("thrk", 272, F4), ("resetv", 256, F4), ("wtf", 1, F4), ("wt", 1, BF), ("wbig", 1, BF), ("thr", 1, F4)):
+        ("X", XW, BF), ("CAN", CW, F4), ("cin", 1024, I4), ("tin", 256, I4), ("vin", 256, I4), ("zin", 256, BF),
+        ("xg", 4096, BF), ("ab", 4096, BF), ("th", 4096, BF), ("sc", 4096, BF), ("lo", 1024, F4), ("go", 256, F4),
+        ("Kn", 272, HF), ("Ku", 256, U2), ("eqw", EQO[16], BF), ("eqc", EQO[16], BF), ("repw", 272, HF), ("repc", 256, HF),
+        ("uW", 16, F4), ("cW", 16, F4), ("TC", 256, HF), ("yw", 32, F4), ("yc", 16, F4), ("sco", 256, F4), ("q1", 16, I4), ("q2", 16, I4),
+        ("Lc", 16, HF), ("cu", 16, U2), ("vl", 16, U2), ("dwu", 16, U2), ("dwl", 16, U2), ("dcu", 16, U2), ("cwl", 16, U2),
+        ("xc", 256, BF), ("r1", 256, BF), ("rf", 512, BF), ("cw", 256, HF), ("cf", 512, F4), ("ga", 256, HF), ("sg", 256, BF),
+        ("acc", 1, F4), ("p32", 1, F4), ("si", 1, HF), ("s0", 1, F4),
+        ("Z", 512 * NT, BF), ("ZS", 256 * NT, BF),
+        ("i128", 128, F4), ("pc", 1, F4), ("pci", 1, I4), ("col", 16, F4), ("k256", 256, F4), ("w144", 144, F4), ("c16", 128, F4),
+        ("RM", 16, F4), ("RMn", 16, F4), ("RO", 16, HF), ("RE", 16, HF), ("I16", 128, HF), ("Ib", 128, BF), ("Ibn", 128, BF), ("Ih", 128, BF),
+        ("Ihn", 128, BF), ("IBp", 128, BF), ("IBn", 128, BF), ("It", 1024, HF), ("Ioff", 128, F4), ("blkf", 8, F4), ("blkb", 8, BF),
+        ("blkS", 8, BF), ("selk", 64, HF), ("WD", 8, BF), ("WO", 8, BF), ("thr", 256, BF), ("W72", 144, HF), ("E8", 128, HF), ("RA", 128, HF),
+        ("dum", 32, F4), ("resetv", 256, F4), ("c160", 256, BF), ("zero", 128, BF), ("c32", 128, F4)):
     SCRATCH[_n] = ("sbuf", [128, _s], _d)
 for _k in range(2):
-    for _n, _s, _d in (("Kn", 256, HF), ("Ku", 256, U2), ("Gn", 256, HF), ("Gu", 256, U2), ("cutv", 256, BF), ("Lc", 16, F4),
-                       ("cu", 16, U2), ("vl", 16, U2), ("dwu", 16, U2), ("dwl", 16, U2), ("dcu", 16, U2)):
+    for _n, _s, _d in (("Gn", 256, HF), ("Gu", 256, U2), ("TW", 256, HF), ("sI", 128, BF)):
         SCRATCH["%s%d" % (_n, _k)] = ("sbuf", [128, _s], _d)
 for _k in range(8):
     SCRATCH["ps%d" % _k] = ("psum", [128, 512], F4)
 
 SEMAPHORES = (["qv", "qs", "qt", "qg"] + ["ld_" + n for n in ("cut", "z", "trail", "canal", "x0", "x1", "x2", "x3")]
-              + ["st_" + n for n in ("o0", "o1", "o2", "o3", "ol", "og")] + ["row%d" % k for k in range(NT)]
+              + ["st_" + n for n in ("o0", "o1", "o2", "o3", "ol", "og")]
               + ["arr%d" % k for k in range(1, NT)] + ["snt%d" % k for k in range(1, NT)])
 
-CY, GA, PEC, SYNC = 0.00083, 1.5, 0.0006, 0.1
-BONUS = {'cn_v': 1.5, 'dwu_v': 3, 'cnt_t': -1.5, 'zs_v': -1.5, 'nw_v': -0.7, 'SPs_v': 0.7, 'BCc_t': -6, 'sevL_v': 3, 'Aw_v': -1.5,
-         'd_t': -3, 'X_v': -6, 'gm_v': -3, 'eqc_v': -3, 'N_t': -6, 'vl_v': -1.5, 'UW_v': -1.5, 'wrow_y': 1.5, 'th_v': -0.7, 'lim_v': 6,
-         'A_v': 6, 'Gu_v': -3, 'sc_v': 3, 'sco_v': 3, 'ab_s': 3, 'eqw_v': 3, 'xw_s': -0.7, 'Ku_v': 3, 'cw_v': 3, 'r_v': -3,
-         'zrep_s': -1.5, 'si_v': -6, 'uf_v': -0.7, 'Ibn_v': 6, 'SP_t': 3, 'cm_v': 1.5, 'cw_s': 0.7, 'rn_v': 6, 'lo_v': 3, 'CAN_v': -3,
-         'R_t': -3, 'xg_s': -3, 'Ww_t': 3, 'Ac_v': -3, 'Lc_v': 0.7, 'nc_v': 6, 'Z_x': -0.7, 'S_t': -3, 'sf_s': -1.5, 'cu_v': -0.7,
-         'wall_g': -3, 'Gn_v': -3, 'key_t': 0.7, 'dwl_v': 1.5, 'Wc_t': 0.7, 'cutv_s': -3, 'Z_v': -3, 'q_v': -1.5, 'EQw_t': 3,
-         'EQc_t': -1.5, 'cW_t': 6, 'rm_v': 1.5, 'df_s': 0.7, 'sevT_v': 3, 'way_g': -3, 'xs_v': 0.7, 'G_t': -3}
-EA = (0, 1, 2)
+CY, GA, SC, PEC, PEF, SYNC = 0.00083, 1.5, 3.5, 0.0005, 0.002, 0.1
+BONUS = {'TCb_s': -2, 'key_t': 4, 'Kt_t': -3, 'T_t': 1, 'S_t': 4, 'sI_s': -6, 'cnt_t': -6, 'N_t': -2, 'rc_t': 1, 'X_v': 3, 'vl_v': -3, 'r_s': 2, 'Ku_v': -4, 'xc_s': -4, 'TWa_s': 1, 'th_v': -3, 'q_v': -2, 'sk_t': -6, 'cw_s': -6, 'TW_t': 0.5, 'yc_v': 0.5, 'selk_s': 6, 'CAN_v': 4, 'TCa_s': 3, 'dwl_v': -4, 'si_s': 3, 'sg_s': 3, 'sc_v': -1, 's_s': 3, 'rf_s': 6, 'Gn_v': -2, 'dcu_v': -3, 'Kn_s': -0.5, 'repc_s': 0.5, 'ga_s': 0.5, 'It_s': -0.5, 'yw_v': 2, 'repw_s': -3, 'ZS_t': -4, 'cwl_v': -0.5, 'TWc_s': 6, 'ab_s': -6, 'eqc_v': 2, 'sco_v': -1, 'xg_s': -3, 'yc_t': 3, 'cW_t': -1, 'zs_s': -2, 'Zb_s': -4, 'dwu_v': 3, 'rw_t': -6, 'Gu_v': -1, 'Pw_t': 2, 'p_s': 6, 'G_t': -0.5, 'R_t': 0.5, 'd_t': -4, 'Lc_v': 0.5, 'cf_s': -0.5, 'cW_s': 6, 'cu_v': 4, 'TWb_s': -4, 'eqw_v': -0.5}
+LOOK = 0.3
+VBANKS = ()
+TWICE = True
 
 
-def dv(n): return 0.06 + n * CY
+def dv(n): return 0.06 + max(n, 64) * CY
 def dh(n): return 0.06 + max(n * 0.5, 64) * CY
 def dg(n): return 0.05 + n * GA * CY
-def ds(n): return 0.05 + n * 3.5 * CY
+def ds(n): return 0.05 + n * SC * CY
 def sg(n): return 0.065 + n * GA * CY
 def sa(n): return 0.065 + n * CY
-def pe(*ns): return sum(max(64, n) for n in ns) * PEC + 0.02
+def pe(*ns): return sum(ns) * PEC + PEF * len(ns) + 0.02
 
 
 def rank_program(g, core, T, topo):
@@ -72,25 +68,27 @@ def rank_program(g, core, T, topo):
     def v(cost, f, R, W): op("v", cost, [f], R, W)
     def s(cost, f, R, W): op("s", cost, [f], R, W)
     def vp(cost, f, tile, R, W): op("v", cost, lambda B: [lambda: f(B)], R, W, tile=tile)
-    mm = PE.matmul
+    def sp(cost, f, tile, R, W): op("s", cost, lambda B: [lambda: f(B)], R, W, tile=tile)
+    mm, act = PE.matmul, S.activation
+
+    def t_(tile, prods, R, W=()):
+        op("t", pe(*[p[5] for p in prods(T.ps0)]), lambda B: [lambda p=p: mm(*p[:5]) for p in prods(B)], R, W, tile=tile)
 
     def ts(out, i0, s1, s2, o0, o1=None):
         if o1 is None:
             return V.tensor_scalar(out, i0, s1, None, o0)
         return V.tensor_scalar(out, i0, s1, s2, o0, o1)
+    one, sone = dv(64), sa(16)
 
     def load(name, out, src, W, lat, R=()):
         op("y", 0.1, [lambda: Y.dma_start(out, src)], R, W, lat=lat, sem="ld_" + name, cnt=16)
 
-    v(dv(256), lambda: V.memset(T.vin[:], 0), [], ["vin"])
-    v(dh(2048), lambda: V.memset(T.X[:, 4096:XW], BIAS), [], ["Xd"])
-    v(dv(512), lambda: V.memset(T.CAN[:, 1024:CW], 0.0), [], ["CANd"])
-    load("z", T.xw[:], T.z[:], ["xw"], 2.0)
+    load("cut", T.vin[0:8, :], T.cut[:], ["vin"], 2.0)
     load("trail", T.tin[:], T.trail[:], ["tin"], 2.2)
-    load("canal", T.cin[:], T.canal[:], ["cin"], 4.0)
+    load("canal", T.cin[:], T.canal[:], ["cin"], 3.0)
     for q in range(4):
-        load("x%d" % q, T.X[:, 1024 * q:1024 * q + 1024], T.x[:, 1024 * q:1024 * q + 1024], ["X%d" % q], 4.0 + q)
-    load("cut", T.vin[0:128:16, :], T.cut[:], ["vin2"], 2.0, ["vin"])
+        load("x%d" % q, T.X[:, 1024 * q:1024 * q + 1024], T.x[:, 1024 * q:1024 * q + 1024], ["X%d" % q], 3.5 + 0.5 * q)
+    load("z", T.zin[:], T.z[:], ["zin"], 5.0)
     XC = ["X0", "X1", "X2", "X3"]
     XR = XC + ["Xd"]
 
@@ -101,272 +99,238 @@ def rank_program(g, core, T, topo):
         kw = {"allow_small_or_imprecise_dtypes": True} if f else {}
         op("g", 0.13 + 2 * n * CY, [lambda: g.iota(out, pat, base, cm, **kw)], [], [name])
 
+    def fill(name, ap, val, n, R=()):
+        v(dv(n), lambda: V.memset(ap, val), R, [name])
+
     iota("pci", T.pci[:], [[0, 1]], 0, 1, False)
     iota("pc", T.pc[:], [[0, 1]], 0, 1)
     iota("i128", T.i128[:], [[1, 128]], 0, 0)
-    iota("k272", T.k272[:], [[0, 17], [1, 16]], 0, 0)
-    iota("zli", T.zli[:], [[1, 256]], 0, 0, False)
-    iota("v1", T.v1[:], [[-1024, 2], [0, 128]], -2052, -8)
     iota("w144", T.w144[:], [[1, 144]], -15, 0)
-    iota("sklia", T.skli[:, 0:64], [[1, 4], [16, 16]], 12, 0, False)
-    iota("sklib", T.skli[:, 64:128], [[1, 4], [16, 16]], 0, 0, False)
-    one = dv(64)
-    v(one, lambda: ts(T.q1[:, 0:1], T.pci[:], 4, None, A.arith_shift_right), ["pci"], ["q1"])
-    v(one, lambda: ts(T.q2[:, 0:1], T.pci[:], 15, None, A.bitwise_and), ["pci"], ["q2"])
-    v(one, lambda: V.tensor_copy(T.pg[:], T.q1[:, 0:1]), ["q1"], ["pg"])
-    v(one, lambda: V.tensor_copy(T.pk[:], T.q2[:, 0:1]), ["q2"], ["pk"])
-    v(one, lambda: ts(T.p16[:], T.pg[:], 16.0, None, A.mult), ["pg"], ["p16"])
-    v(one, lambda: ts(T.rc[:], T.pk[:], 0.0, 2048.0, A.is_equal, A.mult), ["pk"], ["rc"])
-    v(one, lambda: ts(T.RM[:], T.i128[:, 0:16], T.pk[:], None, A.is_equal), ["i128", "pk"], ["RM"])
-    v(one, lambda: ts(T.RM1[:], T.RM[:], 0.25, None, A.mult), ["RM"], ["RM1"])
-    v(one, lambda: ts(T.RM2[:], T.RM[:], 1536.375, None, A.mult), ["RM"], ["RM2"])
-    v(one, lambda: ts(T.RMn[:], T.RM[:], -1.0, 1.0, A.mult, A.add), ["RM"], ["RMn"])
-    for name, val in (("I16", 1.0), ("Ib", 1.0), ("Ibn", -1.0), ("I8n", -8192.0), ("I8p", 8192.0), ("Ih", 0.5), ("I5n", -512.0)):
-        v(dv(128), lambda name=name, val=val: ts(T[name][:], T.i128[:], T.pc[:], val, A.is_equal, A.mult), ["i128", "pc"], [name])
-    for name, val in (("blkf", 1.0), ("blk1", 1.0), ("blkb", 1.0), ("blkS", 4096.0)):
-        v(one, lambda name=name, val=val: ts(T[name][:], T.i128[:, 0:8], T.pg[:], val, A.is_equal, A.mult), ["i128", "pg"], [name])
-    v(dv(256), lambda: ts(T.ones16[:], T.k272[:, 0:256], 0.0, 1.0, A.mult, A.add), ["k272"], ["ones16"])
-    v(dh(128), lambda: V.memset(T.onesb[:], 1.0), [], ["onesb"])
-    v(dh(128), lambda: ts(T.qtr[:], T.ones16[:, 0:128], -0.25 / 128, None, A.mult), ["ones16"], ["qtr"])
-    v(one, lambda: V.memset(T.wbig[:], float(2.0 ** 90)), [], ["wbig"])
-    v(one, lambda: V.memset(T.lim[:, 0:1], 16.0), [], ["lim0"])
-    op("v", 8 * dh(128), [lambda k=k: ts(T.onesg[:, 128 * k:128 * k + 128], T.ones16[:, 0:128], T.blkf[:, k:k + 1], None, A.mult)
-                          for k in range(8)], ["ones16", "blkf"], ["onesg"])
-    v(dv(256), lambda: ts(T.dmask[:], T.k272[:, 0:256], T.pk[:], None, A.is_equal), ["k272", "pk"], ["dmask"])
-    v(dv(256), lambda: ts(T.resetv[:], T.k272[:, 0:256], 0.0, -2.0e7, A.is_equal, A.mult), ["k272"], ["resetv"])
-    v(dv(272), lambda: ts(T.sco[:], T.v1[:], -4096.0, None, A.add), ["v1"], ["sco"])
-    v(dv(512), lambda: V.tensor_tensor(T.go[:], T.sco[:], T.dmask[:], A.mult), ["sco", "dmask"], ["go"])
-    v(dv(256), lambda: ts(T.in1c[:], T.go[:], 4096.0, None, A.add), ["go"], ["in1c"])
-    v(dv(272), lambda: ts(T.thrk[:], T.k272[:], 15.0, 100.0, A.is_equal, A.mult), ["k272"], ["thrk0"])
-    v(dv(272), lambda: ts(T.thrk[:], T.thrk[:], 8.5, None, A.add), ["thrk0"], ["thrk"])
-    v(dv(144), lambda: ts(T.wide[:], T.w144[:], T.p16[:], None, A.is_equal), ["w144", "p16"], ["wide"])
-    v(dv(256), lambda: V.tensor_copy(T.zl[:], T.zli[:]), ["zli"], ["zl"])
-    v(dv(128), lambda: V.tensor_copy(T.skl[:], T.skli[:]), ["sklia", "sklib"], ["skl"])
-    op("v", 8 * one, [lambda t=t: ts(T.selk[:, 8 * t:8 * t + 8], T.blkf[:], T.RM[:, (t + 12) % 16:(t + 12) % 16 + 1], None, A.mult)
-                      for t in range(NT)], ["blkf", "RM"], ["selk"])
-    op("v", 8 * dh(128), [lambda t=t: ts(T.It[:, 128 * t:128 * t + 128], T.I16[:], T.RMn[:, t:t + 1], None, A.mult)
-                          for t in range(NT)], ["I16", "RMn"], ["It"])
-    v(dv(128), lambda: V.memset(T.cm[:, 0:128], 0.5), [], ["cm"])
-    v(dv(128), lambda: V.memset(T.cn[:, 0:128], 0.0), [], ["cn"])
-    v(dv(128), lambda: V.tensor_tensor_scan(T.cw[:, 0:128], T.cm[:, 0:128], T.cn[:, 0:128], float(2.0 ** 64), A.mult, A.add), ["cm", "cn"], ["cw"])
-    v(dv(256), lambda: V.tensor_tensor(T.lo[:, 0:128], T.cw[:, 0:128], T.I16[:], A.mult), ["cw", "I16"], ["lo"])
-    v(dv(128), lambda: V.tensor_reduce(T.wtf[:], T.lo[:, 0:128], AxisListType.X, A.add), ["lo"], ["wtf"])
-    v(one, lambda: V.tensor_copy(T.wt[:], T.wtf[:]), ["wtf"], ["wt"])
-    v(one, lambda: ts(T.thr[:], T.wtf[:], 2.5, None, A.mult), ["wtf"], ["thr"])
+    iota("c16", T.c16[:], [[1, 8], [0, 16]], 0, 0)
+    iota("k256", T.k256[:], [[0, 16], [1, 16]], 0, 0)
+    iota("dum0", T.yw[:], [[int(BIG), 2], [-64, 16]], -2048 - 15 * int(BIG), 0)
+    pg, pk, odd, p32, even, p512, pk4, wcol = [T.col[:, k:k + 1] for k in range(8)]
+    v(one, lambda: ts(T.q1[:, 0:1], T.pci[:], 4, None, A.arith_shift_right), ["pci"], ["q1a"])
+    v(one, lambda: ts(T.q1[:, 1:2], T.pci[:], 15, None, A.bitwise_and), ["pci"], ["q1b"])
+    v(one, lambda: ts(T.q1[:, 2:3], T.pci[:], 4, 1, A.arith_shift_right, A.bitwise_and), ["pci"], ["q1c"])
+    v(one, lambda: ts(T.q1[:, 3:4], T.pci[:], 31, None, A.bitwise_and), ["pci"], ["q1d"])
+    v(one, lambda: V.tensor_copy(T.col[:, 0:4], T.q1[:, 0:4]), ["q1a", "q1b", "q1c", "q1d"], ["col", "q1"])
+    s(sone, lambda: act(even, odd, AF.Identity, bias=1.0, scale=-1.0), ["col"], ["even"])
+    s(sone, lambda: act(p512, p32, AF.Copy, scale=16.0), ["col"], ["p512"])
+    s(sone, lambda: act(pk4, pk, AF.Copy, scale=-4.0), ["col"], ["pk4"])
+    s(sone, lambda: act(T.dum[:], T.yw[:], AF.Identity, bias=pk4), ["dum0", "pk4"], ["dum", "yw"])
+    v(one, lambda: ts(T.RM[:], T.i128[:, 0:16], pk, None, A.is_equal), ["i128", "col"], ["RM"])
+    s(sone, lambda: act(T.RMn[:], T.RM[:], AF.Identity, bias=1.0, scale=-1.0), ["RM"], ["RMn"])
+    s(sone, lambda: act(T.RO[:], T.RM[:], AF.Copy, scale=odd), ["RM", "col"], ["RO"])
+    s(sone, lambda: act(T.RE[:], T.RM[:], AF.Copy, scale=even), ["RM", "even"], ["RE"])
+    v(dv(128), lambda: ts(T.Ib[:], T.i128[:], T.pc[:], None, A.is_equal), ["i128", "pc"], ["Ib"])
+    for name, val in (("I16", 1.0), ("sI0", 0.97), ("Ibn", -1.0), ("IBn", -BIG), ("IBp", BIG), ("Ih", 0.5), ("Ihn", -0.5)):
+        s(sa(128), lambda name=name, val=val: act(T[name][:], T.Ib[:], AF.Copy, scale=val), ["Ib"], [name])
+    s(sa(128), lambda: act(T.Ioff[:], T.Ib[:], AF.Identity, bias=-10000.0, scale=10000.0 + 0.97 - 307.2), ["Ib"], ["Ioff"])
+    v(one, lambda: ts(T.blkf[:], T.i128[:, 0:8], pg, None, A.is_equal), ["i128", "col"], ["blkf"])
+    for name, val in (("blkb", 1.0), ("blkS", 4096.0), ("WO", 4.0)):
+        s(sone, lambda name=name, val=val: act(T[name][:], T.blkf[:], AF.Copy, scale=val), ["blkf"], [name])
+    for t in range(NT):
+        k0 = (t + 12) % 16
+        s(sone, lambda t=t, k0=k0: act(T.selk[:, 8 * t:8 * t + 8], T.blkf[:], AF.Copy, scale=T.RM[:, k0:k0 + 1]), ["blkf", "RM"], ["selk%d" % t])
+        s(sa(128), lambda t=t: act(T.It[:, 128 * t:128 * t + 128], T.Ib[:], AF.Copy, scale=T.RMn[:, t:t + 1]), ["Ib", "RMn"], ["It%d" % t])
+    v(dv(256), lambda: ts(T.cf[:, 0:256], T.k256[:], 0.0, 0.5, A.not_equal, A.mult), ["k256"], ["cf"])
+    v(dv(256), lambda: ts(T.go[:], T.k256[:], 0.0, -2.5, A.is_equal, A.mult), ["k256"], ["go"])
+    v(dv(256), lambda: V.tensor_tensor_scan(T.thr[:], T.cf[:, 0:256], T.go[:], 0.0, A.mult, A.add), ["cf", "go"], ["thr"])
+    s(sa(256), lambda: act(T.resetv[:], T.go[:], AF.Copy, scale=8.0e6), ["go"], ["resetv"])
+    v(one, lambda: V.tensor_tensor(T.yc[:], T.thr[:, 0:16], T.RM[:], A.mult), ["thr", "RM"], ["yc"])
+    v(one, lambda: V.tensor_reduce(wcol, T.yc[:], AxisListType.X, A.add), ["yc"], ["wcol"])
+    v(one, lambda: ts(T.WD[:], T.blkf[:], wcol, -0.4, A.mult, A.mult), ["blkf", "wcol"], ["WD"])
+    fill("W72", T.W72[:], 0.0, 72)
+    fill("W72", T.W72[0:9, :], -BIG, 72)
+    for p0, val in ((0, 1.0), (32, -BIG), (64, -BIG)):
+        v(dv(144), lambda p0=p0, val=val: ts(T.W72[p0:p0 + 8, :], T.w144[p0:p0 + 8, :], T.col[p0:p0 + 8, 5:6], val, A.is_equal, A.mult),
+          ["w144", "p512"], ["W72"])
+    fill("RA", T.RA[:], 0.0, 64)
+    fill("RA", T.RA[0:9, :], BIAS + 63.25, 64)
+    fill("RA", T.RA[0:8, :], 0.0, 64)
+    for name, p0, val in (("E8", 0, 1.0), ("E8", 64, -512.0), ("RA", 64, 512.0)):
+        v(dv(128), lambda name=name, p0=p0, val=val: ts(T[name][p0:p0 + 8, :], T.c16[p0:p0 + 8, :], T.col[p0:p0 + 8, 3:4], val, A.is_equal, A.mult),
+          ["c16", "col"], [name])
+    fill("c160", T.c160[:], BIAS, 128)
+    fill("zero", T.zero[:], 0.0, 64)
+    fill("c32", T.c32[:], -0.025, 128)
+    fill("Xd", T.X[:, 4096:XW], BIAS, 512)
+    fill("CANd", T.CAN[:, 1024:CW], 0.0, 256)
+    fill("Knp", T.Kn[:, 0:16], 0.0, 16)
+    for name in ("TC", "TW0", "TW1"):
+        op("v", dh(256), [lambda name=name: ts(T[name][:], T.c160[:], 0.0, 1.0, A.mult, A.add)], ["c160"], [name + "a", name + "b", name + "c"])
 
-    v(dv(256), lambda: ts(T.UW[:], T.vin[:], -1.0, T.rc[:], A.mult, A.add), ["vin", "vin2", "rc"], ["UW"])
+    v(dv(256), lambda: ts(T.TC[0:8, :], T.vin[0:8, :], -1.0, 2048.0, A.mult, A.add), ["vin"], ["TCa"])
     v(dv(256), lambda: ts(T.Gn0[:], T.tin[:], -1.0, 2048.0, A.mult, A.add), ["tin"], ["Gn0"])
     v(dv(256), lambda: V.tensor_copy(T.Gu0[:], T.tin[:]), ["tin"], ["Gu0"])
-    v(dh(256), lambda: ts(T.Z[:, 0:256], T.xw[:], BIAS, None, A.add), ["xw"], ["Z0"])
+    v(dh(256), lambda: ts(T.Z[:, 0:256], T.zin[:], BIAS, None, A.add), ["zin"], ["Z0"])
     v(dv(1024), lambda: ts(T.CAN[:, 0:1024], T.cin[:], -1.0, 2048.0, A.mult, A.add), ["cin"], ["CAN"])
     for q in range(4):
         v(dh(1024), lambda q=q: ts(T.X[:, 1024 * q:1024 * q + 1024], T.X[:, 1024 * q:1024 * q + 1024], BIAS, None, A.add),
           ["X%d" % q], ["X%d" % q])
 
-    def halves(src, rhs):
-        return lambda B: [lambda h=h: mm(B[:, 8 * h:8 * h + 8], T[src][:, 128 * h:128 * h + 128], rhs, True, True) for h in range(2)]
+    def wrap(buf, rows, c0):
+        return lambda B: [(B[:, c0:c0 + 16], T.W72[0:rows, 15 - b:143 - b], T[buf][0:rows, b:256:16], b == 0, b == 15, 64) for b in range(16)]
 
-    def spread_lists(key, tname):
-        op("t", pe(64, 64), halves(key, T.blk1[:]), [key, "blk1"], [], tile=tname)
+    def later(tag, t, rep, colbuf, eq, buf):
+        tn = "P%s%d" % (tag, t)
+        t_(tn, lambda B: [(B[32:40, 0:256], T.Ib[0:8, 0:8], T.thr[0:8, :], True, False, 256)], ["Ib", "thr", rep], [tn])
+        for blocks in (range(0, 3), range(3, 7), range(7, 11), range(11, 16)):
+            nm = "%s_%d" % (eq, blocks[0])
+            op("v", sum(dh(EQN[a]) for a in blocks),
+               [lambda a=a: ts(T[eq][:, EQO[a]:EQO[a + 1]], T[rep][:, 16 * a:256], T[colbuf][:, a:a + 1], None, A.is_equal) for a in blocks],
+               [rep, colbuf], [nm])
 
-    def same(t, tag, src, col0, Lname, eq, pb):
-        k0 = (t + 12) % 16
-        if pb:
-            op("y", 0.1, [lambda: Y.dma_start(T.wrow[0:1, :], T[src][k0:128:16, :])], [src], ["wrow"], lat=2.0, sem="row%d" % t, cnt=16)
-            op("g", 0.14 + 4 * 2048 * CY, [lambda: g.partition_broadcast(T.wall[:], T.wrow[0:1, :], 128)], ["wrow"], ["wall"])
-        for b in range(4):
-            ks = (2 * b, 2 * b + 1)
-
-            def cmp(W, off, k, h):
-                return lambda: ts(T[eq][:, 384 * k + 256 * h:384 * k + 256 + 128 * h], W[:, off + 128 * h:off + 256],
-                                  T[Lname][:, col0 + 8 * h + k:col0 + 8 * h + k + 1], None, A.is_equal)
-
-            def dist(B, k, h):
-                return lambda: S.activation(T.df[:, 384 * k + 256 * h:384 * k + 256 + 128 * h], B[:, 256 * (k % 2) + 128 * h:256 * (k % 2) + 256],
-                                            AF.Abs, bias=T[Lname][:, col0 + 8 * h + k:col0 + 8 * h + k + 1], scale=-1.0)
-            if pb:
-                op("v", 2 * dh(256) + 2 * dh(128), [cmp(T.wall, 256 * k, k, h) for k in ks for h in range(2)], [Lname, "wall"], ["%s_%d" % (eq, b)])
-                continue
-            tn = "BC%s%d_%d" % (tag, t, b)
-            op("t", pe(256, 256), lambda B, ks=ks: [lambda k=k: mm(B[:, 256 * (k % 2):256 * (k % 2) + 256], T.onesg[:, 128 * k:128 * k + 128],
-               T[src][:], True, True) for k in ks], [src, "onesg"], [], tile=tn)
-            if b in EA:
-                op("s", 2 * sa(256) + 2 * sa(128), lambda B, ks=ks, dist=dist: [dist(B, k, h) for k in ks for h in range(2)],
-                   [Lname], ["df_%d" % b], tile=tn)
-                v(dh(768), lambda b=b: ts(T[eq][:, 768 * b:768 * b + 768], T.df[:, 768 * b:768 * b + 768], 0.0, None, A.is_equal),
-                  ["df_%d" % b], ["%s_%d" % (eq, b)])
-            else:
-                op("v", 2 * dv(256) + 2 * dv(128), lambda B, ks=ks, cmp=cmp: [cmp(B, 256 * (k % 2), k, h) for k in ks for h in range(2)],
-                   [Lname], ["%s_%d" % (eq, b)], tile=tn)
-        tn = "EQ%s%d" % (tag, t)
-        for b in range(4):
-            def sums(B, b=b):
+            def sums(B, blocks=blocks):
                 r = []
-                for k in (2 * b, 2 * b + 1):
-                    o = 384 * k
-                    r.append(lambda k=k, o=o: mm(B[:, k:k + 1], T[eq][:, o:o + 128], T.wt[:], True, True))
-                    r.append(lambda k=k, o=o: mm(B[:, 8 + k:9 + k], T[eq][:, o + 128:o + 256], T.wbig[:], True, False))
-                    r.append(lambda k=k, o=o: mm(B[:, 8 + k:9 + k], T[eq][:, o + 256:o + 384], T.wt[:], False, True))
+                for a in blocks:
+                    r.append((B[32:40, 16 * a:16 * a + 16], T.WD[:], T[eq][:, EQO[a]:EQO[a] + 16], False, a == 15, 16))
+                    if a < 15:
+                        r.append((B[32:40, 16 * a + 16:256], T.WO[:], T[eq][:, EQO[a] + 16:EQO[a + 1]], False, False, EQN[a] - 16))
                 return r
-            op("t", pe(64, 64, 64, 64, 64, 64), sums, ["%s_%d" % (eq, b), "wt", "wbig"], [], tile=tn)
-        return tn
+            t_(tn, sums, [nm, "WD", "WO", tn], [tn])
+        sp(sa(256), lambda B: act(T[buf][32:40, :], B[32:40, 0:256], AF.Sign), tn, [], [buf + "b"])
 
-    def place(t, par, first):
-        v(dg(256), lambda: V.tensor_tensor(T.A1[:], T["Lc%d" % par][:, 0:16].indirect(T.zl[:, 0:16]), T.dmask[:], A.mult),
-          ["Lc%d" % par, "zl", "dmask"], ["A1"])
+    def place(t):
         tn = "cW%d" % t
-        spread_lists("A1", tn)
-        if not first:
-            vp(one, lambda B: ts(T["cu%d" % par][:], B[:, 0:16], -1.0, 2048.0, A.mult, A.add), tn, [], ["cu%d" % par])
+        t_(tn, wrap("TC", 8, 0), ["TCa", "W72"])
+        if t >= 0:
+            vp(one, lambda B: ts(T.cu[:], B[:, 0:16], -1.0, 2048.0, A.mult, A.add), tn, [], ["cu"])
         if t < NT - 1:
-            vp(one, lambda B: ts(T.uf[:], B[:, 0:16], 0.25, 1536.375, A.mult, A.add), tn, [], ["uf"])
-            v(one, lambda: ts(T["vl%d" % par][:], T.uf[:], -1.0, 2048.0, A.mult, A.add), ["uf"], ["vl%d" % par])
+            vp(one, lambda B: ts(T.vl[:], B[:, 0:16], -0.25, 511.625, A.mult, A.add), tn, [], ["vl"])
+        if t >= 0:
+            sp(sone, lambda B: act(T.cW[:], B[:, 0:16], AF.Copy), tn, [], ["cW"])
 
-    op("t", pe(64, 64), halves("UW", T.blk1[:]), ["UW", "blk1"], [], tile="cut0")
-    vp(one, lambda B: V.tensor_copy(T.Lc1[:], B[:, 0:16]), "cut0", [], ["Lc1"])
-    place(-1, 1, True)
+    place(-1)
 
     def step(t):
         p, q = t % 2, 1 - t % 2
         last = t == NT - 1
         k0 = (t + 12) % 16
-        Z, Kn, Ku, Gn, Gu, xg = "Z%d" % t, "Kn%d" % p, "Ku%d" % p, "Gn%d" % p, "Gu%d" % p, "xg%d" % p
-        Lc, cu, dcu, dwu, dwl, cutv = "Lc%d" % p, "cu%d" % p, "dcu%d" % p, "dwu%d" % p, "dwl%d" % p, "cutv%d" % p
-        Gn1, Gu1, vl = "Gn%d" % q, "Gu%d" % q, "vl%d" % q
-        z0, z1 = 256 * t, 256 * t + 256
-        v(dg(256), lambda: V.tensor_copy(T[Kn][:], T.CAN[:, 0:1024].indirect(T[vl][:])), ["CAN", vl], [Kn])
-        v(dh(256), lambda: ts(T[Ku][:], T[Kn][:], -1.0, 2048.0, A.mult, A.add), [Kn], [Ku])
+        Z, Gn, Gu, TW, sI = "Z%d" % t, "Gn%d" % p, "Gu%d" % p, "TW%d" % p, "sI%d" % p
+        Gn1, Gu1, sI1 = "Gn%d" % q, "Gu%d" % q, "sI%d" % q
+        z0 = 512 * t
+        zz = T.Z[:, z0:z0 + 256]
+        Kn = T.Kn[:, 16:272]
+        s(sg(256), lambda: act(Kn, T.CAN[:, 0:1024].indirect(T.vl[:]), AF.Copy), ["CAN", "vl"], ["Kn"])
+        tn = "Kt%d" % t
+        t_(tn, lambda B: [(B[32 * u:32 * u + 32, a:256:16], T.Kn[32 * u:32 * u + 32, 16 * a:16 * a + 32], T.RO[32 * u:32 * u + 32, :], True, True, 32)
+                          for a in range(16) for u in range(4)], ["Kn", "Knp", "RO"], [tn])
+        t_(tn, lambda B: [(B[32 * u:32 * u + 16, a:256:16], T.Kn[32 * u:32 * u + 32, 16 * a + 16:16 * a + 32], T.RE[32 * u:32 * u + 32, :], True, True, 16)
+                          for a in range(16) for u in range(4)], ["Kn", "RE", tn], [tn])
+        vp(dv(256), lambda B: ts(T.Ku[:], B[:, 0:256], -1.0, 2048.0, A.mult, A.add), tn, [], ["Ku"])
         for c in range(4):
-            s(sg(1024), lambda c=c: S.activation(T[xg][:, 1024 * c:1024 * c + 1024],
-              T.X[:, 0:4096].indirect(T[Gu][:, 64 * c:64 * c + 64]), AF.Copy), XC + [Gu], ["%s_%d" % (xg, c)])
-        v(dh(256), lambda: ts(T.UW[:], T[Gn][:], T.RM1[:, k0:k0 + 1], T.RM2[:, k0:k0 + 1], A.mult, A.add), [Gn, "RM1", "RM2"], ["UW"])
-
-        def callsL(B):
-            r = []
-            for h in range(2):
-                r.append(lambda h=h: mm(B[:, 8 * h:8 * h + 8], T[Gn][:, 128 * h:128 * h + 128], T.selk[:, 8 * t:8 * t + 8], True, True))
-                r.append(lambda h=h: mm(B[:, 16 + 8 * h:24 + 8 * h], T.UW[:, 128 * h:128 * h + 128], T.blk1[:], True, True))
-            return r
-        op("t", pe(64, 64, 64, 64), callsL, [Gn, "UW", "selk", "blk1"], [], tile="LwU%d" % t)
-        op("s", sa(32), lambda B: [lambda: S.activation(T.LwU[:], B[:, 0:32], AF.Copy)], [], ["LwU"], tile="LwU%d" % t)
-        tn = same(t, "w", "UW", 16, "LwU", "eqw", True)
-        vp(one, lambda B: ts(T.nw[:], B[:, 0:16], T.thr[:], -10000.0, A.is_gt, A.mult), tn, ["thr"], ["nw"])
-        v(one, lambda: V.tensor_tensor(T.n1w[:], T.nw[:], T.LwU[:, 0:16], A.add), ["nw", "LwU"], ["n1w"])
-        v(dg(256), lambda: V.tensor_tensor(T.A2w[:], T.n1w[:, 0:16].indirect(T.zl[:, 0:16]), T.in1c[:], A.max), ["n1w", "zl", "in1c"], ["A2w"])
-        spread_lists("A2w", "W2w%d" % t)
-        vp(one, lambda B: ts(T[dwu][:], B[:, 0:16], -1.0, 63488.0, A.mult, A.add), "W2w%d" % t, [], [dwu])
-        vp(one, lambda B: ts(T.ufw[:], B[:, 0:16], -0.25, 16896.625, A.mult, A.add), "W2w%d" % t, [], ["ufw"])
-        v(one, lambda: ts(T[dwl][:], T.ufw[:], -1025.0, None, A.add), ["ufw"], [dwl])
-        s(sg(256), lambda: S.activation(T.xw[:], T.X[:].indirect(T[dwu][:]), AF.Copy), XR + [dwu], ["xw"])
-        s(sg(256), lambda: S.activation(T.cw[:], T.CAN[:].indirect(T[dwl][:]), AF.Copy), ["CAN", "CANd", dwl], ["cw"])
-        v(dh(256), lambda: ts(T.r2[:], T.xw[:], 4.0, BIAS + 63.0, A.add, A.min), ["xw"], ["r2"])
-        for h in range(2):
-            s(sg(2048), lambda h=h: S.activation(T.zrep[:, 2048 * h:2048 * h + 2048], T.Z[:, z0:z1].indirect(T.zl[:, 128 * h:128 * h + 128]), AF.Copy),
-              [Z, "zl"], ["zrep%d" % h])
-        for h in range(2):
-            v(dg(2048), lambda h=h: V.tensor_tensor(T.sc[:, 2048 * h:2048 * h + 2048], T.X[:, 0:4096].indirect(T[Ku][:, 128 * h:128 * h + 128]),
-              T.zrep[:, 2048 * h:2048 * h + 2048], A.max), XC + [Ku, "zrep%d" % h], ["sc%d" % h])
-
-            def callsK(B, h=h):
-                r = [lambda: mm(B[:, 128 * h:128 * h + 128], T[Kn][:, 128 * h:128 * h + 128], T.I16[:], True, False)]
-                for k in range(16):
-                    r.append(lambda k=k: mm(B[:, 128 * h + k:128 * h + 128:16], T.sc[:, 2048 * h + k:2048 * h + 2048:16], T.blkS[:], False, k == 15))
-                return r
-            op("t", pe(128, *([64] * 16)), callsK, [Kn, "I16", "blkS", "sc%d" % h], [], tile="key%d" % t)
-        vp(dv(256), lambda B: V.tensor_tensor_scan(T.sco[:], T.resetv[:], B[:, 0:256], 0.0, A.add, A.max), "key%d" % t, ["resetv"], ["sco"])
+            s(sg(1024), lambda c=c: act(T.xg[:, 1024 * c:1024 * c + 1024], T.X[:, 0:4096].indirect(T[Gu][:, 64 * c:64 * c + 64]), AF.Copy, scale=-1.0),
+              XC + [Gu], ["xg_%d" % c])
+        t_("TW%d" % t, lambda B: [(B[0:8, 0:256], T.selk[:, 8 * t:8 * t + 8], T[Gn][:], True, True, 256)], [Gn, "selk%d" % t])
+        sp(sa(256), lambda B: act(T[TW][0:8, :], B[0:8, 0:256], AF.Copy), "TW%d" % t, [], [TW + "a"])
+        t_("rw%d" % t, lambda B: [(B[:, 0:256], T.E8[0:8, :], T[TW][0:8, :], True, True, 256)] + wrap(TW, 8, 256)(B), [TW + "a", "E8", "W72"])
+        sp(sa(272), lambda B: act(T.repw[:], B[:, 0:272], AF.Identity, bias=1536.375, scale=0.25), "rw%d" % t, [], ["repw"])
+        s(sone, lambda: act(T.uW[:], T.repw[:, 256:272], AF.Copy), ["repw"], ["uW"])
+        v(one, lambda: ts(T.cwl[:], T.repw[:, 256:272], -1.0, 2048.0, A.mult, A.add), ["repw"], ["cwl"])
+        s(sg(256), lambda: act(T.cw[:], T.CAN[:, 0:1024].indirect(T.cwl[:]), AF.Copy), ["CAN", "cwl"], ["cw"])
+        later("w", t, "repw", "uW", "eqw", TW)
+        t_("yw%d" % t, wrap(TW, 40, 0), [TW + "a", TW + "b", "W72"])
+        if TWICE:
+            s(sa(256), lambda: act(T.Z[:, z0 + 256:z0 + 512], zz, AF.Copy), [Z], ["Zb"])
+        tn = "key%d" % t
+        t_(tn, lambda B: [(B[:, 0:256], T.zero[:], T.c160[:], True, False, 256)]
+           + [(B[:, 128 * h:128 * h + 128], T.Kn[:, 16 + 128 * h:144 + 128 * h], T.I16[:], False, False, 128) for h in range(2)],
+           ["zero", "c160", "Kn", "I16", "Ku"], [tn])
+        for c in range(4):
+            w = 2 if TWICE else 1
+            op("v", 4 // w * dg(256 * w),
+               [lambda k=k, w=w: V.tensor_tensor(T.sc[:, 256 * k:256 * (k + w)], T.X[:, 0:4096].indirect(T.Ku[:, 16 * k:16 * (k + w)]),
+                                                 T.Z[:, z0:z0 + 256 * w], A.max) for k in range(4 * c, 4 * c + 4, w)],
+               XC + ["Ku", Z] + (["Zb"] if TWICE else []), ["sc%d" % c])
+            t_(tn, lambda B, c=c: [(B[:, 128 * h + k:128 * h + 128:16], T.sc[:, 256 * k + 128 * h:256 * k + 128 * h + 128], T.blkS[:], False,
+                                    k == 15 and h == 1, 64) for k in range(4 * c, 4 * c + 4) for h in range(2)], ["sc%d" % c, "blkS", tn], [tn])
+        vp(dv(256), lambda B: V.tensor_tensor_scan(T.sco[:], T.resetv[:], B[:, 0:256], 0.0, A.add, A.max), tn, ["resetv"], ["sco"])
         v(one, lambda: ts(T.q1[:], T.sco[:, 15:256:16], 2047.0, None, A.add), ["sco"], ["q1"])
         v(one, lambda: ts(T.q2[:], T.q1[:], 4095, None, A.bitwise_and), ["q1"], ["q2"])
-        v(one, lambda: ts(T[Lc][:], T.q2[:], -2047.0, None, A.add), ["q2"], [Lc])
-        place(t, p, False)
+        v(one, lambda: ts(T.Lc[:], T.q2[:], -2047.0, None, A.add), ["q2"], ["Lc"])
+        t_("T1%d" % t, lambda B: [(B[0:8, 128 * h:128 * h + 128], T.Lc[:, 8 * h:8 * h + 8], T.I16[:], True, True, 128) for h in range(2)], ["Lc", "I16"])
+        sp(sa(256), lambda B: act(T.TC[0:8, :], B[0:8, 0:256], AF.Copy), "T1%d" % t, [], ["TCa"])
+        place(t)
+        s(sg(256), lambda: act(T.xc[:], T.X[:, 0:4096].indirect(T.cu[:]), AF.Identity, bias=-BIAS / 2 - 0.25, scale=0.5), XC + ["cu"], ["xc"])
         if not last:
             snt, arr = "snt%d" % (t + 1), "arr%d" % (t + 1)
-            v(dg(256), lambda: V.tensor_tensor(T.xs[:], T.X[:, 0:4096].indirect(T[cu][:]), T.Z[:, z0:z1], A.add), XC + [cu, Z], ["xs"])
-            v(dh(256), lambda: ts(T.ZS[:, z0:z1], T.xs[:], 0.5, -0.25, A.mult, A.add), ["xs"], ["zs%d" % t])
+            t_("ZS%d" % t, lambda B: [(B[:, 0:256], T.Ih[:], zz, True, False, 256), (B[:, 0:256], T.Ib[:], T.xc[:], False, True, 256)], ["Ih", "Ib", Z, "xc"])
+            sp(sa(256), lambda B: act(T.ZS[:, 256 * t:256 * t + 256], B[:, 0:256], AF.Identity, bias=BIAS / 2), "ZS%d" % t, [], ["zs%d" % t])
             dst = T.cores[(rank + 1 + t % 3) % len(T.cores)]
             rid, pid = topo.addr(dst)[0], topo.addr(dst)[1]
             ne = len(topo.engines(core, dst))
-            op("g", 1.0, [lambda: g.remote_dma(T.Z[:, z1:z1 + 256], T.ZS[:, z0:z1], T.sem[arr], T.sem[snt], pid=pid, routing_id=rid,
+            op("g", 1.0, [lambda: g.remote_dma(T.Z[:, z0 + 512:z0 + 768], T.ZS[:, 256 * t:256 * t + 256], T.sem[arr], T.sem[snt], pid=pid, routing_id=rid,
                                                dma_engine_mask=topo.mask(core, dst))], ["zs%d" % t], ["way%d" % t], sem=snt, cnt=ne)
             op("x", 0.0, [], ["way%d" % t], ["Z%d" % (t + 1)], lat=2.5, sem=arr, cnt=ne)
-        s(sg(256), lambda: S.activation(T[cutv][:], T.X[:, 0:4096].indirect(T[cu][:]), AF.Identity, bias=BIAS / 2 - 0.25, scale=0.5), XC + [cu], [cutv])
-        op("t", pe(128, 128), lambda B: [lambda h=h: mm(B[:, 128 * h:128 * h + 128], T.A1[:, 128 * h:128 * h + 128], T.I16[:], True, True)
-                                         for h in range(2)], ["A1", "I16"], [], tile="SP%d" % t)
-        vp(dv(256), lambda B: V.tensor_copy(T.SPs[:], B[:, 0:256]), "SP%d" % t, [], ["SPs"])
-        tn = same(t, "c", "SPs", 0, Lc, "eqc", False)
-        vp(one, lambda B: ts(T.nc[:], B[:, 0:16], T.thr[:], -10000.0, A.is_gt, A.mult), tn, ["thr"], ["nc"])
-        v(one, lambda: V.tensor_tensor(T.n1c[:], T.nc[:], T[Lc][:], A.add), ["nc", Lc], ["n1c"])
-        v(dg(256), lambda: V.tensor_tensor(T.A2c[:], T.n1c[:, 0:16].indirect(T.zl[:, 0:16]), T.in1c[:], A.max), ["n1c", "zl", "in1c"], ["A2c"])
-        spread_lists("A2c", "W2c%d" % t)
-        vp(one, lambda B: ts(T[dcu][:], B[:, 0:16], -1.0, 63488.0, A.mult, A.add), "W2c%d" % t, [], [dcu])
-        for b in range(8):
+        t_("rc%d" % t, lambda B: [(B[:, 0:256], T.E8[0:8, :], T.TC[0:8, :], True, True, 256)], ["TCa", "E8"])
+        sp(sa(256), lambda B: act(T.repc[:], B[:, 0:256], AF.Copy), "rc%d" % t, [], ["repc"])
+        later("c", t, "repc", "cW", "eqc", "TC")
+        t_("yc%d" % t, wrap("TC", 40, 0), ["TCa", "TCb", "W72"])
+        vp(one, lambda B: V.tensor_tensor(T.yc[:], B[:, 0:16], T.dum[:, 0:16], A.max), "yc%d" % t, ["dum"], ["yc"])
+        v(one, lambda: ts(T.dcu[:], T.yc[:], -1.0, 2048.0 - 15 * BIG, A.mult, A.add), ["yc"], ["dcu"])
+        banks = [(h, kb) for h in range(2) for kb in sorted(range(4), key=lambda kb: kb != k0 % 4)]
+        for b, (h, kb) in enumerate(banks):
             tn = "d%d_%d" % (t, b)
-            h, kb = b // 4, 4 * (b % 4)
-
-            def callsD(B, h=h, kb=kb):
-                r = []
-                for j in range(4):
-                    r.append(lambda j=j: mm(B[:, 128 * j:128 * j + 128], T.Ib[:], T[xg][:, 2048 * h + kb + j:2048 * h + 2048:16], True, False))
-                    r.append(lambda j=j: mm(B[:, 128 * j:128 * j + 128], T.Ibn[:], T.Z[:, z0 + 128 * h:z0 + 128 * h + 128], False, True))
-                return r
-            op("t", pe(*([128] * 8)), callsD, ["Ib", "Ibn", Z] + ["%s_%d" % (xg, c) for c in (2 * h, 2 * h + 1)], [], tile=tn)
-            op("s", sa(512), lambda B, b=b: [lambda: S.activation(T.ab[:, 512 * b:512 * b + 512], B[:], AF.Abs)], [], ["ab%d" % b], tile=tn)
-            if b % 2 == 1:
-                c = b // 2
-                v(dh(1024), lambda c=c: ts(T.th[:, 1024 * c:1024 * c + 1024], T.ab[:, 1024 * c:1024 * c + 1024], T.lim[:, t:t + 1], None, A.is_gt),
-                  ["ab%d" % (b - 1), "ab%d" % b, "lim%d" % t], ["th%d" % c])
-        for c in range(4):
-            h = c // 2
-            op("t", pe(*([64] * 8)), lambda B, c=c, h=h: [
-                lambda k=k: mm(B[:, 128 * h + k:128 * h + 128:16], T.th[:, 2048 * h + 128 * k:2048 * h + 128 * k + 128], T.blkb[:], True, True)
-                for k in range(8 * (c % 2), 8 * (c % 2) + 8)], ["th%d" % c, "blkb"], [], tile="cnt%d" % t)
-        vp(dv(256), lambda B: ts(T.sevL[:], B[:, 0:256], 8.5, None, A.is_gt), "cnt%d" % t, [], ["sevL"])
-        vp(dv(256), lambda B: V.tensor_tensor(T.sevT[:], B[:, 0:256], T.thrk[:, 15 - t:271 - t], A.is_gt), "cnt%d" % t, ["thrk"], ["sevT"])
-        s(sg(256), lambda: S.activation(T.skrep[:], T.sevL[:].indirect(T.skl[:, 16 * t:16 * t + 16]), AF.Copy), ["sevL", "skl"], ["skrep"])
+            t_(tn, lambda B, h=h, kb=kb: [(B[:], T[sI][:], T.xg[:, 2048 * h + kb:2048 * h + 2048:4], True, False, 512)]
+               + [(B[:, j:512:4], T[sI][:], T.Z[:, z0 + 128 * h:z0 + 128 * h + 128], False, j == 3, 128) for j in range(4)],
+               [sI, Z, "xg_%d" % (2 * h), "xg_%d" % (2 * h + 1)])
+            if b in VBANKS:
+                vp(dv(512), lambda B, b=b: ts(T.th[:, 512 * b:512 * b + 512], B[:], GRID, GRID, A.add, A.not_equal), tn, [], ["th%d" % b])
+            else:
+                sp(sa(512), lambda B, b=b: act(T.ab[:, 512 * b:512 * b + 512], B[:], AF.Abs), tn, [], ["ab%d" % b])
+        run = []
+        for b in range(9):
+            if run and (b == 8 or b in VBANKS or len(run) == 2):
+                v(dh(512 * len(run)), lambda a=run[0], e=run[-1] + 1: ts(T.th[:, 512 * a:512 * e], T.ab[:, 512 * a:512 * e], 16.0, None, A.is_gt),
+                  ["ab%d" % x for x in run], ["th%d" % x for x in run])
+                run = []
+            if b < 8 and b not in VBANKS:
+                run.append(b)
+        for b0 in range(0, 8, 2):
+            t_("cnt%d" % t, lambda B, b0=b0: [(B[:, 128 * banks[b][0] + banks[b][1] + 4 * j:128 * banks[b][0] + 128:16], T.th[:, 512 * b + j:512 * b + 512:4],
+                                               T.blkb[:], True, True, 64) for b in (b0, b0 + 1) for j in range(4)], ["th%d" % b0, "th%d" % (b0 + 1), "blkb"])
+        sp(sa(256), lambda B: act(T.sg[:], B[:, 0:256], AF.Sign, bias=-8.5), "cnt%d" % t, [], ["sg"])
+        t_("sk%d" % t, lambda B: [(B[64:72, 128 * h:128 * h + 128], T.blkb[:], T.th[:, 2048 * h + k0 // 4:2048 * h + 512:4], True, True, 128) for h in range(2)],
+           ["th0", "th4", "blkb"])
+        sp(sa(256) + 0.02, lambda B: act(T[TW][64:72, :], B[64:72, 0:256], AF.Sign, bias=-8.5, accum_out=T.acc[64:72, :]), "sk%d" % t, [], [TW + "c", "acc"])
         if not last:
-            op("t", pe(64), lambda B: [lambda: mm(B[:, 0:16], T.onesb[:], T.sevL[:, k0:256:16], True, True)], ["onesb", "sevL"], [], tile="S%d" % t)
-            op("s", sa(16) + 0.14, lambda B: [lambda: S.activation(T.sj[:], B[:, 0:16], AF.Identity, bias=385.0, accum_out=T.sf[:])],
-               [], ["sf"], tile="S%d" % t)
-            v(one, lambda: ts(T.si[:], T.sf[:], 0.25, -4.375, A.mult, A.add), ["sf"], ["si"])
-            v(one, lambda: ts(T.lim[:, t + 1:t + 2], T.si[:], -4.0, T.sf[:], A.mult, A.add), ["si", "sf"], ["lim%d" % (t + 1)])
+            t_("S%d" % t, lambda B: [(B[:, 0:1], T.c32[64:72, :], T.acc[64:72, :], True, True, 256)], ["c32", "acc"])
+            sp(sone, lambda B: act(T.p32[:], B[:, 0:1], AF.Copy), "S%d" % t, [], ["p32"])
+            s(sone, lambda: act(T.si[:], T.p32[:], AF.Identity, bias=1535.625, scale=-5.0), ["p32"], ["si"])
+            s(sone, lambda: act(T.s0[:], T.si[:], AF.Identity, bias=T.p32[:], scale=0.2), ["si", "p32"], ["s0"])
+            s(sa(128), lambda: act(T[sI1][:], T.Ioff[:], AF.Relu, bias=T.s0[:]), ["Ioff", "s0"], [sI1])
+        t_("yw%d" % t, wrap(TW, 72, 16), [TW + "a", TW + "b", TW + "c", "W72"])
+        vp(one, lambda B: V.tensor_tensor(T.yw[:], B[:, 0:32], T.dum[:], A.max), "yw%d" % t, ["dum"], ["yw"])
+        v(one, lambda: ts(T.dwu[:], T.yw[:, 0:16], -1.0, 2048.0 - 15 * BIG, A.mult, A.add), ["yw"], ["dwu"])
+        v(one, lambda: ts(T.dwl[:], T.yw[:, 16:32], -0.25, 511.625 - 3.5 * BIG, A.mult, A.add), ["yw"], ["dwl"])
 
-        def blend(ident, extra, sevs):
-            def calls(B):
-                r = []
-                for o, m in ((0, "I8n"), (256, "I8p")):
-                    r.append(lambda o=o: mm(B[:, o:o + 256], ident, T[Gn][:], True, False))
-                    if extra:
-                        r.append(lambda o=o: mm(B[:, o:o + 256], T.wide[:, 15 - t:143 - t], T.SPs[:], False, False))
-                    for n in sevs:
-                        for h in range(2):
-                            r.append(lambda o=o, m=m, h=h, n=n: mm(B[:, o + 128 * h:o + 128 * h + 128], T[n][:, 128 * h:128 * h + 128], T[m][:],
-                                                                   False, h == 1 and n == sevs[-1]))
-                return r
-            return calls
-        op("t", pe(*([256] * 6)), blend(T.It[:, 128 * t:128 * t + 128], True, ["sevT"]),
-           ["It", Gn, "wide", "SPs", "sevT", "I8n", "I8p"], [], tile="G%d" % t)
-        vp(dv(256), lambda B: V.tensor_tensor(T.gm[:], T[Kn][:], B[:, 0:256], A.max), "G%d" % t, [Kn], ["gm"])
-        vp(dv(256), lambda B: V.tensor_tensor(T[Gn1][:], T.gm[:], B[:, 256:512], A.min), "G%d" % t, ["gm"], [Gn1])
+        def sign(B, o, m, stop):
+            return [(B[:, o + 128 * h:o + 128 * h + 128], T.sg[:, 128 * h:128 * h + 128], T[m][:], False, stop and h == 1, 128) for h in range(2)]
+        It = T.It[:, 128 * t:128 * t + 128]
+        t_("G%d" % t, lambda B: [(B[:, 0:256], It, Kn, True, False, 256)] + sign(B, 0, "IBp", False)
+           + [(B[:, 0:256], T.W72[0:8, 15 - t:143 - t], T.TC[0:8, :], False, True, 256), (B[:, 256:512], It, T[Gn][:], True, False, 256)]
+           + sign(B, 256, "IBn", False) + [(B[:, 256:512], T.W72[0:9, 15 - t:143 - t], T.TC[0:9, :], False, True, 256)],
+           ["It%d" % t, "Kn", Gn, "W72", "TCa", "sg", "IBp", "IBn"])
+        sp(sa(256), lambda B: act(T.ga[:], B[:, 0:256], AF.Identity, bias=-BIG), "G%d" % t, [], ["ga"])
+        vp(dv(256), lambda B: V.tensor_tensor(T[Gn1][:], T.ga[:], B[:, 256:512], A.max), "G%d" % t, ["ga"], [Gn1])
         if not last:
             v(dh(256), lambda: ts(T[Gu1][:], T[Gn1][:], -1.0, 2048.0, A.mult, A.add), [Gn1], [Gu1])
-        op("t", pe(*([256] * 6)), blend(T.I16[:], False, ["sevL", "skrep"]), ["I16", Gn, "sevL", "skrep", "I8n", "I8p"], [], tile="N%d" % t)
-        vp(dv(256), lambda B: V.tensor_tensor(T.cm[:], T.cw[:], B[:, 0:256], A.max), "N%d" % t, ["cw"], ["cm"])
-        vp(dv(256), lambda B: V.tensor_tensor(T.cn[:], T.cm[:], B[:, 256:512], A.min), "N%d" % t, ["cm"], ["cn"])
-        v(ds(256), lambda: V.tensor_copy(T.CAN[:].indirect(T[dwl][:]), T.cn[:]), ["cn", dwl], ["CAN", "CANd"])
-
-        def callsR(B):
-            r = [lambda: mm(B[:, 0:256], T.Ih[:], T.xw[:], True, False),
-                 lambda: mm(B[:, 0:256], T.Ih[:], T.Z[:, z0:z1], False, False),
-                 lambda: mm(B[:, 0:256], T.qtr[:], T.ones16[:], False, False)]
-            for h in range(2):
-                r.append(lambda h=h: mm(B[:, 128 * h:128 * h + 128], T.skrep[:, 128 * h:128 * h + 128], T.I5n[:], False, h == 1))
-            for h in range(2):
-                r.append(lambda h=h: mm(B[:, 256 + 128 * h:384 + 128 * h], T.skrep[:, 128 * h:128 * h + 128], T.Ib[:], True, True))
-            return r
-        op("t", pe(256, 256, 256, 128, 128, 128, 128), callsR, ["Ih", "xw", Z, "qtr", "ones16", "skrep", "I5n", "Ib"], [], tile="R%d" % t)
-        vp(dv(256), lambda B: V.tensor_tensor(T.r2m[:], T.r2[:], B[:, 256:512], A.mult), "R%d" % t, ["r2"], ["r2m"])
-        vp(dv(256), lambda B: V.tensor_tensor(T.rn[:], T.r2m[:], B[:, 0:256], A.max), "R%d" % t, ["r2m"], ["rn"])
-        v(ds(256), lambda: V.tensor_copy(T.X[:].indirect(T[dwu][:]), T.rn[:]), ["rn", dwu], XR)
-        v(ds(256), lambda: V.tensor_copy(T.X[:].indirect(T[dcu][:]), T[cutv][:]), [cutv, dcu], XR)
+        t_("N%d" % t, lambda B: [(B[:, 0:256], T.I16[:], T.cw[:], True, False, 256)] + sign(B, 0, "IBp", True)
+           + [(B[:, 256:512], T.I16[:], T[Gn][:], True, False, 256)] + sign(B, 256, "IBn", True), ["I16", "cw", Gn, "sg", "IBp", "IBn"])
+        sp(sa(512), lambda B: act(T.cf[:], B[:], AF.Identity, bias=-BIG), "N%d" % t, [], ["cf"])
+        v(ds(256), lambda: V.tensor_tensor(T.CAN[:].indirect(T.dwl[:]), T.cf[:, 0:256], T.cf[:, 256:512], A.max), ["cf", "dwl"], ["CAN", "CANd"])
+        xw = T.xg[:, k0:4096:16]
+        XG = ["xg_%d" % c for c in range(4)]
+        s(sa(256), lambda: act(T.r1[:], xw, AF.Relu, bias=BIAS + 59.0), XG, ["r1"])
+        t_("R%d" % t, lambda B: [(B[:, 256:512], T.Ihn[:], xw, True, False, 256), (B[:, 256:512], T.Ih[:], zz, False, False, 256),
+                                 (B[:, 256:512], T.E8[64:72, :], T[TW][64:72, :], False, True, 256),
+                                 (B[:, 0:256], T.Ibn[:], T.r1[:], True, False, 256), (B[:, 0:256], T.RA[0:72, :], T[TW][0:72, :], False, True, 256)],
+           XG + ["Ihn", "Ih", "Ibn", Z, "r1", "E8", "RA", TW + "a", TW + "b", TW + "c"])
+        sp(sa(512), lambda B: act(T.rf[:], B[:], AF.Relu, bias=-512.25), "R%d" % t, [], ["rf"])
+        v(ds(256), lambda: V.tensor_tensor(T.X[:].indirect(T.dwu[:]), T.rf[:, 0:256], T.rf[:, 256:512], A.add), ["rf", "dwu"], XR)
+        v(ds(256), lambda: V.tensor_tensor(T.X[:].indirect(T.dcu[:]), T.xc[:], T.c160[:], A.add), ["xc", "dcu", "c160"], XR)
 
     for t in range(NT):
         step(t)
@@ -374,17 +338,17 @@ def rank_program(g, core, T, topo):
     def store(name, out, src, R):
         op("y", 0.1, [lambda: Y.dma_start(out, src)], R, ["y" + name], lat=3.0, sem="st_" + name, cnt=16)
 
-    s(sa(1024), lambda: S.activation(T.lo[:], T.CAN[:, 0:1024], AF.Identity, bias=2048.0, scale=-1.0), ["CAN"], ["lo"])
+    s(sa(1024), lambda: act(T.lo[:], T.CAN[:, 0:1024], AF.Identity, bias=2048.0, scale=-1.0), ["CAN"], ["lo"])
     store("ol", T.yl[:], T.lo[:], ["lo"])
-    v(dv(256), lambda: ts(T.go[:], T["Gn%d" % (NT % 2)][:], -1.0, 2048.0, A.mult, A.add), ["Gn%d" % (NT % 2)], ["go"])
+    s(sa(256), lambda: act(T.go[:], T["Gn%d" % (NT % 2)][:], AF.Identity, bias=2048.0, scale=-1.0), ["Gn%d" % (NT % 2)], ["go"])
     store("og", T.yg[:], T.go[:], ["go"])
     for c in range(4):
         a, b = 1024 * c, 1024 * c + 1024
         if c < 3:
-            v(dh(1024), lambda a=a, b=b: ts(T.th[:, a:b], T.X[:, a:b], -BIAS, None, A.add), ["X%d" % c], ["th%d" % c])
+            v(dh(1024), lambda a=a, b=b: ts(T.sc[:, a:b], T.X[:, a:b], -BIAS, None, A.add), ["X%d" % c], ["sc%d" % c])
         else:
-            s(sa(1024), lambda a=a, b=b: S.activation(T.th[:, a:b], T.X[:, a:b], AF.Identity, bias=-BIAS), ["X%d" % c], ["th%d" % c])
-        store("o%d" % c, T.yx[:, a:b], T.th[:, a:b], ["th%d" % c])
+            s(sa(1024), lambda a=a, b=b: act(T.sc[:, a:b], T.X[:, a:b], AF.Identity, bias=-BIAS), ["X%d" % c], ["sc%d" % c])
+        store("o%d" % c, T.yx[:, a:b], T.sc[:, a:b], ["sc%d" % c])
     emit(g, T, ops, schedule(ops))
 
 
@@ -423,7 +387,8 @@ def schedule(ops):
     for i in range(n - 1, -1, -1):
         prio[i] = ops[i]["c"] + ops[i]["lat"] + SYNC + max([prio[j] for j in succ[i]] or [0.0])
     for o in ops:
-        prio[o["i"]] += BONUS.get("".join(c for c in (o["W"] or [o["tile"]])[0] if c.isalpha()) + "_" + o["e"], 0.0)
+        o["n"] = "".join(c for c in (o["W"] or [o["tile"]])[0] if c.isalpha()) + "_" + o["e"]
+        prio[o["i"]] += BONUS.get(o["n"], 0.0)
     users = {}
     for o in ops:
         if o["tile"]:
@@ -450,7 +415,9 @@ def schedule(ops):
             cand.append((st, -prio[i], i, bk))
         if not cand:
             raise ValueError("no bank for any ready op")
-        st, _, i, bk = min(cand, key=lambda c: c[:3])
+        first = min(cand, key=lambda c: (c[0] + LOOK * ops[c[2]]["c"], c[1], c[2]))
+        end, eng = first[0] + LOOK * ops[first[2]]["c"], ops[first[2]]["e"]
+        st, _, i, bk = min((c for c in cand if ops[c[2]]["e"] == eng and c[0] <= end), key=lambda c: (c[1], c[0], c[2]))
         ready.remove(i)
         o = ops[i]
         if bk is not None:

@@ -4,8 +4,8 @@ A = AluOpType
 AF = ActivationFunctionType
 NT = 8
 BIAS = 160.0
-XW = 5120
-CW = 1280
+XW = 5568
+CW = 1392
 BIG = 8192.0
 GRID = 402653184.0
 EQN = [256 - 16 * a for a in range(16)]
@@ -16,20 +16,21 @@ SCRATCH = {}
 for _n, _s, _d in (
         ("X", XW, BF), ("CAN", CW, F4), ("cin", 1024, I4), ("tin", 256, I4), ("vin", 256, I4), ("zin", 256, BF),
         ("xg", 4096, BF), ("ab", 4096, BF), ("th", 4096, BF), ("sc", 4096, BF), ("lo", 1024, F4), ("go", 256, F4),
-        ("Kn", 272, HF), ("Ku", 256, U2), ("eqw", EQO[16], BF), ("eqc", EQO[16], BF), ("repw", 272, HF), ("repc", 256, HF),
-        ("uW", 16, F4), ("cW", 16, F4), ("TC", 256, HF), ("yw", 32, F4), ("yc", 16, F4), ("sco", 256, F4), ("q1", 16, I4), ("q2", 16, I4),
-        ("Lc", 16, HF), ("cu", 16, U2), ("vl", 16, U2), ("dwu", 16, U2), ("dwl", 16, U2), ("dcu", 16, U2), ("cwl", 16, U2),
+        ("Kn", 272, HF), ("Ku", 256, U2), ("eqw", EQO[16], BF), ("eqc", 512, BF), ("dw", 576, BF), ("repw", 272, HF), ("repc", 512, HF),
+        ("uW", 16, F4), ("A1", 256, HF), ("At", 256, HF), ("TC", 256, HF), ("yw", 32, F4), ("yc", 16, F4), ("sco", 256, I4), ("q2", 16, I4),
+        ("Lc", 16, F4), ("cu", 16, U2), ("vl", 16, U2), ("dwu", 16, U2), ("dwl", 16, U2), ("dcu", 16, U2),
         ("xc", 256, BF), ("r1", 256, BF), ("rf", 512, BF), ("cw", 256, HF), ("cf", 512, F4), ("ga", 256, HF), ("sg", 256, BF),
-        ("acc", 1, F4), ("p32", 1, F4), ("si", 1, HF), ("s0", 1, F4),
-        ("Z", 512 * NT, BF), ("ZS", 256 * NT, BF),
-        ("i128", 128, F4), ("pc", 1, F4), ("pci", 1, I4), ("col", 16, F4), ("k256", 256, F4), ("w144", 144, F4), ("c16", 128, F4),
-        ("RM", 16, F4), ("RMn", 16, F4), ("RO", 16, HF), ("RE", 16, HF), ("I16", 128, HF), ("Ib", 128, BF), ("Ibn", 128, BF), ("Ih", 128, BF),
-        ("Ihn", 128, BF), ("IBp", 128, BF), ("IBn", 128, BF), ("It", 1024, HF), ("Ioff", 128, F4), ("blkf", 8, F4), ("blkb", 8, BF),
-        ("blkS", 8, BF), ("selk", 64, HF), ("WD", 8, BF), ("WO", 8, BF), ("thr", 256, BF), ("W72", 144, HF), ("E8", 128, HF), ("RA", 128, HF),
-        ("dum", 32, F4), ("resetv", 256, F4), ("c160", 256, BF), ("zero", 128, BF), ("c32", 128, F4)):
+        ("acc", 1, F4), ("si", 1, HF), ("s0", 1, F4),
+        ("Z", 1024 * NT, BF), ("ZS", 256 * NT, BF),
+        ("pci", 1, I4), ("col", 2, F4), ("k256", 256, BF), ("I16", 128, HF), ("Ib", 128, BF), ("Ibn", 128, BF), ("Ih", 128, BF),
+        ("Ihn", 128, BF), ("IBp", 128, BF), ("IBn", 128, BF), ("Ioff", 128, F4), ("IB8", 8, HF), ("blk1", 8, HF),
+        ("blkb", 8, BF), ("blkS", 8, BF), ("WD", 8, BF), ("WO", 8, BF), ("WN", 8, BF), ("comb", 144, HF), ("thr", 256, BF), ("BLK", 256, HF),
+        ("dmask", 256, HF), ("WB", 144, HF), ("E8", 128, HF), ("RA", 128, HF), ("dum", 48, F4), ("resetv", 256, BF), ("c160", 256, BF),
+        ("krow", 128, HF), ("ones", 256, HF), ("neg", 144, HF), ("c32", 128, F4), ("zl", 32, U2), ("tmp", 128, HF)):
     SCRATCH[_n] = ("sbuf", [128, _s], _d)
 for _k in range(2):
-    for _n, _s, _d in (("Gn", 256, HF), ("Gu", 256, U2), ("TW", 256, HF), ("sI", 128, BF)):
+    for _n, _s, _d in (("Gn", 256, HF), ("Gu", 256, U2), ("TW", 512, HF), ("sI", 128, BF), ("lim", 1, F4), ("SEL", 128, HF), ("Wk", 144, HF),
+                       ("wW", 16, HF), ("It", 128, HF), ("cwl", 16, U2)):
         SCRATCH["%s%d" % (_n, _k)] = ("sbuf", [128, _s], _d)
 for _k in range(8):
     SCRATCH["ps%d" % _k] = ("psum", [128, 512], F4)
@@ -38,19 +39,42 @@ SEMAPHORES = (["qv", "qs", "qt", "qg"] + ["ld_" + n for n in ("cut", "z", "trail
               + ["st_" + n for n in ("o0", "o1", "o2", "o3", "ol", "og")]
               + ["arr%d" % k for k in range(1, NT)] + ["snt%d" % k for k in range(1, NT)])
 
-CY, GA, SC, PEC, PEF, SYNC = 0.00083, 1.5, 3.5, 0.0005, 0.002, 0.1
-BONUS = {'TCb_s': -2, 'key_t': 4, 'Kt_t': -3, 'T_t': 1, 'S_t': 4, 'sI_s': -6, 'cnt_t': -6, 'N_t': -2, 'rc_t': 1, 'X_v': 3, 'vl_v': -3, 'r_s': 2, 'Ku_v': -4, 'xc_s': -4, 'TWa_s': 1, 'th_v': -3, 'q_v': -2, 'sk_t': -6, 'cw_s': -6, 'TW_t': 0.5, 'yc_v': 0.5, 'selk_s': 6, 'CAN_v': 4, 'TCa_s': 3, 'dwl_v': -4, 'si_s': 3, 'sg_s': 3, 'sc_v': -1, 's_s': 3, 'rf_s': 6, 'Gn_v': -2, 'dcu_v': -3, 'Kn_s': -0.5, 'repc_s': 0.5, 'ga_s': 0.5, 'It_s': -0.5, 'yw_v': 2, 'repw_s': -3, 'ZS_t': -4, 'cwl_v': -0.5, 'TWc_s': 6, 'ab_s': -6, 'eqc_v': 2, 'sco_v': -1, 'xg_s': -3, 'yc_t': 3, 'cW_t': -1, 'zs_s': -2, 'Zb_s': -4, 'dwu_v': 3, 'rw_t': -6, 'Gu_v': -1, 'Pw_t': 2, 'p_s': 6, 'G_t': -0.5, 'R_t': 0.5, 'd_t': -4, 'Lc_v': 0.5, 'cf_s': -0.5, 'cW_s': 6, 'cu_v': 4, 'TWb_s': -4, 'eqw_v': -0.5}
-LOOK = 0.3
-VBANKS = ()
-TWICE = True
+CY, GA, SC, PEC, PEF, SF, SG, SYNC, WAY = 0.00087, 1.5, 3.5, 0.00049, 0.001, 0.075, 0.065, 0.11, 4.2
+ORDER = """
+sc_v0 SEL_g++ key_t0 Zc_g Ge_t xg_s3 d_t0 It_g++ sc_v1 Pw_t3 d_t2 xg_s2 d_t3 key_t1 sc_v2 d_t1 key_t2 ab_s3 d_t4 r_s sc_v3 d_t6 ab_s0 key_t3 ab_s1
+d_t5 ab_s4 th_v0 ZSe_t key_t4 ab_s5 d_t7 sco_v eqw_v11 ab_s6 eqw_v15 q_v Re_t th_v2 Lc_s cnt_t0 ab_s2 At_g Pw_t4 A_v sk_t TWb_s cnt_t2 th_v3 rc_t
+TWc_s TWd_g tv_v cnt_t3 repc_s cW_t R_t cu_v th_v1 cnt_t4 rf_s yw_t eqc_v xc_s cnt_t1 Pce_t cwl_s sg_s ZS_t yw_v cw_v Pc_t dwu_s zs_s G_t X_v
+TCb_s way_g yc_t ga_s Ne_t yc_v dwl_s vl_s Gn_v dcu_s N_t Az_g+ cut_v0 S_t Z_x cf_s rw_t+ cut_v1 si_v Gu_s cut_v2 cut_v3 CAN_v repw_s+ wW_s+
+Pw_t0+ cut_v4 s_v cut_v5 uW_v+ Kn_s+ sI_s cut_v6 Kt_t0+ eqw_v12+ cut_v7 eqw_v3+ xg_s0+ eqw_v6+ eqw_v4+ eqw_v10+ eqw_v0+ Kt_t1+ eqw_v1+ eqw_v13+
+Wk_g+++ eqw_v9+ eqw_v2+ eqw_v5+ Pw_t1+ xg_s1+ eqw_v8+ eqw_v7+ Ku_v+ Zb_g+ eqw_v14+ Pw_t2+
+""".split()
+PERIOD, SOON, AHEAD = 15.5, 0.05, 2.0
+VBANKS = (7,)
+LAST = {}
+LOADS = "cut trail x0 x1 x2 canal x3 z".split()
+SHORT = 0
+RUNS = ((0, 1), (2, 3), (4, 5), (6,), (7,))
+
+
+def phases(words):
+    ph = {}
+    for p, w in enumerate(words):
+        name = w.rstrip("+-")
+        kind = name.rstrip("0123456789")
+        ph.setdefault(kind, {})[int(name[len(kind):] or 0)] = PERIOD * (p / len(words) - w.count("+") + w.count("-"))
+    return {k: [d[j] for j in sorted(d)] for k, d in ph.items()}
+
+
+PHASE = phases(ORDER)
 
 
 def dv(n): return 0.06 + max(n, 64) * CY
 def dh(n): return 0.06 + max(n * 0.5, 64) * CY
 def dg(n): return 0.05 + n * GA * CY
 def ds(n): return 0.05 + n * SC * CY
-def sg(n): return 0.065 + n * GA * CY
-def sa(n): return 0.065 + n * CY
+def sg(n): return SG + n * GA * CY
+def sa(n): return SF + n * CY
+def ga(n): return 0.17 + 2 * n * CY
 def pe(*ns): return sum(ns) * PEC + PEF * len(ns) + 0.02
 
 
@@ -59,38 +83,70 @@ def rank_program(g, core, T, topo):
     if rank is None:
         return
     V, S, PE, Y = g.vector, g.scalar, g.tensor, g.sync
-    ops = []
+    ops, now = [], [None]
 
     def op(eng, cost, calls, R=(), W=(), tile=None, lat=0.0, sem=None, cnt=0):
         ops.append({"e": eng, "c": cost, "f": calls, "R": list(R), "W": list(W), "tile": tile, "lat": lat,
-                    "sem": sem, "cnt": cnt, "i": len(ops)})
+                    "sem": sem, "cnt": cnt, "i": len(ops), "t": now[0]})
 
     def v(cost, f, R, W): op("v", cost, [f], R, W)
     def s(cost, f, R, W): op("s", cost, [f], R, W)
     def vp(cost, f, tile, R, W): op("v", cost, lambda B: [lambda: f(B)], R, W, tile=tile)
     def sp(cost, f, tile, R, W): op("s", cost, lambda B: [lambda: f(B)], R, W, tile=tile)
+    def on_v(kind): return kind + "_v" in PHASE
     mm, act = PE.matmul, S.activation
 
     def t_(tile, prods, R, W=()):
         op("t", pe(*[p[5] for p in prods(T.ps0)]), lambda B: [lambda p=p: mm(*p[:5]) for p in prods(B)], R, W, tile=tile)
 
+    def parts(name, t, early, R1, late, R2):
+        tn = "%s%d" % (name, t)
+
+        def flags(ps, first): return [p[:3] + (first and j == 0, not first and j == len(ps) - 1, p[3]) for j, p in enumerate(ps)]
+        t_(tn, lambda B: flags(early(B), True), R1, [name + "e"])
+        t_(tn, lambda B: flags(late(B), False), R2 + [name + "e"])
+
     def ts(out, i0, s1, s2, o0, o1=None):
         if o1 is None:
             return V.tensor_scalar(out, i0, s1, None, o0)
         return V.tensor_scalar(out, i0, s1, s2, o0, o1)
-    one, sone = dv(64), sa(16)
 
-    def load(name, out, src, W, lat, R=()):
-        op("y", 0.1, [lambda: Y.dma_start(out, src)], R, W, lat=lat, sem="ld_" + name, cnt=16)
+    def pick(name, out, src, R, pat, cmp, base, cm):
+        n = 1
+        for _, b in pat:
+            n *= b
+        op("g", ga(n), [lambda: g.affine_select(out, src, pat, cmp, 0.0, base, cm)], R, [name])
 
-    load("cut", T.vin[0:8, :], T.cut[:], ["vin"], 2.0)
-    load("trail", T.tin[:], T.trail[:], ["tin"], 2.2)
-    load("canal", T.cin[:], T.canal[:], ["cin"], 3.0)
+    def lin(kind, out, src, scale, bias, n, R, W, tile=None, how="plain", relu=False, e=None):
+        if kind + "_g" in PHASE:
+            return pick(W[0], out, src, R, [[0, n]], A.is_ge, 0, 0)
+
+        def on_vector(x): return ts(out, x, bias, 0.0, A.add, A.max) if relu else ts(out, x, scale, bias, A.mult, A.add)
+        def on_scalar(x): return act(out, x, AF.Relu if relu else AF.Identity, bias=bias, scale=scale)
+        e = e or ("v" if on_v(kind) else "s")
+        f = on_vector if e == "v" else on_scalar
+        cost = {"v": {"plain": dv, "half": dh, "gather": dg}, "s": {"plain": sa, "half": sa, "gather": sg}}[e][how](n)
+        op(e, cost, (lambda B: [lambda: f(src(B))]) if tile else [lambda: f(src)], R, W, tile=tile)
+
+    def sign(kind, out, src, bar, tile, W, half=False):
+        if on_v(kind):
+            vp(dv(256), lambda B: ts(out, src(B), bar, 0.5, A.is_gt, A.subtract) if half else ts(out, src(B), bar, 2.0, A.is_gt, A.mult), tile, [], W)
+        else:
+            sp(sa(256), lambda B: act(out, src(B), AF.Sign, bias=-bar), tile, [], W)
+    one = dv(64)
+
+    def load(name, out, src, W, lat):
+        op("y", 0.1, [lambda: Y.dma_start(out, src)], [], W, lat=lat, sem="ld_" + name, cnt=16)
+
+    what = {"cut": (T.vin[0:8, :], T.cut[:], "vin", 0.0), "trail": (T.tin[:], T.trail[:], "tin", 0.3), "canal": (T.cin[:], T.canal[:], "cin", 1.3),
+            "z": (T.zin[:], T.z[:], "zin", 0.1)}
     for q in range(4):
-        load("x%d" % q, T.X[:, 1024 * q:1024 * q + 1024], T.x[:, 1024 * q:1024 * q + 1024], ["X%d" % q], 3.5 + 0.5 * q)
-    load("z", T.zin[:], T.z[:], ["zin"], 5.0)
+        what["x%d" % q] = (T.X[:, 1024 * q:1024 * q + 1024], T.x[:, 1024 * q:1024 * q + 1024], "X%d" % q, 0.6)
+    lat = 2.0
+    for name in LOADS:
+        lat += what[name][3]
+        load(name, what[name][0], what[name][1], [what[name][2]], lat)
     XC = ["X0", "X1", "X2", "X3"]
-    XR = XC + ["Xd"]
 
     def iota(name, out, pat, base, cm, f=True):
         n = 1
@@ -99,110 +155,121 @@ def rank_program(g, core, T, topo):
         kw = {"allow_small_or_imprecise_dtypes": True} if f else {}
         op("g", 0.13 + 2 * n * CY, [lambda: g.iota(out, pat, base, cm, **kw)], [], [name])
 
-    def fill(name, ap, val, n, R=()):
-        v(dv(n), lambda: V.memset(ap, val), R, [name])
+    def fill(name, ap, val, n):
+        v(dv(n), lambda: V.memset(ap, val), [], [name])
 
-    iota("pci", T.pci[:], [[0, 1]], 0, 1, False)
-    iota("pc", T.pc[:], [[0, 1]], 0, 1)
-    iota("i128", T.i128[:], [[1, 128]], 0, 0)
-    iota("w144", T.w144[:], [[1, 144]], -15, 0)
-    iota("c16", T.c16[:], [[1, 8], [0, 16]], 0, 0)
-    iota("k256", T.k256[:], [[0, 16], [1, 16]], 0, 0)
-    iota("dum0", T.yw[:], [[int(BIG), 2], [-64, 16]], -2048 - 15 * int(BIG), 0)
-    pg, pk, odd, p32, even, p512, pk4, wcol = [T.col[:, k:k + 1] for k in range(8)]
-    v(one, lambda: ts(T.q1[:, 0:1], T.pci[:], 4, None, A.arith_shift_right), ["pci"], ["q1a"])
-    v(one, lambda: ts(T.q1[:, 1:2], T.pci[:], 15, None, A.bitwise_and), ["pci"], ["q1b"])
-    v(one, lambda: ts(T.q1[:, 2:3], T.pci[:], 4, 1, A.arith_shift_right, A.bitwise_and), ["pci"], ["q1c"])
-    v(one, lambda: ts(T.q1[:, 3:4], T.pci[:], 31, None, A.bitwise_and), ["pci"], ["q1d"])
-    v(one, lambda: V.tensor_copy(T.col[:, 0:4], T.q1[:, 0:4]), ["q1a", "q1b", "q1c", "q1d"], ["col", "q1"])
-    s(sone, lambda: act(even, odd, AF.Identity, bias=1.0, scale=-1.0), ["col"], ["even"])
-    s(sone, lambda: act(p512, p32, AF.Copy, scale=16.0), ["col"], ["p512"])
-    s(sone, lambda: act(pk4, pk, AF.Copy, scale=-4.0), ["col"], ["pk4"])
-    s(sone, lambda: act(T.dum[:], T.yw[:], AF.Identity, bias=pk4), ["dum0", "pk4"], ["dum", "yw"])
-    v(one, lambda: ts(T.RM[:], T.i128[:, 0:16], pk, None, A.is_equal), ["i128", "col"], ["RM"])
-    s(sone, lambda: act(T.RMn[:], T.RM[:], AF.Identity, bias=1.0, scale=-1.0), ["RM"], ["RMn"])
-    s(sone, lambda: act(T.RO[:], T.RM[:], AF.Copy, scale=odd), ["RM", "col"], ["RO"])
-    s(sone, lambda: act(T.RE[:], T.RM[:], AF.Copy, scale=even), ["RM", "even"], ["RE"])
-    v(dv(128), lambda: ts(T.Ib[:], T.i128[:], T.pc[:], None, A.is_equal), ["i128", "pc"], ["Ib"])
-    for name, val in (("I16", 1.0), ("sI0", 0.97), ("Ibn", -1.0), ("IBn", -BIG), ("IBp", BIG), ("Ih", 0.5), ("Ihn", -0.5)):
-        s(sa(128), lambda name=name, val=val: act(T[name][:], T.Ib[:], AF.Copy, scale=val), ["Ib"], [name])
-    s(sa(128), lambda: act(T.Ioff[:], T.Ib[:], AF.Identity, bias=-10000.0, scale=10000.0 + 0.97 - 307.2), ["Ib"], ["Ioff"])
-    v(one, lambda: ts(T.blkf[:], T.i128[:, 0:8], pg, None, A.is_equal), ["i128", "col"], ["blkf"])
+    def scaled(name, out, src, R, val, n, bias=0.0):
+        s(sa(n), lambda: act(out, src, AF.Identity, bias=bias, scale=val), R, [name])
+
+    def between(name, out, src, R, pat, lo, hi):
+        n = 1
+        for _, b in pat:
+            n *= b
+        pick("tmp", T.tmp[:, 0:n], src, R, pat, A.is_ge, -lo, 1)
+        pick(name, out, T.tmp[:, 0:n], ["tmp"], [[-a, b] for a, b in pat], A.is_ge, hi, -1)
+
+    fill("ones", T.ones[:], 1.0, 128)
+    fill("neg", T.neg[0:40, :], -BIG, 72)
+    fill("c160", T.c160[:], BIAS, 128)
+    fill("WB", T.WB[0:40, :], 0.0, 72)
+    for p0 in (0, 32):
+        pick("WB", T.WB[p0:p0 + 8, :], T.neg[p0:p0 + 8, :], ["neg"], [[1, 144]], A.is_equal, -15, -16)
+    for name in ("I16", "Ib"):
+        pick(name, T[name][:], T.ones[:, 0:128], ["ones"], [[-1, 128]], A.is_equal, 0, 1)
+    big = 2 * BIG if on_v("sg") else BIG
+    for name, val in (("Ibn", -1.0), ("IBn", -big), ("IBp", big), ("Ih", 0.5), ("Ihn", -0.5)) + ((("sI0", 0.97),) if VBANKS else ()):
+        scaled(name, T[name][:], T.I16[:], ["I16"], val, 128)
+    if VBANKS:
+        scaled("Ioff", T.Ioff[:], T.I16[:], ["I16"], 10000.0 + 0.97 - 307.2, 128, -10000.0)
+    else:
+        fill("lim0", T.lim0[:], -6144.0, 1)
+    scaled("IB8", T.IB8[0:8, :], T.I16[0:8, 0:8], ["I16"], -BIG, 8)
+    between("blk1", T.blk1[:], T.ones[:, 0:8], ["ones"], [[-16, 8]], 0, 15)
     for name, val in (("blkb", 1.0), ("blkS", 4096.0), ("WO", 4.0)):
-        s(sone, lambda name=name, val=val: act(T[name][:], T.blkf[:], AF.Copy, scale=val), ["blkf"], [name])
-    for t in range(NT):
-        k0 = (t + 12) % 16
-        s(sone, lambda t=t, k0=k0: act(T.selk[:, 8 * t:8 * t + 8], T.blkf[:], AF.Copy, scale=T.RM[:, k0:k0 + 1]), ["blkf", "RM"], ["selk%d" % t])
-        s(sa(128), lambda t=t: act(T.It[:, 128 * t:128 * t + 128], T.Ib[:], AF.Copy, scale=T.RMn[:, t:t + 1]), ["Ib", "RMn"], ["It%d" % t])
-    v(dv(256), lambda: ts(T.cf[:, 0:256], T.k256[:], 0.0, 0.5, A.not_equal, A.mult), ["k256"], ["cf"])
-    v(dv(256), lambda: ts(T.go[:], T.k256[:], 0.0, -2.5, A.is_equal, A.mult), ["k256"], ["go"])
-    v(dv(256), lambda: V.tensor_tensor_scan(T.thr[:], T.cf[:, 0:256], T.go[:], 0.0, A.mult, A.add), ["cf", "go"], ["thr"])
-    s(sa(256), lambda: act(T.resetv[:], T.go[:], AF.Copy, scale=8.0e6), ["go"], ["resetv"])
-    v(one, lambda: V.tensor_tensor(T.yc[:], T.thr[:, 0:16], T.RM[:], A.mult), ["thr", "RM"], ["yc"])
-    v(one, lambda: V.tensor_reduce(wcol, T.yc[:], AxisListType.X, A.add), ["yc"], ["wcol"])
-    v(one, lambda: ts(T.WD[:], T.blkf[:], wcol, -0.4, A.mult, A.mult), ["blkf", "wcol"], ["WD"])
-    fill("W72", T.W72[:], 0.0, 72)
-    fill("W72", T.W72[0:9, :], -BIG, 72)
-    for p0, val in ((0, 1.0), (32, -BIG), (64, -BIG)):
-        v(dv(144), lambda p0=p0, val=val: ts(T.W72[p0:p0 + 8, :], T.w144[p0:p0 + 8, :], T.col[p0:p0 + 8, 5:6], val, A.is_equal, A.mult),
-          ["w144", "p512"], ["W72"])
-    fill("RA", T.RA[:], 0.0, 64)
+        scaled(name, T[name][:], T.blk1[:], ["blk1"], val, 8)
+    between("BLKa", T.BLK[:, 0:128], T.ones[:, 0:128], ["ones"], [[-16, 8], [0, 16]], 0, 15)
+    between("BLK", T.BLK[:, 128:256], T.ones[:, 0:128], ["ones", "BLKa"], [[-16, 8], [0, 16]], 16, 31)
+    fill("WN", T.WN[:], 0.0, 8)
+    s(sa(4), lambda: act(T.WN[:, 1:8:2], T.blk1[:, 0:8:2], AF.Copy, scale=4.0), ["blk1"], ["WN"])
+    pick("comb", T.comb[:], T.ones[:, 0:144], ["ones"], [[0, 9], [1, 16]], A.is_equal, -15, 0)
+    pick("tmp", T.tmp[32:40, :], T.ones[32:40, 0:128], ["ones"], [[-1, 8], [0, 16]], A.is_equal, 0, 1)
+    scaled("E8", T.E8[32:40, :], T.tmp[32:40, :], ["tmp"], -512.0, 128)
+    fill("RA", T.RA[0:32, :], 0.0, 64)
     fill("RA", T.RA[0:9, :], BIAS + 63.25, 64)
     fill("RA", T.RA[0:8, :], 0.0, 64)
-    for name, p0, val in (("E8", 0, 1.0), ("E8", 64, -512.0), ("RA", 64, 512.0)):
-        v(dv(128), lambda name=name, p0=p0, val=val: ts(T[name][p0:p0 + 8, :], T.c16[p0:p0 + 8, :], T.col[p0:p0 + 8, 3:4], val, A.is_equal, A.mult),
-          ["c16", "col"], [name])
-    fill("c160", T.c160[:], BIAS, 128)
-    fill("zero", T.zero[:], 0.0, 64)
-    fill("c32", T.c32[:], -0.025, 128)
-    fill("Xd", T.X[:, 4096:XW], BIAS, 512)
-    fill("CANd", T.CAN[:, 1024:CW], 0.0, 256)
+    scaled("RAb", T.RA[32:40, :], T.E8[32:40, :], ["E8"], -1.0, 128)
+    iota("dum", T.dum[:], [[-int(BIG), 3], [-64, 16]], 2 * int(BIG) - 2048, -4)
+    iota("pci", T.pci[:], [[0, 1]], 0, 1, False)
+    iota("k256", T.k256[:], [[0, 16], [1, 16]], 0, 0)
+    pk, wcol = T.col[:, 0:1], T.col[:, 1:2]
+    v(one, lambda: ts(T.q2[:, 0:1], T.pci[:], 15, None, A.bitwise_and), ["pci"], ["q2"])
+    v(one, lambda: V.tensor_copy(pk, T.q2[:, 0:1]), ["q2"], ["pk"])
+    v(dh(256), lambda: ts(T.dmask[:], T.k256[:], pk, None, A.is_equal), ["k256", "pk"], ["dmask"])
+    v(one, lambda: V.tensor_copy(T.zl[:], T.k256[:, 0:32]), ["k256"], ["zl"])
+    v(dh(256), lambda: ts(T.r1[:], T.k256[:], 0.0, 0.5, A.not_equal, A.mult), ["k256"], ["r1"])
+    v(dh(256), lambda: ts(T.xc[:], T.k256[:], 0.0, -2.5, A.is_equal, A.mult), ["k256"], ["xc"])
+    v(dh(256), lambda: V.tensor_tensor_scan(T.thr[:], T.r1[:], T.xc[:], 0.0, A.mult, A.add), ["r1", "xc"], ["thr"])
+    v(dh(256), lambda: ts(T.resetv[:], T.xc[:], 8.0e6, None, A.mult), ["xc"], ["resetv"])
+    v(one, lambda: V.tensor_tensor(T.yc[:], T.thr[:, 0:16], T.dmask[:, 0:16], A.mult), ["thr", "dmask"], ["yc"])
+    v(one, lambda: V.tensor_reduce(wcol, T.yc[:], AxisListType.X, A.add), ["yc"], ["wcol"])
+    v(one, lambda: ts(T.WD[:], T.blk1[:], wcol, -0.4, A.mult, A.mult), ["blk1", "wcol"], ["WD"])
+    fill("k2047", T.krow[0:1, :], 2047.0, 64)
+    fill("kB", T.krow[32:33, :], -BIG, 64)
+    fill("c32", T.c32[32:40, :], -0.025 if VBANKS else 0.5, 128)
     fill("Knp", T.Kn[:, 0:16], 0.0, 16)
-    for name in ("TC", "TW0", "TW1"):
-        op("v", dh(256), [lambda name=name: ts(T[name][:], T.c160[:], 0.0, 1.0, A.mult, A.add)], ["c160"], [name + "a", name + "b", name + "c"])
+    fill("At", T.At[:], 0.0, 128)
+    for name in ("TW0", "TW1"):
+        op("v", dh(256), [lambda name=name: V.memset(T[name][0:40, 0:256], 1.0)], [], [name + "b", name + "c"])
+        op("v", dh(256), [lambda name=name: V.memset(T[name][0:40, 256:512], 0.0)], [], [name + "d"])
 
-    v(dv(256), lambda: ts(T.TC[0:8, :], T.vin[0:8, :], -1.0, 2048.0, A.mult, A.add), ["vin"], ["TCa"])
-    v(dv(256), lambda: ts(T.Gn0[:], T.tin[:], -1.0, 2048.0, A.mult, A.add), ["tin"], ["Gn0"])
-    v(dv(256), lambda: V.tensor_copy(T.Gu0[:], T.tin[:]), ["tin"], ["Gu0"])
-    v(dh(256), lambda: ts(T.Z[:, 0:256], T.zin[:], BIAS, None, A.add), ["zin"], ["Z0"])
-    v(dv(1024), lambda: ts(T.CAN[:, 0:1024], T.cin[:], -1.0, 2048.0, A.mult, A.add), ["cin"], ["CAN"])
+    lin("", T.TC[0:8, :], T.vin[0:8, :], -1.0, 2048.0, 256, ["vin"], ["TCb"], e="v")
+    lin("", T.Gn0[:], T.tin[:], -1.0, 2048.0, 256, ["tin"], ["Gn0"], e="v")
+    lin("", T.Gu0[:], T.tin[:], 1.0, 0.0, 256, ["tin"], ["Gu0"], e="v")
+    lin("", T.Z[:, 0:256], T.zin[:], 1.0, BIAS, 256, ["zin"], ["Z0"], how="half", e="v")
+    lin("", T.CAN[:, 0:1024], T.cin[:], -1.0, 2048.0, 1024, ["cin"], ["CAN"], e="v")
     for q in range(4):
-        v(dh(1024), lambda q=q: ts(T.X[:, 1024 * q:1024 * q + 1024], T.X[:, 1024 * q:1024 * q + 1024], BIAS, None, A.add),
-          ["X%d" % q], ["X%d" % q])
+        lin("", T.X[:, 1024 * q:1024 * q + 1024], T.X[:, 1024 * q:1024 * q + 1024], 1.0, BIAS, 1024, ["X%d" % q], ["X%d" % q], how="half", e="vsvv"[q])
 
-    def wrap(buf, rows, c0):
-        return lambda B: [(B[:, c0:c0 + 16], T.W72[0:rows, 15 - b:143 - b], T[buf][0:rows, b:256:16], b == 0, b == 15, 64) for b in range(16)]
-
-    def later(tag, t, rep, colbuf, eq, buf):
-        tn = "P%s%d" % (tag, t)
-        t_(tn, lambda B: [(B[32:40, 0:256], T.Ib[0:8, 0:8], T.thr[0:8, :], True, False, 256)], ["Ib", "thr", rep], [tn])
-        for blocks in (range(0, 3), range(3, 7), range(7, 11), range(11, 16)):
-            nm = "%s_%d" % (eq, blocks[0])
-            op("v", sum(dh(EQN[a]) for a in blocks),
-               [lambda a=a: ts(T[eq][:, EQO[a]:EQO[a + 1]], T[rep][:, 16 * a:256], T[colbuf][:, a:a + 1], None, A.is_equal) for a in blocks],
-               [rep, colbuf], [nm])
+    def firsts(t):
+        k0 = (t + 12) % 16
+        wW, cwl, TW, SEL, Wk, Gn = ["%s%d" % (n, t % 2) for n in ("wW", "cwl", "TW", "SEL", "Wk", "Gn")]
+        pick(SEL, T[SEL][:], T.ones[:, 0:128], ["ones"], [[-16, 8], [0, 16]], A.is_equal, -k0, 1)
+        pick(Wk, T[Wk][:], T.comb[:], ["comb"], [[1, 144]], A.is_equal, k0 - 15, -1)
+        t_("rw%d" % t, lambda B: [(B[:, 0:256], T[SEL][:], T[Gn][:], True, True, 256)]
+           + [(B[:, 256:272], T[Wk][:, 15 - b:143 - b], T[Gn][:, b:256:16], b == 0, b == 15, 64) for b in range(16)], [Gn, SEL, Wk])
+        lin("repw", T.repw[:], lambda B: B[:, 0:272], 0.25, 1536.375, 272, [], ["repw"], "rw%d" % t)
+        lin("wW", T[wW][:], lambda B: B[:, 256:272], 1.0, 0.0, 16, [], [wW], "rw%d" % t)
+        lin("uW", T.uW[:], T.repw[:, 256:272], 1.0, 0.0, 16, ["repw"], ["uW"])
+        lin("cwl", T[cwl][:], T.repw[:, 256:272], -1.0, 2048.0, 16, ["repw"], [cwl])
+        tn = "Pw%d" % t
+        t_(tn, lambda B: [(B[0:8, 0:256], T.Ib[0:8, 0:8], T.thr[0:8, :], True, False, 256)], ["Ib", "thr", "repw"], [tn])
+        for blocks in (range(0, 3), range(3, 7), range(7, min(11, 16 - SHORT)), range(min(11, 16 - SHORT), 16)):
+            for a in blocks:
+                if a < 16 - SHORT:
+                    v(dh(EQN[a]), lambda a=a: ts(T.eqw[:, EQO[a]:EQO[a + 1]], T.repw[:, 16 * a:256], T.uW[:, a:a + 1], None, A.is_equal),
+                      ["repw", "uW"], ["eqw_%d" % a])
+                else:
+                    s(sa(EQN[a]), lambda a=a: act(T.dw[:, EQO[a] - EQO[8]:EQO[a + 1] - EQO[8]], T.repw[:, 16 * a:256], AF.Abs, bias=T.uW[:, a:a + 1], scale=-1.0),
+                      ["repw", "uW"], ["dw_%d" % a])
+            if SHORT and blocks[-1] == 15:
+                a0 = EQO[16 - SHORT]
+                v(dh(EQO[16] - a0), lambda: ts(T.eqw[:, a0:EQO[16]], T.dw[:, a0 - EQO[8]:EQO[16] - EQO[8]], 0.0, None, A.is_equal),
+                  ["dw_%d" % a for a in range(16 - SHORT, 16)], ["eqs"] + ["eqw_%d" % a for a in range(16 - SHORT, 16)])
 
             def sums(B, blocks=blocks):
                 r = []
                 for a in blocks:
-                    r.append((B[32:40, 16 * a:16 * a + 16], T.WD[:], T[eq][:, EQO[a]:EQO[a] + 16], False, a == 15, 16))
+                    r.append((B[0:8, 16 * a:16 * a + 16], T.WD[:], T.eqw[:, EQO[a]:EQO[a] + 16], False, a == 15, 16))
                     if a < 15:
-                        r.append((B[32:40, 16 * a + 16:256], T.WO[:], T[eq][:, EQO[a] + 16:EQO[a + 1]], False, False, EQN[a] - 16))
+                        r.append((B[0:8, 16 * a + 16:256], T.WO[:], T.eqw[:, EQO[a] + 16:EQO[a + 1]], False, False, EQN[a] - 16))
                 return r
-            t_(tn, sums, [nm, "WD", "WO", tn], [tn])
-        sp(sa(256), lambda B: act(T[buf][32:40, :], B[32:40, 0:256], AF.Sign), tn, [], [buf + "b"])
+            t_(tn, sums, ["eqw_%d" % a for a in blocks] + ["WD", "WO", tn], [tn])
+        sign("TWb", T[TW][0:8, 0:256], lambda B: B[0:8, 0:256], 0.0, tn, [TW + "b"])
+        pick(TW + "d", T[TW][0:8, 256:512], T[TW][0:8, 0:256], [TW + "b"], [[0, 256]], A.is_ge, 0, 0)
 
-    def place(t):
-        tn = "cW%d" % t
-        t_(tn, wrap("TC", 8, 0), ["TCa", "W72"])
-        if t >= 0:
-            vp(one, lambda B: ts(T.cu[:], B[:, 0:16], -1.0, 2048.0, A.mult, A.add), tn, [], ["cu"])
-        if t < NT - 1:
-            vp(one, lambda B: ts(T.vl[:], B[:, 0:16], -0.25, 511.625, A.mult, A.add), tn, [], ["vl"])
-        if t >= 0:
-            sp(sone, lambda B: act(T.cW[:], B[:, 0:16], AF.Copy), tn, [], ["cW"])
-
-    place(-1)
+    t_("cW", lambda B: [(B[:, 0:16], T.WB[0:8, 15 - b:143 - b], T.TC[0:8, b:256:16], b == 0, b == 15, 64) for b in range(16)], ["TCb", "WB"])
+    vp(one, lambda B: ts(T.vl[:], B[:, 0:16], 0.25 / BIG, 511.625, A.mult, A.add), "cW", [], ["vl"])
+    firsts(0)
 
     def step(t):
         p, q = t % 2, 1 - t % 2
@@ -210,144 +277,159 @@ def rank_program(g, core, T, topo):
         k0 = (t + 12) % 16
         Z, Gn, Gu, TW, sI = "Z%d" % t, "Gn%d" % p, "Gu%d" % p, "TW%d" % p, "sI%d" % p
         Gn1, Gu1, sI1 = "Gn%d" % q, "Gu%d" % q, "sI%d" % q
-        z0 = 512 * t
+        wW, cwl, It, lim, lim1 = "wW%d" % p, "cwl%d" % p, "It%d" % p, "lim%d" % p, "lim%d" % q
+        z0 = 1024 * t
         zz = T.Z[:, z0:z0 + 256]
         Kn = T.Kn[:, 16:272]
-        s(sg(256), lambda: act(Kn, T.CAN[:, 0:1024].indirect(T.vl[:]), AF.Copy), ["CAN", "vl"], ["Kn"])
+        if t:
+            lin("Kn", Kn, T.CAN[:, 0:1024].indirect(T.vl[:]), 1.0, 0.0, 256, ["CAN", "vl"], ["Kn"], how="gather")
+        else:
+            lin("Kn", Kn, T.cin[:].indirect(T.vl[:]), -1.0, 2048.0, 256, ["cin", "vl"], ["Kn"], how="gather")
         tn = "Kt%d" % t
-        t_(tn, lambda B: [(B[32 * u:32 * u + 32, a:256:16], T.Kn[32 * u:32 * u + 32, 16 * a:16 * a + 32], T.RO[32 * u:32 * u + 32, :], True, True, 32)
-                          for a in range(16) for u in range(4)], ["Kn", "Knp", "RO"], [tn])
-        t_(tn, lambda B: [(B[32 * u:32 * u + 16, a:256:16], T.Kn[32 * u:32 * u + 32, 16 * a + 16:16 * a + 32], T.RE[32 * u:32 * u + 32, :], True, True, 16)
-                          for a in range(16) for u in range(4)], ["Kn", "RE", tn], [tn])
-        vp(dv(256), lambda B: ts(T.Ku[:], B[:, 0:256], -1.0, 2048.0, A.mult, A.add), tn, [], ["Ku"])
+        t_(tn, lambda B: [(B[u:u + 32, a:256:16], T.Kn[u:u + 32, 16 * a:16 * a + 32], T.I16[u:u + 32, u + 16:u + 32], True, True, 32)
+                          for a in range(16) for u in (0, 32, 64, 96)], ["Kn", "Knp", "I16"], [tn])
+        t_(tn, lambda B: [(B[u:u + 16, a:256:16], T.Kn[u:u + 32, 16 * a + 16:16 * a + 32], T.I16[u:u + 32, u:u + 16], True, True, 16)
+                          for a in range(16) for u in (0, 32, 64, 96)], ["Kn", "I16", tn], [tn])
+        lin("Ku", T.Ku[:], lambda B: B[:, 0:256], -1.0, 2048.0, 256, [], ["Ku"], tn)
         for c in range(4):
             s(sg(1024), lambda c=c: act(T.xg[:, 1024 * c:1024 * c + 1024], T.X[:, 0:4096].indirect(T[Gu][:, 64 * c:64 * c + 64]), AF.Copy, scale=-1.0),
               XC + [Gu], ["xg_%d" % c])
-        t_("TW%d" % t, lambda B: [(B[0:8, 0:256], T.selk[:, 8 * t:8 * t + 8], T[Gn][:], True, True, 256)], [Gn, "selk%d" % t])
-        sp(sa(256), lambda B: act(T[TW][0:8, :], B[0:8, 0:256], AF.Copy), "TW%d" % t, [], [TW + "a"])
-        t_("rw%d" % t, lambda B: [(B[:, 0:256], T.E8[0:8, :], T[TW][0:8, :], True, True, 256)] + wrap(TW, 8, 256)(B), [TW + "a", "E8", "W72"])
-        sp(sa(272), lambda B: act(T.repw[:], B[:, 0:272], AF.Identity, bias=1536.375, scale=0.25), "rw%d" % t, [], ["repw"])
-        s(sone, lambda: act(T.uW[:], T.repw[:, 256:272], AF.Copy), ["repw"], ["uW"])
-        v(one, lambda: ts(T.cwl[:], T.repw[:, 256:272], -1.0, 2048.0, A.mult, A.add), ["repw"], ["cwl"])
-        s(sg(256), lambda: act(T.cw[:], T.CAN[:, 0:1024].indirect(T.cwl[:]), AF.Copy), ["CAN", "cwl"], ["cw"])
-        later("w", t, "repw", "uW", "eqw", TW)
-        t_("yw%d" % t, wrap(TW, 40, 0), [TW + "a", TW + "b", "W72"])
-        if TWICE:
-            s(sa(256), lambda: act(T.Z[:, z0 + 256:z0 + 512], zz, AF.Copy), [Z], ["Zb"])
+        pick(It, T[It][:], T.I16[:], ["I16"], [[0, 8], [1, 16]], A.not_equal, -t, 0)
+        lin("cw", T.cw[:], T.CAN[:, 0:1024].indirect(T[cwl][:]), 1.0, 0.0, 256, ["CAN", cwl], ["cw"], how="gather")
+        for nm, n, src in (("Zb", 256, Z), ("Zc", 512, "Zb")):
+            pick(nm, T.Z[:, z0 + n:z0 + 2 * n], T.Z[:, z0:z0 + n], [Z, src], [[0, n]], A.is_ge, 0, 0)
         tn = "key%d" % t
-        t_(tn, lambda B: [(B[:, 0:256], T.zero[:], T.c160[:], True, False, 256)]
+        t_(tn, lambda B: [(B[:, 0:256], T.krow[0:1, :], T.ones[0:1, :], True, False, 256)]
            + [(B[:, 128 * h:128 * h + 128], T.Kn[:, 16 + 128 * h:144 + 128 * h], T.I16[:], False, False, 128) for h in range(2)],
-           ["zero", "c160", "Kn", "I16", "Ku"], [tn])
+           ["k2047", "ones", "Kn", "I16", "Ku"], [tn])
         for c in range(4):
-            w = 2 if TWICE else 1
+            w = (1, 2, 4, 4)[c]
             op("v", 4 // w * dg(256 * w),
                [lambda k=k, w=w: V.tensor_tensor(T.sc[:, 256 * k:256 * (k + w)], T.X[:, 0:4096].indirect(T.Ku[:, 16 * k:16 * (k + w)]),
                                                  T.Z[:, z0:z0 + 256 * w], A.max) for k in range(4 * c, 4 * c + 4, w)],
-               XC + ["Ku", Z] + (["Zb"] if TWICE else []), ["sc%d" % c])
+               XC + ["Ku", Z] + ["Zb", "Zc"][:c], ["sc%d" % c])
             t_(tn, lambda B, c=c: [(B[:, 128 * h + k:128 * h + 128:16], T.sc[:, 256 * k + 128 * h:256 * k + 128 * h + 128], T.blkS[:], False,
                                     k == 15 and h == 1, 64) for k in range(4 * c, 4 * c + 4) for h in range(2)], ["sc%d" % c, "blkS", tn], [tn])
         vp(dv(256), lambda B: V.tensor_tensor_scan(T.sco[:], T.resetv[:], B[:, 0:256], 0.0, A.add, A.max), tn, ["resetv"], ["sco"])
-        v(one, lambda: ts(T.q1[:], T.sco[:, 15:256:16], 2047.0, None, A.add), ["sco"], ["q1"])
-        v(one, lambda: ts(T.q2[:], T.q1[:], 4095, None, A.bitwise_and), ["q1"], ["q2"])
-        v(one, lambda: ts(T.Lc[:], T.q2[:], -2047.0, None, A.add), ["q2"], ["Lc"])
-        t_("T1%d" % t, lambda B: [(B[0:8, 128 * h:128 * h + 128], T.Lc[:, 8 * h:8 * h + 8], T.I16[:], True, True, 128) for h in range(2)], ["Lc", "I16"])
-        sp(sa(256), lambda B: act(T.TC[0:8, :], B[0:8, 0:256], AF.Copy), "T1%d" % t, [], ["TCa"])
-        place(t)
-        s(sg(256), lambda: act(T.xc[:], T.X[:, 0:4096].indirect(T.cu[:]), AF.Identity, bias=-BIAS / 2 - 0.25, scale=0.5), XC + ["cu"], ["xc"])
+        v(one, lambda: ts(T.q2[:], T.sco[:, 15:256:16], 4095, None, A.bitwise_and), ["sco"], ["q2"])
+        lin("Lc", T.Lc[:], T.q2[:], 1.0, -2047.0, 16, ["q2"], ["Lc"])
+        v(dg(256), lambda: V.tensor_tensor(T.A1[:], T.Lc[:].indirect(T.zl[:, 0:16]), T.dmask[:], A.mult), ["Lc", "zl", "dmask"], ["A1"])
+
+        def wrapped(B, stop):
+            return [(B[:, 8 * h:8 * h + 8], T.A1[:, 128 * h:128 * h + 128], T.blk1[:], h == 0, stop and h == 1, 64) for h in range(2)]
+        t_("cW%d" % t, lambda B: wrapped(B, True), ["A1", "blk1"])
+        lin("cu", T.cu[:], lambda B: B[:, 0:16], -1.0, 2048.0, 16, [], ["cu"], "cW%d" % t)
+        if not last:
+            lin("vl", T.vl[:], lambda B: B[:, 0:16], -0.25, 511.625, 16, [], ["vl"], "cW%d" % t)
+        if t:
+            op("g", ga(16), [lambda: g.affine_select(T.At[:, t - 1:256:16], T.ones[:, 0:16], [[0, 16]], A.is_gt, 0.0, 0, 0)], ["ones"], ["Az", "At"])
+        lin("At", T.At[:, t:256:16], T.Lc[:], 1.0, 0.0, 16, ["Lc", "At"], ["At"])
+        lin("xc", T.xc[:], T.X[:, 0:4096].indirect(T.cu[:]), 0.5, -BIAS / 2 - 0.25, 256, XC + ["cu"], ["xc"], how="gather")
         if not last:
             snt, arr = "snt%d" % (t + 1), "arr%d" % (t + 1)
-            t_("ZS%d" % t, lambda B: [(B[:, 0:256], T.Ih[:], zz, True, False, 256), (B[:, 0:256], T.Ib[:], T.xc[:], False, True, 256)], ["Ih", "Ib", Z, "xc"])
-            sp(sa(256), lambda B: act(T.ZS[:, 256 * t:256 * t + 256], B[:, 0:256], AF.Identity, bias=BIAS / 2), "ZS%d" % t, [], ["zs%d" % t])
+            parts("ZS", t, lambda B: [(B[:, 0:256], T.Ih[:], zz, 256)], ["Ih", Z], lambda B: [(B[:, 0:256], T.Ib[:], T.xc[:], 256)], ["Ib", "xc"])
+            lin("zs", T.ZS[:, 256 * t:256 * t + 256], lambda B: B[:, 0:256], 1.0, BIAS / 2, 256, [], ["zs%d" % t], "ZS%d" % t)
             dst = T.cores[(rank + 1 + t % 3) % len(T.cores)]
             rid, pid = topo.addr(dst)[0], topo.addr(dst)[1]
             ne = len(topo.engines(core, dst))
-            op("g", 1.0, [lambda: g.remote_dma(T.Z[:, z0 + 512:z0 + 768], T.ZS[:, 256 * t:256 * t + 256], T.sem[arr], T.sem[snt], pid=pid, routing_id=rid,
+            op("g", 1.0, [lambda: g.remote_dma(T.Z[:, z0 + 1024:z0 + 1280], T.ZS[:, 256 * t:256 * t + 256], T.sem[arr], T.sem[snt], pid=pid, routing_id=rid,
                                                dma_engine_mask=topo.mask(core, dst))], ["zs%d" % t], ["way%d" % t], sem=snt, cnt=ne)
-            op("x", 0.0, [], ["way%d" % t], ["Z%d" % (t + 1)], lat=2.5, sem=arr, cnt=ne)
-        t_("rc%d" % t, lambda B: [(B[:, 0:256], T.E8[0:8, :], T.TC[0:8, :], True, True, 256)], ["TCa", "E8"])
-        sp(sa(256), lambda B: act(T.repc[:], B[:, 0:256], AF.Copy), "rc%d" % t, [], ["repc"])
-        later("c", t, "repc", "cW", "eqc", "TC")
-        t_("yc%d" % t, wrap("TC", 40, 0), ["TCa", "TCb", "W72"])
-        vp(one, lambda B: V.tensor_tensor(T.yc[:], B[:, 0:16], T.dum[:, 0:16], A.max), "yc%d" % t, ["dum"], ["yc"])
-        v(one, lambda: ts(T.dcu[:], T.yc[:], -1.0, 2048.0 - 15 * BIG, A.mult, A.add), ["yc"], ["dcu"])
-        banks = [(h, kb) for h in range(2) for kb in sorted(range(4), key=lambda kb: kb != k0 % 4)]
+            op("x", 0.0, [], ["way%d" % t], ["Z%d" % (t + 1)], lat=WAY, sem=arr, cnt=ne)
+        t_("rc%d" % t, lambda B: [(B[:, 0:256], T.BLK[:, 0:128], T.A1[:], True, True, 256), (B[:, 256:512], T.BLK[:, 128:256], T.A1[:], True, True, 256)],
+           ["A1", "BLK"])
+        lin("repc", T.repc[:], lambda B: B[:], 1.0, 0.0, 512, [], ["repc"], "rc%d" % t)
+        v(dg(512), lambda: V.tensor_tensor(T.eqc[:], T.Lc[:].indirect(T.zl[:]), T.repc[:], A.is_equal), ["Lc", "zl", "repc"], ["eqc"])
+        parts("Pc", t, lambda B: [(B[0:8, 0:256], T.Ib[0:8, 0:8], T.thr[0:8, :], 256)], ["Ib", "thr", "Lc"],
+              lambda B: [(B[0:8, 0:256], T.WD[:], T.eqc[:, 0:256], 256), (B[0:8, 0:256], T.WN[:], T.eqc[:, 256:512], 256)], ["WD", "WN", "eqc"])
+        sign("TCb", T.TC[0:8, :], lambda B: B[0:8, 0:256], 0.0, "Pc%d" % t, ["TCb"])
+        t_("yc%d" % t, lambda B: wrapped(B, False) + [(B[:, 8 * h:8 * h + 8], T.TC[0:8, 128 * h:128 * h + 128], T.IB8[0:8, :], False, h == 1, 64)
+                                                      for h in range(2)], ["A1", "blk1", "TCb", "IB8"])
+        upc = 0 if on_v("TCb") else 1
+        vp(one, lambda B: V.tensor_tensor(T.yc[:], B[:, 0:16], T.dum[:, 32 - 16 * upc:48 - 16 * upc], A.max), "yc%d" % t, ["dum"], ["yc"])
+        lin("dcu", T.dcu[:], T.yc[:], -1.0, 2048.0 + upc * BIG, 16, ["yc"], ["dcu"])
+        banks = [(h, kb) for h in range(2) for kb in sorted(range(4), key=lambda kb: (kb - k0) % 4)]
+        M = sI if VBANKS else "Ib"
         for b, (h, kb) in enumerate(banks):
             tn = "d%d_%d" % (t, b)
-            t_(tn, lambda B, h=h, kb=kb: [(B[:], T[sI][:], T.xg[:, 2048 * h + kb:2048 * h + 2048:4], True, False, 512)]
-               + [(B[:, j:512:4], T[sI][:], T.Z[:, z0 + 128 * h:z0 + 128 * h + 128], False, j == 3, 128) for j in range(4)],
-               [sI, Z, "xg_%d" % (2 * h), "xg_%d" % (2 * h + 1)])
+            t_(tn, lambda B, h=h, kb=kb: [(B[:], T[M][:], T.xg[:, 2048 * h + kb:2048 * h + 2048:4], True, False, 512)]
+               + [(B[:, j:512:4], T[M][:], T.Z[:, z0 + 128 * h:z0 + 128 * h + 128], False, j == 3, 128) for j in range(4)],
+               [M, Z, "xg_%d" % (2 * h), "xg_%d" % (2 * h + 1)])
             if b in VBANKS:
-                vp(dv(512), lambda B, b=b: ts(T.th[:, 512 * b:512 * b + 512], B[:], GRID, GRID, A.add, A.not_equal), tn, [], ["th%d" % b])
+                vp(dv(512), lambda B, b=b: ts(T.th[:, 512 * b:512 * b + 512], B[:], GRID, GRID, A.add, A.not_equal), tn, [], ["tv%d" % b, "th%d" % b])
             else:
                 sp(sa(512), lambda B, b=b: act(T.ab[:, 512 * b:512 * b + 512], B[:], AF.Abs), tn, [], ["ab%d" % b])
-        run = []
-        for b in range(9):
-            if run and (b == 8 or b in VBANKS or len(run) == 2):
-                v(dh(512 * len(run)), lambda a=run[0], e=run[-1] + 1: ts(T.th[:, 512 * a:512 * e], T.ab[:, 512 * a:512 * e], 16.0, None, A.is_gt),
-                  ["ab%d" % x for x in run], ["th%d" % x for x in run])
-                run = []
-            if b < 8 and b not in VBANKS:
-                run.append(b)
-        for b0 in range(0, 8, 2):
-            t_("cnt%d" % t, lambda B, b0=b0: [(B[:, 128 * banks[b][0] + banks[b][1] + 4 * j:128 * banks[b][0] + 128:16], T.th[:, 512 * b + j:512 * b + 512:4],
-                                               T.blkb[:], True, True, 64) for b in (b0, b0 + 1) for j in range(4)], ["th%d" % b0, "th%d" % (b0 + 1), "blkb"])
-        sp(sa(256), lambda B: act(T.sg[:], B[:, 0:256], AF.Sign, bias=-8.5), "cnt%d" % t, [], ["sg"])
-        t_("sk%d" % t, lambda B: [(B[64:72, 128 * h:128 * h + 128], T.blkb[:], T.th[:, 2048 * h + k0 // 4:2048 * h + 512:4], True, True, 128) for h in range(2)],
+        for run in RUNS:
+            a, e = 512 * run[0], 512 * run[-1] + 512
+            if run[0] not in VBANKS:
+                v(dh(e - a), lambda a=a, e=e: ts(T.th[:, a:e], T.ab[:, a:e], 0.0 if VBANKS else T[lim][:], 16.0 if VBANKS else 6160.0, A.subtract, A.is_gt),
+                  ["ab%d" % b for b in run] + ([] if VBANKS else [lim]), ["th%d" % b for b in run])
+            t_("cnt%d" % t, lambda B, run=run: [(B[:, 128 * banks[b][0] + banks[b][1] + 4 * j:128 * banks[b][0] + 128:16], T.th[:, 512 * b + j:512 * b + 512:4],
+                                                 T.blkb[:], True, True, 64) for b in run for j in range(4)], ["th%d" % b for b in run] + ["blkb"])
+        sign("sg", T.sg[:], lambda B: B[:, 0:256], 8.5, "cnt%d" % t, ["sg"], half=True)
+        t_("sk%d" % t, lambda B: [(B[32:40, 128 * h:128 * h + 128], T.blkb[:], T.th[:, 2048 * h + k0 // 4:2048 * h + 512:4], True, True, 128) for h in range(2)],
            ["th0", "th4", "blkb"])
-        sp(sa(256) + 0.02, lambda B: act(T[TW][64:72, :], B[64:72, 0:256], AF.Sign, bias=-8.5, accum_out=T.acc[64:72, :]), "sk%d" % t, [], [TW + "c", "acc"])
+        sp(sa(256) + 0.02, lambda B: act(T[TW][32:40, 0:256], B[32:40, 0:256], AF.Sign, bias=-8.5, accum_out=T.acc[32:40, :]), "sk%d" % t, [], [TW + "c", "acc"])
         if not last:
-            t_("S%d" % t, lambda B: [(B[:, 0:1], T.c32[64:72, :], T.acc[64:72, :], True, True, 256)], ["c32", "acc"])
-            sp(sone, lambda B: act(T.p32[:], B[:, 0:1], AF.Copy), "S%d" % t, [], ["p32"])
-            s(sone, lambda: act(T.si[:], T.p32[:], AF.Identity, bias=1535.625, scale=-5.0), ["p32"], ["si"])
-            s(sone, lambda: act(T.s0[:], T.si[:], AF.Identity, bias=T.p32[:], scale=0.2), ["si", "p32"], ["s0"])
-            s(sa(128), lambda: act(T[sI1][:], T.Ioff[:], AF.Relu, bias=T.s0[:]), ["Ioff", "s0"], [sI1])
-        t_("yw%d" % t, wrap(TW, 72, 16), [TW + "a", TW + "b", TW + "c", "W72"])
-        vp(one, lambda B: V.tensor_tensor(T.yw[:], B[:, 0:32], T.dum[:], A.max), "yw%d" % t, ["dum"], ["yw"])
-        v(one, lambda: ts(T.dwu[:], T.yw[:, 0:16], -1.0, 2048.0 - 15 * BIG, A.mult, A.add), ["yw"], ["dwu"])
-        v(one, lambda: ts(T.dwl[:], T.yw[:, 16:32], -0.25, 511.625 - 3.5 * BIG, A.mult, A.add), ["yw"], ["dwl"])
+            t_("S%d" % t, lambda B: [(B[:, 0:1], T.c32[32:40, :], T.acc[32:40, :], True, True, 256)], ["c32", "acc"])
+            if VBANKS:
+                vp(one, lambda B: ts(T.si[:], B[:, 0:1], -5.0, 1535.625, A.mult, A.add), "S%d" % t, [], ["si"])
+                vp(one, lambda B: ts(T.s0[:], T.si[:], 0.2, B[:, 0:1], A.mult, A.add), "S%d" % t, ["si"], ["s0"])
+                lin("sI", T[sI1][:], T.Ioff[:], 1.0, T.s0[:], 128, ["Ioff", "s0"], [sI1], relu=True)
+            else:
+                vp(one, lambda B: ts(T.si[:], B[:, 0:1], 0.25, 1535.625, A.mult, A.add), "S%d" % t, [], ["si"])
+                vp(one, lambda B: ts(T[lim1][:], T.si[:], -4.0, B[:, 0:1], A.mult, A.add), "S%d" % t, ["si"], [lim1])
+        t_("yw%d" % t, lambda B: [(B[:, c0:c0 + 16], T.I16[:], T[wW][:], c0 == 0, False, 64) for c0 in (0, 16)]
+           + [(B[:, 0:32], T.WB[0:40, 15 - b:143 - b], T[TW][0:40, b:512:16], False, b == 15, 64) for b in range(16)],
+           [wW, "I16", TW + "b", TW + "c", TW + "d", "WB"])
+        up = 0 if on_v("TWb") else 1
+        vp(one, lambda B: V.tensor_tensor(T.yw[:], B[:, 0:32], T.dum[:, 16 - 16 * up:48 - 16 * up], A.max), "yw%d" % t, ["dum"], ["yw"])
+        lin("dwu", T.dwu[:], T.yw[:, 16:32], -1.0, 2048.0 + up * BIG, 16, ["yw"], ["dwu"])
+        lin("dwl", T.dwl[:], T.yw[:, 0:16], -0.25, 511.625 + (up + 1) * BIG / 4, 16, ["yw"], ["dwl"])
 
-        def sign(B, o, m, stop):
-            return [(B[:, o + 128 * h:o + 128 * h + 128], T.sg[:, 128 * h:128 * h + 128], T[m][:], False, stop and h == 1, 128) for h in range(2)]
-        It = T.It[:, 128 * t:128 * t + 128]
-        t_("G%d" % t, lambda B: [(B[:, 0:256], It, Kn, True, False, 256)] + sign(B, 0, "IBp", False)
-           + [(B[:, 0:256], T.W72[0:8, 15 - t:143 - t], T.TC[0:8, :], False, True, 256), (B[:, 256:512], It, T[Gn][:], True, False, 256)]
-           + sign(B, 256, "IBn", False) + [(B[:, 256:512], T.W72[0:9, 15 - t:143 - t], T.TC[0:9, :], False, True, 256)],
-           ["It%d" % t, "Kn", Gn, "W72", "TCa", "sg", "IBp", "IBn"])
-        sp(sa(256), lambda B: act(T.ga[:], B[:, 0:256], AF.Identity, bias=-BIG), "G%d" % t, [], ["ga"])
+        def signed(B):
+            return [(B[:, o + 128 * h:o + 128 * h + 128], T.sg[:, 128 * h:128 * h + 128], T[m][:], 128) for o, m in ((0, "IBp"), (256, "IBn")) for h in range(2)]
+        parts("G", t, lambda B: [(B[:, 0:256], T[It][:], Kn, 256), (B[:, 256:512], T[It][:], T[Gn][:], 256), (B[:, 256:512], T.krow[32:33, :], T.ones[32:33, :], 256)],
+              [It, "Kn", Gn, "kB", "ones"],
+              lambda B: [(B[:, o + 128 * h:o + 128 * h + 128], T.At[:, 128 * h:128 * h + 128], T.I16[:], 128) for o in (0, 256) for h in range(2)]
+              + signed(B), ["At", "I16", "sg", "IBp", "IBn"])
+        lin("ga", T.ga[:], lambda B: B[:, 0:256], 1.0, -BIG, 256, [], ["ga"], "G%d" % t)
         vp(dv(256), lambda B: V.tensor_tensor(T[Gn1][:], T.ga[:], B[:, 256:512], A.max), "G%d" % t, ["ga"], [Gn1])
         if not last:
-            v(dh(256), lambda: ts(T[Gu1][:], T[Gn1][:], -1.0, 2048.0, A.mult, A.add), [Gn1], [Gu1])
-        t_("N%d" % t, lambda B: [(B[:, 0:256], T.I16[:], T.cw[:], True, False, 256)] + sign(B, 0, "IBp", True)
-           + [(B[:, 256:512], T.I16[:], T[Gn][:], True, False, 256)] + sign(B, 256, "IBn", True), ["I16", "cw", Gn, "sg", "IBp", "IBn"])
-        sp(sa(512), lambda B: act(T.cf[:], B[:], AF.Identity, bias=-BIG), "N%d" % t, [], ["cf"])
-        v(ds(256), lambda: V.tensor_tensor(T.CAN[:].indirect(T.dwl[:]), T.cf[:, 0:256], T.cf[:, 256:512], A.max), ["cf", "dwl"], ["CAN", "CANd"])
+            lin("Gu", T[Gu1][:], T[Gn1][:], -1.0, 2048.0, 256, [Gn1], [Gu1], how="half")
+        parts("N", t, lambda B: [(B[:, 0:256], T.I16[:], T.cw[:], 256), (B[:, 256:512], T.I16[:], T[Gn][:], 256)], ["I16", "cw", Gn], signed, ["sg", "IBp", "IBn"])
+        lin("cf", T.cf[:], lambda B: B[:], 1.0, -BIG, 512, [], ["cf"], "N%d" % t)
+        v(ds(256), lambda: V.tensor_tensor(T.CAN[:].indirect(T.dwl[:]), T.cf[:, 0:256], T.cf[:, 256:512], A.max), ["cf", "dwl"], ["CAN"])
         xw = T.xg[:, k0:4096:16]
         XG = ["xg_%d" % c for c in range(4)]
-        s(sa(256), lambda: act(T.r1[:], xw, AF.Relu, bias=BIAS + 59.0), XG, ["r1"])
-        t_("R%d" % t, lambda B: [(B[:, 256:512], T.Ihn[:], xw, True, False, 256), (B[:, 256:512], T.Ih[:], zz, False, False, 256),
-                                 (B[:, 256:512], T.E8[64:72, :], T[TW][64:72, :], False, True, 256),
-                                 (B[:, 0:256], T.Ibn[:], T.r1[:], True, False, 256), (B[:, 0:256], T.RA[0:72, :], T[TW][0:72, :], False, True, 256)],
-           XG + ["Ihn", "Ih", "Ibn", Z, "r1", "E8", "RA", TW + "a", TW + "b", TW + "c"])
-        sp(sa(512), lambda B: act(T.rf[:], B[:], AF.Relu, bias=-512.25), "R%d" % t, [], ["rf"])
-        v(ds(256), lambda: V.tensor_tensor(T.X[:].indirect(T.dwu[:]), T.rf[:, 0:256], T.rf[:, 256:512], A.add), ["rf", "dwu"], XR)
-        v(ds(256), lambda: V.tensor_tensor(T.X[:].indirect(T.dcu[:]), T.xc[:], T.c160[:], A.add), ["xc", "dcu", "c160"], XR)
+        lin("r", T.r1[:], xw, 1.0, BIAS + 59.0, 256, XG, ["r1"], how="half", relu=True)
+        parts("R", t, lambda B: [(B[:, 256:512], T.Ihn[:], xw, 256), (B[:, 256:512], T.Ih[:], zz, 256), (B[:, 0:256], T.Ibn[:], T.r1[:], 256)],
+              XG + ["Ihn", "Ih", "Ibn", Z, "r1"],
+              lambda B: [(B[:, 256:512], T.E8[32:40, :], T[TW][32:40, 0:256], 256), (B[:, 0:256], T.RA[0:40, :], T[TW][0:40, 0:256], 256)],
+              ["E8", "RA", "RAb", TW + "b", TW + "c"])
+        lin("rf", T.rf[:], lambda B: B[:], 1.0, -512.25, 512, [], ["rf"], "R%d" % t, relu=True)
+        v(ds(256), lambda: V.tensor_tensor(T.X[:].indirect(T.dwu[:]), T.rf[:, 0:256], T.rf[:, 256:512], A.add), ["rf", "dwu"], XC)
+        for a in range(8):
+            v(ds(32), lambda a=a: V.tensor_tensor(T.X[:].indirect(T.dcu[:, 2 * a:2 * a + 2]), T.xc[:, 32 * a:32 * a + 32], T.c160[:, 0:32], A.add),
+              ["xc", "dcu", "c160"], ["cut"] + XC)
+        if not last:
+            now[0] = t + 1
+            firsts(t + 1)
 
     for t in range(NT):
+        now[0] = t
         step(t)
+    now[0] = None
 
     def store(name, out, src, R):
         op("y", 0.1, [lambda: Y.dma_start(out, src)], R, ["y" + name], lat=3.0, sem="st_" + name, cnt=16)
 
-    s(sa(1024), lambda: act(T.lo[:], T.CAN[:, 0:1024], AF.Identity, bias=2048.0, scale=-1.0), ["CAN"], ["lo"])
+    lin("", T.lo[:], T.CAN[:, 0:1024], -1.0, 2048.0, 1024, ["CAN"], ["lo"], e="s")
     store("ol", T.yl[:], T.lo[:], ["lo"])
-    s(sa(256), lambda: act(T.go[:], T["Gn%d" % (NT % 2)][:], AF.Identity, bias=2048.0, scale=-1.0), ["Gn%d" % (NT % 2)], ["go"])
+    lin("", T.go[:], T["Gn%d" % (NT % 2)][:], -1.0, 2048.0, 256, ["Gn%d" % (NT % 2)], ["go"], e="s")
     store("og", T.yg[:], T.go[:], ["go"])
     for c in range(4):
         a, b = 1024 * c, 1024 * c + 1024
-        if c < 3:
-            v(dh(1024), lambda a=a, b=b: ts(T.sc[:, a:b], T.X[:, a:b], -BIAS, None, A.add), ["X%d" % c], ["sc%d" % c])
-        else:
-            s(sa(1024), lambda a=a, b=b: act(T.sc[:, a:b], T.X[:, a:b], AF.Identity, bias=-BIAS), ["X%d" % c], ["sc%d" % c])
+        lin("", T.sc[:, a:b], T.X[:, a:b], 1.0, -BIAS, 1024, ["X%d" % c], ["sc%d" % c], how="half", e="vvvs"[c])
         store("o%d" % c, T.yx[:, a:b], T.sc[:, a:b], ["sc%d" % c])
     emit(g, T, ops, schedule(ops))
 
@@ -373,72 +455,109 @@ def depend(ops):
             d.update(tl[1])
             tl[2].append(o["i"])
         d.discard(o["i"])
-        o["d"] = d
-
-
-def schedule(ops):
-    depend(ops)
-    n = len(ops)
-    succ = [[] for _ in range(n)]
-    for o in ops:
-        for j in o["d"]:
-            succ[j].append(o["i"])
-    prio = [0.0] * n
-    for i in range(n - 1, -1, -1):
-        prio[i] = ops[i]["c"] + ops[i]["lat"] + SYNC + max([prio[j] for j in succ[i]] or [0.0])
-    for o in ops:
+        o["d"], o["s"] = d, []
+        for j in d:
+            ops[j]["s"].append(o["i"])
         o["n"] = "".join(c for c in (o["W"] or [o["tile"]])[0] if c.isalpha()) + "_" + o["e"]
-        prio[o["i"]] += BONUS.get(o["n"], 0.0)
+
+
+def dues(ops, phase):
+    n = len(ops)
+    due, seen = [None] * n, {}
+    for o in ops:
+        if o["t"] is not None:
+            key = (o["t"], o["n"])
+            o["k"] = seen.get(key, 0)
+            seen[key] = o["k"] + 1
+            if o["t"] == NT - 1 and o["n"] in LAST:
+                kind, k = LAST[o["n"]][o["k"]]
+                due[o["i"]] = PERIOD * o["t"] + phase[kind][k] + 0.001
+                continue
+            ph = phase[o["n"]]
+            due[o["i"]] = PERIOD * o["t"] + ph[min(o["k"], len(ph) - 1)]
+            if o["e"] == "g":
+                due[o["i"]] = max(due[o["i"]], AHEAD + 1.0 if o["t"] else -1.0)
+    first = min(o["i"] for o in ops if o["t"] is not None)
+    for o in ops[first:]:
+        if o["t"] is None:
+            due[o["i"]] = max(due[j] for j in o["d"] if j >= first) + 0.001
+    for o in ops[first - 1::-1]:
+        due[o["i"]] = min(due[j] for j in o["s"]) - o["c"] - SYNC if o["e"] != "y" else o["i"] - 1000.0
+    return due, first
+
+
+def place(ops, due, first):
+    n = len(ops)
     users = {}
     for o in ops:
         if o["tile"]:
             users.setdefault(o["tile"], []).append(o["i"])
     left = {k: len(u) for k, u in users.items()}
-    bank = {}
+    bank, extra = {}, {}
     free = {k: [] for k in range(8)}
     need = [len(o["d"]) for o in ops]
-    rt, fin = [0.0] * n, [0.0] * n
-    ready = [i for i in range(n) if need[i] == 0]
+    rt, fin, t0 = [0.0] * n, [0.0] * n, [0.0] * n
+    ready = sorted((due[i], i) for i in range(n) if need[i] == 0)
     et = {"v": 0.0, "s": 0.0, "t": 0.0, "g": 0.0, "y": 0.0, "x": 0.0}
-    order = []
+    order, early, begun = [], first, False
     while ready:
-        cand = []
-        for i in ready:
-            o = ops[i]
-            st = max(rt[i], et[o["e"]] if o["e"] != "x" else 0.0)
-            bk = None
-            if o["tile"] and o["tile"] not in bank:
-                if not free:
-                    continue
+        p = 0
+        while ops[ready[p][1]]["tile"] and ops[ready[p][1]]["tile"] not in bank and not free:
+            p += 1
+            if p == len(ready):
+                raise ValueError("no bank for any ready op")
+        i = ready[p][1]
+        if not begun:
+            can = [(max(rt[j], et[ops[j]["e"]]), q) for q, (_, j) in enumerate(ready) if q == p or
+                   (j < first or due[j] < AHEAD) and (not ops[j]["tile"] or ops[j]["tile"] in bank or len(free) > 3)]
+            p = min((ops[ready[q][1]]["n"] != "sc_v", q) for x, q in can if x <= min(can)[0] + SOON)[1]
+            i = ready[p][1]
+            begun = ops[i]["n"] == "sc_v"
+        elif early:
+            start = max(rt[i], et[ops[i]["e"]])
+            for q, (_, j) in enumerate(ready):
+                if j < first and j != i and (not ops[j]["tile"] or ops[j]["tile"] in bank) and max(rt[j], et[ops[j]["e"]]) + ops[j]["c"] <= start:
+                    p, i = q, j
+                    break
+        e = ops[i]["e"]
+        del ready[p]
+        o = ops[i]
+        early -= i < first
+        st = rt[i] if e == "x" else max(rt[i], et[e])
+        tl = o["tile"]
+        if tl:
+            if tl not in bank:
                 a, bk = min((max([fin[u] for u in us] or [0.0]), k) for k, us in free.items())
                 st = max(st, a + SYNC)
-            cand.append((st, -prio[i], i, bk))
-        if not cand:
-            raise ValueError("no bank for any ready op")
-        first = min(cand, key=lambda c: (c[0] + LOOK * ops[c[2]]["c"], c[1], c[2]))
-        end, eng = first[0] + LOOK * ops[first[2]]["c"], ops[first[2]]["e"]
-        st, _, i, bk = min((c for c in cand if ops[c[2]]["e"] == eng and c[0] <= end), key=lambda c: (c[1], c[0], c[2]))
-        ready.remove(i)
-        o = ops[i]
-        if bk is not None:
-            bank[o["tile"]] = bk
-            o["d"] = set(o["d"]) | set(free.pop(bk))
-        if o["tile"]:
-            o["b"] = bank[o["tile"]]
-            left[o["tile"]] -= 1
-            if left[o["tile"]] == 0:
-                free[o["b"]] = users[o["tile"]]
-        et[o["e"]] = st + o["c"]
-        fin[i] = st + o["c"] + o["lat"]
-        o["t0"] = st
+                bank[tl] = bk
+                extra[i] = free.pop(bk)
+            left[tl] -= 1
+            if left[tl] == 0:
+                free[bank[tl]] = users[tl]
+        et[e] = st + o["c"]
+        fin[i] = f = st + o["c"] + o["lat"]
+        t0[i] = st
         order.append(i)
-        for j in succ[i]:
+        for j in o["s"]:
             need[j] -= 1
-            rt[j] = max(rt[j], fin[i] + SYNC)
+            if f + SYNC > rt[j]:
+                rt[j] = f + SYNC
             if need[j] == 0:
-                ready.append(j)
+                ready.append((due[j], j))
+                ready.sort()
     if len(order) != n:
         raise ValueError("schedule stuck")
+    return order, t0, fin, bank, extra
+
+
+def schedule(ops):
+    depend(ops)
+    order, t0, fin, bank, extra = place(ops, *dues(ops, PHASE))
+    for o in ops:
+        o["t0"] = t0[o["i"]]
+        o["d"] = set(o["d"]) | set(extra.get(o["i"], ()))
+        if o["tile"]:
+            o["b"] = bank[o["tile"]]
     return order
 
 
@@ -461,6 +580,9 @@ def emit(g, T, ops, order):
                 for a, b in snap.items():
                     if b > kn.get(a, 0):
                         kn[a] = b
+        if e == "g" and count.get("qg", 0) > kn.get("qg", 0):
+            kn["qg"] = count["qg"]
+            g.wait_ge(T.sem["qg"], kn["qg"])
         calls = o["f"](T["ps%d" % o["b"]]) if o["tile"] else o["f"]
         for f in calls:
             r = f()

@@ -4,56 +4,71 @@ A = AluOpType
 AF = ActivationFunctionType
 NT = 8
 BIAS = 160.0
-XW = 5568
+MID = BIAS + 31.5
+XW = 4464
 CW = 1392
 BIG = 8192.0
 GRID = 402653184.0
+ADDED = 2
 EQN = [256 - 16 * a for a in range(16)]
 EQO = [sum(EQN[:a]) for a in range(17)]
 
 F4, BF, HF, I4, U2 = "float32", "bfloat16", "float16", "int32", "uint16"
 SCRATCH = {}
 for _n, _s, _d in (
-        ("X", XW, BF), ("CAN", CW, F4), ("cin", 1024, I4), ("tin", 256, I4), ("vin", 256, I4), ("zin", 256, BF),
-        ("xg", 4096, BF), ("ab", 4096, BF), ("th", 4096, BF), ("sc", 4096, BF), ("lo", 1024, F4), ("go", 256, F4),
-        ("Kn", 272, HF), ("Ku", 256, U2), ("eqw", EQO[16], BF), ("eqc", 512, BF), ("dw", 576, BF), ("repw", 272, HF), ("repc", 512, HF),
-        ("uW", 16, F4), ("A1", 256, HF), ("At", 256, HF), ("TC", 256, HF), ("yw", 32, F4), ("yc", 16, F4), ("sco", 256, I4), ("q2", 16, I4),
-        ("Lc", 16, F4), ("cu", 16, U2), ("vl", 16, U2), ("dwu", 16, U2), ("dwl", 16, U2), ("dcu", 16, U2),
+        ("X", XW, BF), ("XO", XW, BF), ("CAN", CW, F4), ("cin", 1024, I4), ("tin", 256, I4), ("vin", 256, I4), ("zin", 256, BF),
+        ("xg", 4096, BF), ("ab", 4096, BF), ("th", 4096, BF), ("sc", 4096, BF), ("go", 256, F4), ("zq", 1024, BF),
+        ("Kn", 272, HF), ("Ku", 256, U2), ("eqw", EQO[16], BF), ("eqc", 384, BF), ("repw", 256, HF),
+        ("uW", 16, F4), ("A1", 256, HF), ("At", 256, HF), ("TC", 256, HF), ("TW", 512, HF), ("yw", 32, F4), ("yc", 16, F4), ("sco", 256, I4),
+        ("q2", 24, I4), ("Lc", 16, F4), ("Lx", 32, HF), ("cu", 16, U2), ("vl", 16, U2), ("dwl", 32, U2), ("dcu", 16, U2),
         ("xc", 256, BF), ("r1", 256, BF), ("rf", 512, BF), ("cw", 256, HF), ("cf", 512, F4), ("ga", 256, HF), ("sg", 256, BF),
         ("acc", 1, F4), ("si", 1, HF), ("s0", 1, F4),
         ("Z", 1024 * NT, BF), ("ZS", 256 * NT, BF),
-        ("pci", 1, I4), ("col", 2, F4), ("k256", 256, BF), ("I16", 128, HF), ("Ib", 128, BF), ("Ibn", 128, BF), ("Ih", 128, BF),
-        ("Ihn", 128, BF), ("IBp", 128, BF), ("IBn", 128, BF), ("Ioff", 128, F4), ("IB8", 8, HF), ("blk1", 8, HF),
-        ("blkb", 8, BF), ("blkS", 8, BF), ("WD", 8, BF), ("WO", 8, BF), ("WN", 8, BF), ("comb", 144, HF), ("thr", 256, BF), ("BLK", 256, HF),
-        ("dmask", 256, HF), ("WB", 144, HF), ("E8", 128, HF), ("RA", 128, HF), ("dum", 48, F4), ("resetv", 256, BF), ("c160", 256, BF),
-        ("krow", 128, HF), ("ones", 256, HF), ("neg", 144, HF), ("c32", 128, F4), ("zl", 32, U2), ("tmp", 128, HF)):
+        ("pci", 4, I4), ("col", 3, F4), ("k256", 256, BF), ("I16", 128, HF), ("In16", 128, HF), ("Ib", 128, BF), ("Ibn", 128, BF), ("Ih", 128, BF),
+        ("Ihn", 128, BF), ("IBp", 128, BF), ("IBn", 128, BF), ("blk1", 8, HF), ("lx", 2, U2), ("blkb", 40, BF), ("blkS", 8, BF), ("WD", 8, BF),
+        ("WO", 8, BF), ("WN", 24, BF), ("tri", 384, HF), ("cc", 4, F4), ("thr", 256, BF), ("BLK", 384, HF), ("dmask", 256, HF), ("WB", 144, HF),
+        ("E8", 128, HF), ("RA", 128, HF), ("dum", 48, F4), ("resetv", 256, BF), ("c160", 64, BF), ("krow", 128, HF), ("ones", 256, HF),
+        ("neg", 144, HF), ("c32", 128, F4), ("zl", 16, U2), ("tmp", 128, HF)):
     SCRATCH[_n] = ("sbuf", [128, _s], _d)
 for _k in range(2):
-    for _n, _s, _d in (("Gn", 256, HF), ("Gu", 256, U2), ("TW", 512, HF), ("sI", 128, BF), ("lim", 1, F4), ("SEL", 128, HF), ("Wk", 144, HF),
-                       ("wW", 16, HF), ("It", 128, HF), ("cwl", 16, U2)):
+    for _n, _s, _d in (("Gn", 272, HF), ("Gu", 256, U2), ("sI", 128, BF), ("SEL", 128, HF), ("sv", 4, F4), ("wW", 32, HF), ("It", 128, HF),
+                       ("cwl", 16, U2)):
         SCRATCH["%s%d" % (_n, _k)] = ("sbuf", [128, _s], _d)
 for _k in range(8):
     SCRATCH["ps%d" % _k] = ("psum", [128, 512], F4)
 
-SEMAPHORES = (["qv", "qs", "qt", "qg"] + ["ld_" + n for n in ("cut", "z", "trail", "canal", "x0", "x1", "x2", "x3")]
-              + ["st_" + n for n in ("o0", "o1", "o2", "o3", "ol", "og")]
-              + ["arr%d" % k for k in range(1, NT)] + ["snt%d" % k for k in range(1, NT)])
-
-CY, GA, SC, PEC, PEF, SF, SG, SYNC, WAY = 0.00087, 1.5, 3.5, 0.00049, 0.001, 0.075, 0.065, 0.11, 4.2
-ORDER = """
-sc_v0 SEL_g++ key_t0 Zc_g Ge_t xg_s3 d_t0 It_g++ sc_v1 Pw_t3 d_t2 xg_s2 d_t3 key_t1 sc_v2 d_t1 key_t2 ab_s3 d_t4 r_s sc_v3 d_t6 ab_s0 key_t3 ab_s1
-d_t5 ab_s4 th_v0 ZSe_t key_t4 ab_s5 d_t7 sco_v eqw_v11 ab_s6 eqw_v15 q_v Re_t th_v2 Lc_s cnt_t0 ab_s2 At_g Pw_t4 A_v sk_t TWb_s cnt_t2 th_v3 rc_t
-TWc_s TWd_g tv_v cnt_t3 repc_s cW_t R_t cu_v th_v1 cnt_t4 rf_s yw_t eqc_v xc_s cnt_t1 Pce_t cwl_s sg_s ZS_t yw_v cw_v Pc_t dwu_s zs_s G_t X_v
-TCb_s way_g yc_t ga_s Ne_t yc_v dwl_s vl_s Gn_v dcu_s N_t Az_g+ cut_v0 S_t Z_x cf_s rw_t+ cut_v1 si_v Gu_s cut_v2 cut_v3 CAN_v repw_s+ wW_s+
-Pw_t0+ cut_v4 s_v cut_v5 uW_v+ Kn_s+ sI_s cut_v6 Kt_t0+ eqw_v12+ cut_v7 eqw_v3+ xg_s0+ eqw_v6+ eqw_v4+ eqw_v10+ eqw_v0+ Kt_t1+ eqw_v1+ eqw_v13+
-Wk_g+++ eqw_v9+ eqw_v2+ eqw_v5+ Pw_t1+ xg_s1+ eqw_v8+ eqw_v7+ Ku_v+ Zb_g+ eqw_v14+ Pw_t2+
-""".split()
-PERIOD, SOON, AHEAD = 15.5, 0.05, 2.0
-VBANKS = (7,)
-LAST = {}
 LOADS = "cut trail x0 x1 x2 canal x3 z".split()
-SHORT = 0
-RUNS = ((0, 1), (2, 3), (4, 5), (6,), (7,))
+SEMAPHORES = (["qv", "qs", "qt", "qg"] + ["ld_" + n for n in LOADS] + ["st_ox", "st_ol", "st_og", "add0", "add1"]
+              + ["dd%d" % k for k in range(ADDED)] + ["arr%d" % k for k in range(1, NT)] + ["snt%d" % k for k in range(1, NT)])
+
+ORDER = """
+sc_v0 key_t0 Pw_t1 Ge_t0 Pw_t2 xg_s0 sc_v1 zqb_g Pw_t3 zqc_g Pw_t4 key_t1 d_t0 d_t1 key_t2 dd_g0 dd_g1 xg_s1 XO_g ab_s0 ab_s1 d_t2 ab_s2 r_s
+sc_v2 sc_v3 key_t3 d_t3 key_t4 sc_v4 th_v0 key_t5 sco_v ZSe_t sk_t Re_t TW_s q_v Lc_s Lx_s R_t De_t th_v1 ab_s3 A_v cW_t TWd_g At_g It_g++
+td_v0 th_v2 cu_s cw_s cna_t0 D_t eqc_v xc_s rf_s yw_t cnb_t0 cnb_t1 cnb_t2 ZS_t yw_v dwl_s td_v1 yc_t yc_v cna_t1 cna_t2 cnb_t3 cna_t3 zs_s
+X_v Gt_t0 way_g sg_s0 Ne_t0 S_t sg_s1 si_s Gt_t1 Ne_t1 Az_g+ dcu_s G_t0 ga_s0 G_t1 s_v cut_v0 Gn_v0 Gw_t0+ ga_s1 cut_v1 Gn_v1 rw_t+ SEL_g+++
+Gw_t1+ cut_v2 sI_s cf_s0 vl_s sv_v cut_v3 CAN_v0 cf_s1 repw_s+ Pw_t0+ cut_v4 CAN_v1 wU_s+ cut_v5 uW_s+ Kn_s+ Kt_t0+ cwl_v+ Kt_t1+ cut_v6
+eqw_v7+ eqw_v12+ cut_v7 eqw_v3+ eqw_v14+ eqw_v10+ eqw_v8+ eqw_v13+ eqw_v0+ eqw_v4+ eqw_v5+ eqw_v9+ eqw_v6+ eqw_v11+ eqw_v15+ Gu_s+ eqw_v1+
+wW_s+ Ku_v+ eqw_v2+ xg_s3+ Z_x Dt_t+ Ge_t1+ zq_s+ xg_s2+ Zb_g+
+""".split()
+LAST = """
+Ge_t Pw_t1 Ne_t0 xg_s1 key_t0 Ne_t1 zqb_g Pw_t2 Pw_t3 xg_s0 zqc_g Pw_t4 key_t1 d_t2 ab_s2 dd_g0 dd_g1 d_t3 key_t2 d_t0 d_t1 r_s ab_s0 th_v0
+ab_s1 key_t3 ab_s3 key_t4 key_t5 sco_v th_v1 q_v sk_t TW_s Re_t R_t Lx_s Lc_s TWd_g At_g rf_s XO_s De_t yw_t th_v2 A_v D_t cnb_t1 cnb_t0 td_v0
+yw_v rn_v cna_t1 cnb_t2 cW_t cna_t0 eqc_v cna_t2 Gt_t0 dwl_s X_v cu_s Gt_t1 yc_t yc_v xc_s td_v1 dcu_s cut_v0 cna_t3 cnb_t3 sg_s1 sg_s0 G_t0
+ga_s0 G_t1 ga_s1 cf_s0 cut_v1 cut_v2 cut_v3 add_g0+ cut_v4 cut_v5 XO_v+ cut_v6 cut_v7 Gn_v1 CAN_v0 Gn_v0 cf_s1 CAN_v1 cw_s+ sc_v0+ add_g1+
+sc_v1+ sc_v2+ sc_v3+ sc_v4+
+""".split()
+FIRST = """
+ones_V WN_V cn_V Knp_V Gnp_V0 Gnp_V1 dum_G cc_V1 cc_V3 I_G At_V neg_V tmp_G0 WB_V pci_G blk_G WB_G barb_V k_G bar_G SEL_G tmp_G1 triz_V RA_G
+cb_S p_V0 k_V kB_V c_V TCb_V TWd_V Ib_S In_S Ibn_S IBp_S Ih_S sI_S blkb_S WNb_S cc_V2 blkz_V Ihn_S cW_T cc_V0 lxa_V Gn_S WN_S0 blkS_S sv_S
+Gw_T0 p_V1 pk_V xc_V Gw_T1 rw_T lxb_V r_V zl_V dmask_V thr_V X_V0 yc_V vl_V wcol_V resetv_V X_V1 IBn_S WO_S WN_S1 X_S wU_S repw_S WD_V cwl_V
+X_V2 wW_S uW_S eqw_V1 eqw_V3 eqw_V5 eqw_V6 eqw_V7 eqw_V8 eqw_V13 Kn_s Gu_S Pw_T0 Kt_t0 Kt_t1 eqw_V4 eqw_V14 eqw_V9 eqw_V10 Z_V eqw_V12 eqw_V11
+eqw_V2 CAN_S xg_s3 eqw_V0 Ku_v BLKa_G eqw_V15 It_g Ge_t0 Ge_t1 tmp_G2 c_G BLKb_G tmp_G3 BLKc_G tmp_G4 Pw_T1 key_t0 zq_s xg_s2 Zb_g zqb_g zqc_g
+sc_v0 tri_V Pw_T2 Pw_T3 Pw_T4 Dt_t E_S xg_s0 key_t1 dd_g0 dd_g1 dumc_G qp_G xg_s1 sc_v1 d_t0 key_t2 d_t1 RAb_S WBb_G
+""".split()
+PERIOD, AHEAD = 15.5, 2.0
+SCORES = ((4, 1), (4, 2), (4, 2), (2, 2), (2, 2))
+UNBIAS = "aavs"
+SHARE = {"cna": "n", "cnb": "n", "cW": "c", "yc": "c", "yw": "c", "S": "c", "Ga": "a", "Na": "a", "Gb": "b", "Nb": "b"}
 
 
 def phases(words):
@@ -62,355 +77,352 @@ def phases(words):
         name = w.rstrip("+-")
         kind = name.rstrip("0123456789")
         ph.setdefault(kind, {})[int(name[len(kind):] or 0)] = PERIOD * (p / len(words) - w.count("+") + w.count("-"))
-    return {k: [d[j] for j in sorted(d)] for k, d in ph.items()}
+    return ph
 
 
-PHASE = phases(ORDER)
+def opening(words):
+    return {k: {j: x * (1 + AHEAD / PERIOD) - PERIOD for j, x in d.items()} for k, d in phases(words).items()}
 
 
-def dv(n): return 0.06 + max(n, 64) * CY
-def dh(n): return 0.06 + max(n * 0.5, 64) * CY
-def dg(n): return 0.05 + n * GA * CY
-def ds(n): return 0.05 + n * SC * CY
-def sg(n): return SG + n * GA * CY
-def sa(n): return SF + n * CY
-def ga(n): return 0.17 + 2 * n * CY
-def pe(*ns): return sum(ns) * PEC + PEF * len(ns) + 0.02
+PHASE = [phases(ORDER), phases(LAST), opening(FIRST)]
 
 
 def rank_program(g, core, T, topo):
-    rank = T.rank_of(core)
-    if rank is None:
+    if T.rank_of(core) is None:
         return
+    ops = calls(g, core, T, topo)
+    depend(ops)
+    order, bank, extra = place(ops, dues(ops, PHASE))
+    emit(g, T, ops, order, bank, extra)
+
+
+def calls(g, core, T, topo):
+    rank = T.rank_of(core)
     V, S, PE, Y = g.vector, g.scalar, g.tensor, g.sync
+    mm, act = PE.matmul, S.activation
     ops, now = [], [None]
 
-    def op(eng, cost, calls, R=(), W=(), tile=None, lat=0.0, sem=None, cnt=0):
-        ops.append({"e": eng, "c": cost, "f": calls, "R": list(R), "W": list(W), "tile": tile, "lat": lat,
-                    "sem": sem, "cnt": cnt, "i": len(ops), "t": now[0]})
+    def op(eng, calls, R=(), W=(), tile=None, sem=None, cnt=0):
+        ops.append({"e": eng, "f": calls, "R": list(R), "W": list(W), "tile": tile, "sem": sem, "cnt": cnt, "i": len(ops), "t": now[0]})
 
-    def v(cost, f, R, W): op("v", cost, [f], R, W)
-    def s(cost, f, R, W): op("s", cost, [f], R, W)
-    def vp(cost, f, tile, R, W): op("v", cost, lambda B: [lambda: f(B)], R, W, tile=tile)
-    def sp(cost, f, tile, R, W): op("s", cost, lambda B: [lambda: f(B)], R, W, tile=tile)
-    def on_v(kind): return kind + "_v" in PHASE
-    mm, act = PE.matmul, S.activation
+    def v(f, R, W): op("v", [f], R, W)
+    def s(f, R, W): op("s", [f], R, W)
+    def vp(f, tile, R, W): op("v", lambda B: [lambda: f(B)], R, W, tile=tile)
+    def sp(f, tile, R, W): op("s", lambda B: [lambda: f(B)], R, W, tile=tile)
 
     def t_(tile, prods, R, W=()):
-        op("t", pe(*[p[5] for p in prods(T.ps0)]), lambda B: [lambda p=p: mm(*p[:5]) for p in prods(B)], R, W, tile=tile)
+        op("t", lambda B: [lambda p=p: mm(*p) for p in prods(B)], R, W, tile=tile)
 
-    def parts(name, t, early, R1, late, R2):
-        tn = "%s%d" % (name, t)
+    def group(ps, start, stop):
+        return [p + (start and j == 0, stop and j == len(ps) - 1) for j, p in enumerate(ps)]
 
-        def flags(ps, first): return [p[:3] + (first and j == 0, not first and j == len(ps) - 1, p[3]) for j, p in enumerate(ps)]
-        t_(tn, lambda B: flags(early(B), True), R1, [name + "e"])
-        t_(tn, lambda B: flags(late(B), False), R2 + [name + "e"])
+    def parts(name, t, early, R1, late, R2, start=True):
+        t_("%s%d" % (name, t), lambda B: group(early(B), start, False), R1, [name + "e"])
+        t_("%s%d" % (name, t), lambda B: group(late(B), False, True), R2 + [name + "e"])
 
     def ts(out, i0, s1, s2, o0, o1=None):
         if o1 is None:
             return V.tensor_scalar(out, i0, s1, None, o0)
         return V.tensor_scalar(out, i0, s1, s2, o0, o1)
 
-    def pick(name, out, src, R, pat, cmp, base, cm):
-        n = 1
-        for _, b in pat:
-            n *= b
-        op("g", ga(n), [lambda: g.affine_select(out, src, pat, cmp, 0.0, base, cm)], R, [name])
+    def pick(name, out, src, R, pat, cmp, base, cm, other=0.0):
+        op("g", [lambda: g.affine_select(out, src, pat, cmp, other, base, cm)], R, [name])
 
-    def lin(kind, out, src, scale, bias, n, R, W, tile=None, how="plain", relu=False, e=None):
-        if kind + "_g" in PHASE:
-            return pick(W[0], out, src, R, [[0, n]], A.is_ge, 0, 0)
+    def copy(name, out, src, R, n):
+        pick(name, out, src, R, [[0, n]], A.is_ge, 0, 0)
+
+    def lin(kind, out, src, scale, bias, R, W, tile=None, relu=False, e=None):
+        own = [x for x in "vs" if now[0] == NT - 1 and kind + "_" + x in PHASE[1]]
+        e = e or (own or [x for x in "vs" if kind + "_" + x in PHASE[0]] or ["s"])[0]
 
         def on_vector(x): return ts(out, x, bias, 0.0, A.add, A.max) if relu else ts(out, x, scale, bias, A.mult, A.add)
         def on_scalar(x): return act(out, x, AF.Relu if relu else AF.Identity, bias=bias, scale=scale)
-        e = e or ("v" if on_v(kind) else "s")
         f = on_vector if e == "v" else on_scalar
-        cost = {"v": {"plain": dv, "half": dh, "gather": dg}, "s": {"plain": sa, "half": sa, "gather": sg}}[e][how](n)
-        op(e, cost, (lambda B: [lambda: f(src(B))]) if tile else [lambda: f(src)], R, W, tile=tile)
+        op(e, (lambda B: [lambda: f(src(B))]) if tile else [lambda: f(src)], R, W, tile=tile)
 
-    def sign(kind, out, src, bar, tile, W, half=False):
-        if on_v(kind):
-            vp(dv(256), lambda B: ts(out, src(B), bar, 0.5, A.is_gt, A.subtract) if half else ts(out, src(B), bar, 2.0, A.is_gt, A.mult), tile, [], W)
-        else:
-            sp(sa(256), lambda B: act(out, src(B), AF.Sign, bias=-bar), tile, [], W)
-    one = dv(64)
-
-    def load(name, out, src, W, lat):
-        op("y", 0.1, [lambda: Y.dma_start(out, src)], [], W, lat=lat, sem="ld_" + name, cnt=16)
-
-    what = {"cut": (T.vin[0:8, :], T.cut[:], "vin", 0.0), "trail": (T.tin[:], T.trail[:], "tin", 0.3), "canal": (T.cin[:], T.canal[:], "cin", 1.3),
-            "z": (T.zin[:], T.z[:], "zin", 0.1)}
-    for q in range(4):
-        what["x%d" % q] = (T.X[:, 1024 * q:1024 * q + 1024], T.x[:, 1024 * q:1024 * q + 1024], "X%d" % q, 0.6)
-    lat = 2.0
-    for name in LOADS:
-        lat += what[name][3]
-        load(name, what[name][0], what[name][1], [what[name][2]], lat)
     XC = ["X0", "X1", "X2", "X3"]
+    XOC = ["XO0", "XO1", "XO2", "XO3"]
+    what = {"cut": (T.vin[0:8, :], T.cut[:], "vin"), "trail": (T.tin[:], T.trail[:], "tin"), "canal": (T.cin[:], T.canal[:], "cin"),
+            "z": (T.zin[:], T.z[:], "zin")}
+    for q in range(4):
+        what["x%d" % q] = (T.X[:, 1024 * q:1024 * q + 1024], T.x[:, 1024 * q:1024 * q + 1024], XC[q])
+    for name in LOADS:
+        op("y", [lambda w=what[name]: Y.dma_start(w[0], w[1])], [], [what[name][2]], sem="ld_" + name, cnt=16)
 
     def iota(name, out, pat, base, cm, f=True):
-        n = 1
-        for a, b in pat:
-            n *= b
         kw = {"allow_small_or_imprecise_dtypes": True} if f else {}
-        op("g", 0.13 + 2 * n * CY, [lambda: g.iota(out, pat, base, cm, **kw)], [], [name])
+        op("g", [lambda: g.iota(out, pat, base, cm, **kw)], [], [name])
 
-    def fill(name, ap, val, n):
-        v(dv(n), lambda: V.memset(ap, val), [], [name])
+    def fill(name, ap, val):
+        v(lambda: V.memset(ap, val), [], [name])
 
-    def scaled(name, out, src, R, val, n, bias=0.0):
-        s(sa(n), lambda: act(out, src, AF.Identity, bias=bias, scale=val), R, [name])
+    def scaled(name, out, src, R, val):
+        s(lambda: act(out, src, AF.Identity, bias=0.0, scale=val), R, [name])
 
-    def between(name, out, src, R, pat, lo, hi):
-        n = 1
-        for _, b in pat:
-            n *= b
-        pick("tmp", T.tmp[:, 0:n], src, R, pat, A.is_ge, -lo, 1)
+    def between(name, out, n, pat, lo, hi):
+        pick("tmp", T.tmp[:, 0:n], T.ones[:, 0:n], ["ones"], pat, A.is_ge, -lo, 1)
         pick(name, out, T.tmp[:, 0:n], ["tmp"], [[-a, b] for a, b in pat], A.is_ge, hi, -1)
 
-    fill("ones", T.ones[:], 1.0, 128)
-    fill("neg", T.neg[0:40, :], -BIG, 72)
-    fill("c160", T.c160[:], BIAS, 128)
-    fill("WB", T.WB[0:40, :], 0.0, 72)
-    for p0 in (0, 32):
-        pick("WB", T.WB[p0:p0 + 8, :], T.neg[p0:p0 + 8, :], ["neg"], [[1, 144]], A.is_equal, -15, -16)
-    for name in ("I16", "Ib"):
-        pick(name, T[name][:], T.ones[:, 0:128], ["ones"], [[-1, 128]], A.is_equal, 0, 1)
-    big = 2 * BIG if on_v("sg") else BIG
-    for name, val in (("Ibn", -1.0), ("IBn", -big), ("IBp", big), ("Ih", 0.5), ("Ihn", -0.5)) + ((("sI0", 0.97),) if VBANKS else ()):
-        scaled(name, T[name][:], T.I16[:], ["I16"], val, 128)
-    if VBANKS:
-        scaled("Ioff", T.Ioff[:], T.I16[:], ["I16"], 10000.0 + 0.97 - 307.2, 128, -10000.0)
-    else:
-        fill("lim0", T.lim0[:], -6144.0, 1)
-    scaled("IB8", T.IB8[0:8, :], T.I16[0:8, 0:8], ["I16"], -BIG, 8)
-    between("blk1", T.blk1[:], T.ones[:, 0:8], ["ones"], [[-16, 8]], 0, 15)
-    for name, val in (("blkb", 1.0), ("blkS", 4096.0), ("WO", 4.0)):
-        scaled(name, T[name][:], T.blk1[:], ["blk1"], val, 8)
-    between("BLKa", T.BLK[:, 0:128], T.ones[:, 0:128], ["ones"], [[-16, 8], [0, 16]], 0, 15)
-    between("BLK", T.BLK[:, 128:256], T.ones[:, 0:128], ["ones", "BLKa"], [[-16, 8], [0, 16]], 16, 31)
-    fill("WN", T.WN[:], 0.0, 8)
-    s(sa(4), lambda: act(T.WN[:, 1:8:2], T.blk1[:, 0:8:2], AF.Copy, scale=4.0), ["blk1"], ["WN"])
-    pick("comb", T.comb[:], T.ones[:, 0:144], ["ones"], [[0, 9], [1, 16]], A.is_equal, -15, 0)
+    fill("ones", T.ones[:], 1.0)
+    fill("neg", T.neg[0:40, :], -BIG)
+    fill("c160", T.c160[:, 0:32], BIAS)
+    fill("c160n", T.c160[:, 32:64], -BIAS)
+    fill("At", T.At[:], 0.0)
+    fill("WB", T.WB[0:32, :], 0.0)
+    for name, p0 in (("WB", 0), ("WBb", 32)):
+        pick(name, T.WB[p0:p0 + 8, :], T.neg[p0:p0 + 8, :], ["neg"], [[1, 144]], A.is_equal, -15, -16)
+    pick("I16", T.I16[:], T.ones[:, 0:128], ["ones"], [[-1, 128]], A.is_equal, 0, 1)
+    for name, val in (("Ib", 1.0), ("Ibn", -1.0), ("In16", -1.0), ("IBn", -BIG), ("IBp", BIG), ("Ih", 0.5), ("Ihn", -0.5), ("sI0", 0.97)):
+        scaled(name, T[name][:], T.I16[:], ["I16"], val)
+    between("blk1", T.blk1[:], 8, [[-16, 8]], 0, 15)
+    fill("blkz", T.blkb[:, 0:32], 0.0)
+    for name, out, val in (("blkb", T.blkb[:, 32:40], 1.0), ("blkS", T.blkS[:], 4096.0), ("WO", T.WO[:], 4.0)):
+        scaled(name, out, T.blk1[:], ["blk1"], val)
+    between("BLKa", T.BLK[:, 0:128], 128, [[-16, 8], [0, 16]], 0, 15)
+    between("BLKb", T.BLK[:, 128:256], 128, [[-32, 4], [-200, 2], [0, 16]], 16, 31)
+    between("BLKc", T.BLK[:, 256:384], 128, [[-32, 4], [200, 2], [0, 16]], 200, 215)
+    fill("WN", T.WN[:, 0:16], 0.0)
+    s(lambda: act(T.WN[:, 1:8:2], T.blk1[:, 0:8:2], AF.Copy, scale=-BIG), ["blk1"], ["WN"])
+    s(lambda: act(T.WN[:, 8:16:2], T.blk1[:, 1:8:2], AF.Copy, scale=-BIG), ["blk1"], ["WN"])
+    scaled("WNb", T.WN[:, 16:24], T.blk1[:], ["blk1"], -BIG)
     pick("tmp", T.tmp[32:40, :], T.ones[32:40, 0:128], ["ones"], [[-1, 8], [0, 16]], A.is_equal, 0, 1)
-    scaled("E8", T.E8[32:40, :], T.tmp[32:40, :], ["tmp"], -512.0, 128)
-    fill("RA", T.RA[0:32, :], 0.0, 64)
-    fill("RA", T.RA[0:9, :], BIAS + 63.25, 64)
-    fill("RA", T.RA[0:8, :], 0.0, 64)
-    scaled("RAb", T.RA[32:40, :], T.E8[32:40, :], ["E8"], -1.0, 128)
-    iota("dum", T.dum[:], [[-int(BIG), 3], [-64, 16]], 2 * int(BIG) - 2048, -4)
-    iota("pci", T.pci[:], [[0, 1]], 0, 1, False)
+    scaled("E8", T.E8[32:40, :], T.tmp[32:40, :], ["tmp"], -512.0)
+    pick("RA", T.RA[0:32, :], T.At[0:32, 0:128], ["At"], [[0, 128]], A.not_equal, -8, 1, BIAS + 63.25)
+    scaled("RAb", T.RA[32:40, :], T.E8[32:40, :], ["E8"], -1.0)
+    iota("dum", T.dum[:, 0:32], [[-3072, 2], [-16, 16]], 2 * int(BIG) + 1024, -1)
+    iota("dumc", T.dum[:, 32:48], [[-16, 16]], -2048, -1)
+    iota("pci", T.pci[:, 0:1], [[0, 1]], 0, 1, False)
     iota("k256", T.k256[:], [[0, 16], [1, 16]], 0, 0)
-    pk, wcol = T.col[:, 0:1], T.col[:, 1:2]
-    v(one, lambda: ts(T.q2[:, 0:1], T.pci[:], 15, None, A.bitwise_and), ["pci"], ["q2"])
-    v(one, lambda: V.tensor_copy(pk, T.q2[:, 0:1]), ["q2"], ["pk"])
-    v(dh(256), lambda: ts(T.dmask[:], T.k256[:], pk, None, A.is_equal), ["k256", "pk"], ["dmask"])
-    v(one, lambda: V.tensor_copy(T.zl[:], T.k256[:, 0:32]), ["k256"], ["zl"])
-    v(dh(256), lambda: ts(T.r1[:], T.k256[:], 0.0, 0.5, A.not_equal, A.mult), ["k256"], ["r1"])
-    v(dh(256), lambda: ts(T.xc[:], T.k256[:], 0.0, -2.5, A.is_equal, A.mult), ["k256"], ["xc"])
-    v(dh(256), lambda: V.tensor_tensor_scan(T.thr[:], T.r1[:], T.xc[:], 0.0, A.mult, A.add), ["r1", "xc"], ["thr"])
-    v(dh(256), lambda: ts(T.resetv[:], T.xc[:], 8.0e6, None, A.mult), ["xc"], ["resetv"])
-    v(one, lambda: V.tensor_tensor(T.yc[:], T.thr[:, 0:16], T.dmask[:, 0:16], A.mult), ["thr", "dmask"], ["yc"])
-    v(one, lambda: V.tensor_reduce(wcol, T.yc[:], AxisListType.X, A.add), ["yc"], ["wcol"])
-    v(one, lambda: ts(T.WD[:], T.blk1[:], wcol, -0.4, A.mult, A.mult), ["blk1", "wcol"], ["WD"])
-    fill("k2047", T.krow[0:1, :], 2047.0, 64)
-    fill("kB", T.krow[32:33, :], -BIG, 64)
-    fill("c32", T.c32[32:40, :], -0.025 if VBANKS else 0.5, 128)
-    fill("Knp", T.Kn[:, 0:16], 0.0, 16)
-    fill("At", T.At[:], 0.0, 128)
-    for name in ("TW0", "TW1"):
-        op("v", dh(256), [lambda name=name: V.memset(T[name][0:40, 0:256], 1.0)], [], [name + "b", name + "c"])
-        op("v", dh(256), [lambda name=name: V.memset(T[name][0:40, 256:512], 0.0)], [], [name + "d"])
+    pk, wcol, bar = T.col[:, 0:1], T.col[:, 1:2], T.col[0:40, 2:3]
+    v(lambda: ts(T.pci[:, 1:2], T.pci[:, 0:1], 15, None, A.bitwise_and), ["pci"], ["p15"])
+    v(lambda: V.tensor_copy(pk, T.pci[:, 1:2]), ["p15"], ["pk"])
+    v(lambda: ts(T.dmask[:], T.k256[:], pk, None, A.is_equal), ["k256", "pk"], ["dmask"])
+    fill("triz", T.tri[:, 256:384], 0.0)
+    v(lambda: ts(T.tri[:, 0:256], T.k256[:], pk, BIG, A.is_le, A.mult), ["k256", "pk"], ["tri"])
+    v(lambda: V.tensor_copy(T.zl[:], T.k256[:, 0:16]), ["k256"], ["zl"])
+    v(lambda: ts(T.pci[:, 2:3], T.pci[:, 0:1], 1, 8, A.arith_shift_right, A.bitwise_and), ["pci"], ["p8"])
+    v(lambda: V.tensor_copy(T.lx[:, 0:1], T.pci[:, 1:2]), ["p15"], ["lxa"])
+    v(lambda: ts(T.lx[:, 1:2], T.pci[:, 2:3], pk, None, A.add), ["p8", "pk"], ["lxb"])
+    iota("q2p", T.q2[:, 16:24], [[0, 8]], 0, 0, False)
+    v(lambda: ts(T.r1[:], T.k256[:], 0.0, 0.5, A.not_equal, A.mult), ["k256"], ["r1"])
+    v(lambda: ts(T.xc[:], T.k256[:], 0.0, -2.5, A.is_equal, A.mult), ["k256"], ["xc"])
+    v(lambda: V.tensor_tensor_scan(T.thr[:], T.r1[:], T.xc[:], 0.0, A.mult, A.add), ["r1", "xc"], ["thr"])
+    v(lambda: ts(T.resetv[:], T.xc[:], 8.0e6, None, A.mult), ["xc"], ["resetv"])
+    v(lambda: V.tensor_tensor(T.yc[:], T.thr[:, 0:16], T.dmask[:, 0:16], A.mult), ["thr", "dmask"], ["yc"])
+    v(lambda: V.tensor_reduce(wcol, T.yc[:], AxisListType.X, A.add), ["yc"], ["wcol"])
+    v(lambda: ts(T.WD[:], T.blk1[:], wcol, -0.4, A.mult, A.mult), ["blk1", "wcol"], ["WD"])
+    fill("k2047", T.krow[0:1, :], 2047.0)
+    pick("bar", T.col[0:32, 2:3], T.ones[0:32, 0:1], ["ones"], [[0, 1]], A.is_ge, -8, 1)
+    fill("barb", T.col[32:40, 2:3], -8.5)
+    pick("c32", T.c32[0:32, :], T.At[0:32, 0:128], ["At"], [[0, 128]], A.not_equal, -8, 1, (0.97 - 307.2) / 256)
+    scaled("c32b", T.c32[32:40, :], T.ones[32:40, 0:128], ["ones"], -0.025)
+    fill("kB", T.krow[32:33, :], -BIG)
+    for name, rows in (("Knp", T.Kn), ("Gnp0", T.Gn0), ("Gnp1", T.Gn1)):
+        fill(name, rows[:, 0:16], 0.0)
+    CC = ["cc%d" % j for j in range(4)]
+    for j, val in enumerate((1.0, -MID, -1.0, MID)):
+        fill(CC[j], T.cc[:, j:j + 1], val)
+    scaled("sv0", T.sv0[:], T.cc[:], CC, 0.97)
+    fill("TWd", T.TW[0:40, 256:512], -1.0)
 
-    lin("", T.TC[0:8, :], T.vin[0:8, :], -1.0, 2048.0, 256, ["vin"], ["TCb"], e="v")
-    lin("", T.Gn0[:], T.tin[:], -1.0, 2048.0, 256, ["tin"], ["Gn0"], e="v")
-    lin("", T.Gu0[:], T.tin[:], 1.0, 0.0, 256, ["tin"], ["Gu0"], e="v")
-    lin("", T.Z[:, 0:256], T.zin[:], 1.0, BIAS, 256, ["zin"], ["Z0"], how="half", e="v")
-    lin("", T.CAN[:, 0:1024], T.cin[:], -1.0, 2048.0, 1024, ["cin"], ["CAN"], e="v")
+    lin("", T.TC[0:8, :], T.vin[0:8, :], -1.0, 2048.0, ["vin"], ["TCb"], e="v")
+    lin("", T.Gn0[:, 16:272], T.tin[:], -1.0, 2048.0, ["tin"], ["Gn0_0", "Gn0_1"], e="s")
+    lin("", T.Z[:, 0:256], T.zin[:], 1.0, BIAS, ["zin"], ["Z0"], e="v")
+    lin("", T.CAN[:, 0:1024], T.cin[:], 1.0, 0.0, ["cin"], ["CAN"], e="s")
     for q in range(4):
-        lin("", T.X[:, 1024 * q:1024 * q + 1024], T.X[:, 1024 * q:1024 * q + 1024], 1.0, BIAS, 1024, ["X%d" % q], ["X%d" % q], how="half", e="vsvv"[q])
+        lin("", T.X[:, 1024 * q:1024 * q + 1024], T.X[:, 1024 * q:1024 * q + 1024], 1.0, BIAS, [XC[q]], [XC[q]], e="svvv"[q])
+
+    def turned(B, rows, blocks):
+        return ([(B[u:u + 32, a:256:16], rows[u:u + 32, 16 * a:16 * a + 32], T.I16[u:u + 32, u + 16:u + 32], True, True)
+                 for a in blocks for u in (0, 32, 64, 96)]
+                + [(B[u:u + 16, a:256:16], rows[u:u + 32, 16 * a + 16:16 * a + 32], T.I16[u:u + 32, u:u + 16], True, True)
+                   for a in blocks for u in (0, 32, 64, 96)])
 
     def firsts(t):
         k0 = (t + 12) % 16
-        wW, cwl, TW, SEL, Wk, Gn = ["%s%d" % (n, t % 2) for n in ("wW", "cwl", "TW", "SEL", "Wk", "Gn")]
+        wW, wU, cwl, SEL, Gn, Gu = ["%s%d" % (n, t % 2) for n in ("wW", "wU", "cwl", "SEL", "Gn", "Gu")]
         pick(SEL, T[SEL][:], T.ones[:, 0:128], ["ones"], [[-16, 8], [0, 16]], A.is_equal, -k0, 1)
-        pick(Wk, T[Wk][:], T.comb[:], ["comb"], [[1, 144]], A.is_equal, k0 - 15, -1)
-        t_("rw%d" % t, lambda B: [(B[:, 0:256], T[SEL][:], T[Gn][:], True, True, 256)]
-           + [(B[:, 256:272], T[Wk][:, 15 - b:143 - b], T[Gn][:, b:256:16], b == 0, b == 15, 64) for b in range(16)], [Gn, SEL, Wk])
-        lin("repw", T.repw[:], lambda B: B[:, 0:272], 0.25, 1536.375, 272, [], ["repw"], "rw%d" % t)
-        lin("wW", T[wW][:], lambda B: B[:, 256:272], 1.0, 0.0, 16, [], [wW], "rw%d" % t)
-        lin("uW", T.uW[:], T.repw[:, 256:272], 1.0, 0.0, 16, ["repw"], ["uW"])
-        lin("cwl", T[cwl][:], T.repw[:, 256:272], -1.0, 2048.0, 16, ["repw"], [cwl])
+        t_("rw%d" % t, lambda B: [(B[:, 0:256], T[SEL][:], T[Gn][:, 16:272], True, True)], [Gn + "_0", Gn + "_1", SEL])
+        tn = "Gw%d" % t
+        for h in range(2):
+            t_(tn, lambda B, h=h: turned(B, T[Gn], range(8 * h, 8 * h + 8)), [Gn + "_0", "%s_%d" % (Gn, h), "Gnp%d" % (t % 2), "I16"])
+        lin("repw", T.repw[:], lambda B: B[:, 0:256], 0.25, 1536.375, [], ["repw"], "rw%d" % t)
+        lin("wU", T[wW][:, 0:16], lambda B: B[:, 16 * k0:16 * k0 + 16], 0.25, 1536.375, [], [wU], tn)
+        lin("uW", T.uW[:], T[wW][:, 0:16], 1.0, 0.0, [wU], ["uW"])
+        lin("Gu", T[Gu][:], lambda B: B[:, 0:256], -1.0, 2048.0, [], [Gu], tn)
+        lin("wW", T[wW][:, 16:32], lambda B: B[:, 16 * k0:16 * k0 + 16], 1.0, 0.0, [], [wW], tn)
+        lin("cwl", T[cwl][:], T[wW][:, 0:16], -1.0, 2048.0, [wU], [cwl])
         tn = "Pw%d" % t
-        t_(tn, lambda B: [(B[0:8, 0:256], T.Ib[0:8, 0:8], T.thr[0:8, :], True, False, 256)], ["Ib", "thr", "repw"], [tn])
-        for blocks in (range(0, 3), range(3, 7), range(7, min(11, 16 - SHORT)), range(min(11, 16 - SHORT), 16)):
+        t_(tn, lambda B: [(B[0:40, 256:512], T.Ib[0:8, 0:40], T.thr[0:8, :], True, False)], ["Ib", "thr", "repw"], [tn])
+        for blocks in (range(0, 3), range(3, 7), range(7, 11), range(11, 16)):
             for a in blocks:
-                if a < 16 - SHORT:
-                    v(dh(EQN[a]), lambda a=a: ts(T.eqw[:, EQO[a]:EQO[a + 1]], T.repw[:, 16 * a:256], T.uW[:, a:a + 1], None, A.is_equal),
-                      ["repw", "uW"], ["eqw_%d" % a])
-                else:
-                    s(sa(EQN[a]), lambda a=a: act(T.dw[:, EQO[a] - EQO[8]:EQO[a + 1] - EQO[8]], T.repw[:, 16 * a:256], AF.Abs, bias=T.uW[:, a:a + 1], scale=-1.0),
-                      ["repw", "uW"], ["dw_%d" % a])
-            if SHORT and blocks[-1] == 15:
-                a0 = EQO[16 - SHORT]
-                v(dh(EQO[16] - a0), lambda: ts(T.eqw[:, a0:EQO[16]], T.dw[:, a0 - EQO[8]:EQO[16] - EQO[8]], 0.0, None, A.is_equal),
-                  ["dw_%d" % a for a in range(16 - SHORT, 16)], ["eqs"] + ["eqw_%d" % a for a in range(16 - SHORT, 16)])
+                v(lambda a=a: ts(T.eqw[:, EQO[a]:EQO[a + 1]], T.repw[:, 16 * a:256], T.uW[:, a:a + 1], None, A.is_equal), ["repw", "uW"], ["eqw_%d" % a])
 
             def sums(B, blocks=blocks):
                 r = []
                 for a in blocks:
-                    r.append((B[0:8, 16 * a:16 * a + 16], T.WD[:], T.eqw[:, EQO[a]:EQO[a] + 16], False, a == 15, 16))
+                    r.append((B[0:8, 256 + 16 * a:272 + 16 * a], T.WD[:], T.eqw[:, EQO[a]:EQO[a] + 16], False, False))
                     if a < 15:
-                        r.append((B[0:8, 16 * a + 16:256], T.WO[:], T.eqw[:, EQO[a] + 16:EQO[a + 1]], False, False, EQN[a] - 16))
+                        r.append((B[0:8, 272 + 16 * a:512], T.WO[:], T.eqw[:, EQO[a] + 16:EQO[a + 1]], False, False))
                 return r
             t_(tn, sums, ["eqw_%d" % a for a in blocks] + ["WD", "WO", tn], [tn])
-        sign("TWb", T[TW][0:8, 0:256], lambda B: B[0:8, 0:256], 0.0, tn, [TW + "b"])
-        pick(TW + "d", T[TW][0:8, 256:512], T[TW][0:8, 0:256], [TW + "b"], [[0, 256]], A.is_ge, 0, 0)
 
-    t_("cW", lambda B: [(B[:, 0:16], T.WB[0:8, 15 - b:143 - b], T.TC[0:8, b:256:16], b == 0, b == 15, 64) for b in range(16)], ["TCb", "WB"])
-    vp(one, lambda B: ts(T.vl[:], B[:, 0:16], 0.25 / BIG, 511.625, A.mult, A.add), "cW", [], ["vl"])
+    t_("cW", lambda B: [(B[:, 0:16], T.WB[0:8, 15 - b:143 - b], T.TC[0:8, b:256:16], b == 0, b == 15) for b in range(16)], ["TCb", "WB"])
+    vp(lambda B: ts(T.vl[:], B[:, 0:16], 0.25 / BIG, 511.625, A.mult, A.add), "cW", [], ["vl"])
     firsts(0)
 
     def step(t):
         p, q = t % 2, 1 - t % 2
         last = t == NT - 1
         k0 = (t + 12) % 16
-        Z, Gn, Gu, TW, sI = "Z%d" % t, "Gn%d" % p, "Gu%d" % p, "TW%d" % p, "sI%d" % p
-        Gn1, Gu1, sI1 = "Gn%d" % q, "Gu%d" % q, "sI%d" % q
-        wW, cwl, It, lim, lim1 = "wW%d" % p, "cwl%d" % p, "It%d" % p, "lim%d" % p, "lim%d" % q
+        Z = "Z%d" % t
+        Gn, Gu, sI, wW, cwl, It, sv = ["%s%d" % (n, p) for n in ("Gn", "Gu", "sI", "wW", "cwl", "It", "sv")]
+        Gn1, sI1, sv1 = ["%s%d" % (n, q) for n in ("Gn", "sI", "sv")]
         z0 = 1024 * t
         zz = T.Z[:, z0:z0 + 256]
-        Kn = T.Kn[:, 16:272]
-        if t:
-            lin("Kn", Kn, T.CAN[:, 0:1024].indirect(T.vl[:]), 1.0, 0.0, 256, ["CAN", "vl"], ["Kn"], how="gather")
-        else:
-            lin("Kn", Kn, T.cin[:].indirect(T.vl[:]), -1.0, 2048.0, 256, ["cin", "vl"], ["Kn"], how="gather")
+        TW = T.TW
+        can, CAN = (T.CAN[:, 0:1024], "CAN") if t else (T.cin[:], "cin")
+        lin("Kn", T.Kn[:, 16:272], can.indirect(T.vl[:]), -1.0, 2048.0, [CAN, "vl"], ["Kn"])
         tn = "Kt%d" % t
-        t_(tn, lambda B: [(B[u:u + 32, a:256:16], T.Kn[u:u + 32, 16 * a:16 * a + 32], T.I16[u:u + 32, u + 16:u + 32], True, True, 32)
-                          for a in range(16) for u in (0, 32, 64, 96)], ["Kn", "Knp", "I16"], [tn])
-        t_(tn, lambda B: [(B[u:u + 16, a:256:16], T.Kn[u:u + 32, 16 * a + 16:16 * a + 32], T.I16[u:u + 32, u:u + 16], True, True, 16)
-                          for a in range(16) for u in (0, 32, 64, 96)], ["Kn", "I16", tn], [tn])
-        lin("Ku", T.Ku[:], lambda B: B[:, 0:256], -1.0, 2048.0, 256, [], ["Ku"], tn)
-        for c in range(4):
-            s(sg(1024), lambda c=c: act(T.xg[:, 1024 * c:1024 * c + 1024], T.X[:, 0:4096].indirect(T[Gu][:, 64 * c:64 * c + 64]), AF.Copy, scale=-1.0),
-              XC + [Gu], ["xg_%d" % c])
+        for h in range(2):
+            t_(tn, lambda B, h=h: turned(B, T.Kn, range(8 * h, 8 * h + 8)), ["Kn", "Knp", "I16"])
+        lin("Ku", T.Ku[:], lambda B: B[:, 0:256], -1.0, 2048.0, [], ["Ku"], tn)
+        quads = [(k0 // 4 + j) % 4 for j in range(4)]
+        for j, c in enumerate(quads):
+            how = {"scale": -1.0} if j < 4 - ADDED else {"scale": T[sv][:, 2:3], "bias": T[sv][:, 3:4]}
+            s(lambda c=c, how=how: act(T.xg[:, 1024 * c:1024 * c + 1024], T.X[:, 0:4096].indirect(T[Gu][:, 64 * c:64 * c + 64]), AF.Identity, **how),
+              XC + [Gu, sv], ["xg_%d" % (2 * c), "xg_%d" % (2 * c + 1)])
+        if last:
+            for c, e in enumerate(UNBIAS):
+                a, b = 1024 * c, 1024 * c + 1024
+                if e == "a":
+                    op("g", [lambda a=a, b=b: g.dma_start(T.XO[:, a:b], T.X[:, a:b], accum_op=A.add)], [XC[c], XOC[c]], ["add%d" % c, XOC[c]],
+                       sem="add%d" % c, cnt=16)
+                else:
+                    lin("", T.XO[:, a:b], T.X[:, a:b], 1.0, -BIAS, [XC[c]], ["XO", XOC[c]], e=e)
+        elif t >= 2 and UNBIAS[t - 2:t - 1] == "a":
+            iota(XOC[t - 2], T.XO[:, 1024 * (t - 2):1024 * (t - 1)], [[0, 1024]], -int(BIAS), 0)
         pick(It, T[It][:], T.I16[:], ["I16"], [[0, 8], [1, 16]], A.not_equal, -t, 0)
-        lin("cw", T.cw[:], T.CAN[:, 0:1024].indirect(T[cwl][:]), 1.0, 0.0, 256, ["CAN", cwl], ["cw"], how="gather")
-        for nm, n, src in (("Zb", 256, Z), ("Zc", 512, "Zb")):
-            pick(nm, T.Z[:, z0 + n:z0 + 2 * n], T.Z[:, z0:z0 + n], [Z, src], [[0, n]], A.is_ge, 0, 0)
+        lin("cw", T.cw[:], can.indirect(T[cwl][:]), -1.0, 2048.0, [CAN, cwl], ["cw"])
+        for nm, n, src in (("Zb", 256, Z), ("Zc", 512, "Zb"))[:max(w for _, w in SCORES) - 1]:
+            copy(nm, T.Z[:, z0 + n:z0 + 2 * n], T.Z[:, z0:z0 + n], [Z, src], n)
         tn = "key%d" % t
-        t_(tn, lambda B: [(B[:, 0:256], T.krow[0:1, :], T.ones[0:1, :], True, False, 256)]
-           + [(B[:, 128 * h:128 * h + 128], T.Kn[:, 16 + 128 * h:144 + 128 * h], T.I16[:], False, False, 128) for h in range(2)],
+        t_(tn, lambda B: [(B[:, 0:256], T.krow[0:1, :], T.ones[0:1, :], True, False)]
+           + [(B[:, 128 * h:128 * h + 128], T.Kn[:, 16 + 128 * h:144 + 128 * h], T.I16[:], False, False) for h in range(2)],
            ["k2047", "ones", "Kn", "I16", "Ku"], [tn])
-        for c in range(4):
-            w = (1, 2, 4, 4)[c]
-            op("v", 4 // w * dg(256 * w),
-               [lambda k=k, w=w: V.tensor_tensor(T.sc[:, 256 * k:256 * (k + w)], T.X[:, 0:4096].indirect(T.Ku[:, 16 * k:16 * (k + w)]),
-                                                 T.Z[:, z0:z0 + 256 * w], A.max) for k in range(4 * c, 4 * c + 4, w)],
-               XC + ["Ku", Z] + ["Zb", "Zc"][:c], ["sc%d" % c])
-            t_(tn, lambda B, c=c: [(B[:, 128 * h + k:128 * h + 128:16], T.sc[:, 256 * k + 128 * h:256 * k + 128 * h + 128], T.blkS[:], False,
-                                    k == 15 and h == 1, 64) for k in range(4 * c, 4 * c + 4) for h in range(2)], ["sc%d" % c, "blkS", tn], [tn])
-        vp(dv(256), lambda B: V.tensor_tensor_scan(T.sco[:], T.resetv[:], B[:, 0:256], 0.0, A.add, A.max), tn, ["resetv"], ["sco"])
-        v(one, lambda: ts(T.q2[:], T.sco[:, 15:256:16], 4095, None, A.bitwise_and), ["sco"], ["q2"])
-        lin("Lc", T.Lc[:], T.q2[:], 1.0, -2047.0, 16, ["q2"], ["Lc"])
-        v(dg(256), lambda: V.tensor_tensor(T.A1[:], T.Lc[:].indirect(T.zl[:, 0:16]), T.dmask[:], A.mult), ["Lc", "zl", "dmask"], ["A1"])
+        k1 = 0
+        for c, (n, w) in enumerate(SCORES):
+            op("v", [lambda k=k, w=w: V.tensor_tensor(T.sc[:, 256 * k:256 * (k + w)], T.X[:, 0:4096].indirect(T.Ku[:, 16 * k:16 * (k + w)]),
+                                                      T.Z[:, z0:z0 + 256 * w], A.max) for k in range(k1, k1 + n, w)],
+               XC + ["Ku", Z] + ["Zb", "Zc", "Zc"][:w - 1], ["sc%d" % c])
+            t_(tn, lambda B, ks=range(k1, k1 + n): [(B[:, 128 * h + k:128 * h + 128:16], T.sc[:, 256 * k + 128 * h:256 * k + 128 * h + 128], T.blkS[:],
+                                                     False, k == 15 and h == 1) for k in ks for h in range(2)], ["sc%d" % c, "blkS", tn], [tn])
+            k1 += n
+        vp(lambda B: V.tensor_tensor_scan(T.sco[:], T.resetv[:], B[:, 0:256], 0.0, A.add, A.max), tn, ["resetv"], ["sco"])
+        v(lambda: ts(T.q2[:, 0:16], T.sco[:, 15:256:16], 4095, None, A.bitwise_and), ["sco"], ["q2"])
+        lin("Lc", T.Lc[:], T.q2[:, 0:16], 1.0, -2047.0, ["q2"], ["Lc"])
+        lin("Lx", T.Lx[:], T.q2[:].indirect(T.lx[:]), 1.0, -2047.0, ["q2", "q2p", "lxa", "lxb"], ["Lx"])
+        v(lambda: V.tensor_tensor(T.A1[:], T.Lc[:].indirect(T.zl[:]), T.dmask[:], A.mult), ["Lc", "zl", "dmask"], ["A1"])
 
-        def wrapped(B, stop):
-            return [(B[:, 8 * h:8 * h + 8], T.A1[:, 128 * h:128 * h + 128], T.blk1[:], h == 0, stop and h == 1, 64) for h in range(2)]
-        t_("cW%d" % t, lambda B: wrapped(B, True), ["A1", "blk1"])
-        lin("cu", T.cu[:], lambda B: B[:, 0:16], -1.0, 2048.0, 16, [], ["cu"], "cW%d" % t)
+        def wrapped(B, o):
+            return [(B[:, o + 8 * h:o + 8 * h + 8], T.A1[:, 128 * h:128 * h + 128], T.blk1[:]) for h in range(2)]
+        t_("cW%d" % t, lambda B: group(wrapped(B, 0), True, True), ["A1", "blk1"])
+        lin("cu", T.cu[:], lambda B: B[:, 0:16], -1.0, 2048.0, [], ["cu"], "cW%d" % t)
         if not last:
-            lin("vl", T.vl[:], lambda B: B[:, 0:16], -0.25, 511.625, 16, [], ["vl"], "cW%d" % t)
+            lin("vl", T.vl[:], lambda B: B[:, 0:16], -0.25, 511.625, [], ["vl"], "cW%d" % t)
         if t:
-            op("g", ga(16), [lambda: g.affine_select(T.At[:, t - 1:256:16], T.ones[:, 0:16], [[0, 16]], A.is_gt, 0.0, 0, 0)], ["ones"], ["Az", "At"])
-        lin("At", T.At[:, t:256:16], T.Lc[:], 1.0, 0.0, 16, ["Lc", "At"], ["At"])
-        lin("xc", T.xc[:], T.X[:, 0:4096].indirect(T.cu[:]), 0.5, -BIAS / 2 - 0.25, 256, XC + ["cu"], ["xc"], how="gather")
+            op("g", [lambda: g.affine_select(T.At[:, t - 1:256:16], T.ones[:, 0:16], [[0, 16]], A.is_gt, 0.0, 0, 0)], ["ones"], ["Az", "At"])
+        copy("At", T.At[:, t:256:16], T.Lc[:], ["Lc", "At"], 16)
+        lin("xc", T.xc[:], T.X[:, 0:4096].indirect(T.cu[:]), 0.5, (BIAS if last else -BIAS) / 2 - 0.25, XC + ["cu"], ["xc"])
         if not last:
             snt, arr = "snt%d" % (t + 1), "arr%d" % (t + 1)
-            parts("ZS", t, lambda B: [(B[:, 0:256], T.Ih[:], zz, 256)], ["Ih", Z], lambda B: [(B[:, 0:256], T.Ib[:], T.xc[:], 256)], ["Ib", "xc"])
-            lin("zs", T.ZS[:, 256 * t:256 * t + 256], lambda B: B[:, 0:256], 1.0, BIAS / 2, 256, [], ["zs%d" % t], "ZS%d" % t)
+            parts("ZS", t, lambda B: [(B[:, 0:256], T.Ih[:], zz)], ["Ih", Z], lambda B: [(B[:, 0:256], T.Ib[:], T.xc[:])], ["Ib", "xc"])
+            lin("zs", T.ZS[:, 256 * t:256 * t + 256], lambda B: B[:, 0:256], 1.0, BIAS / 2, [], ["zs%d" % t], "ZS%d" % t)
             dst = T.cores[(rank + 1 + t % 3) % len(T.cores)]
             rid, pid = topo.addr(dst)[0], topo.addr(dst)[1]
             ne = len(topo.engines(core, dst))
-            op("g", 1.0, [lambda: g.remote_dma(T.Z[:, z0 + 1024:z0 + 1280], T.ZS[:, 256 * t:256 * t + 256], T.sem[arr], T.sem[snt], pid=pid, routing_id=rid,
-                                               dma_engine_mask=topo.mask(core, dst))], ["zs%d" % t], ["way%d" % t], sem=snt, cnt=ne)
-            op("x", 0.0, [], ["way%d" % t], ["Z%d" % (t + 1)], lat=WAY, sem=arr, cnt=ne)
-        t_("rc%d" % t, lambda B: [(B[:, 0:256], T.BLK[:, 0:128], T.A1[:], True, True, 256), (B[:, 256:512], T.BLK[:, 128:256], T.A1[:], True, True, 256)],
-           ["A1", "BLK"])
-        lin("repc", T.repc[:], lambda B: B[:], 1.0, 0.0, 512, [], ["repc"], "rc%d" % t)
-        v(dg(512), lambda: V.tensor_tensor(T.eqc[:], T.Lc[:].indirect(T.zl[:]), T.repc[:], A.is_equal), ["Lc", "zl", "repc"], ["eqc"])
-        parts("Pc", t, lambda B: [(B[0:8, 0:256], T.Ib[0:8, 0:8], T.thr[0:8, :], 256)], ["Ib", "thr", "Lc"],
-              lambda B: [(B[0:8, 0:256], T.WD[:], T.eqc[:, 0:256], 256), (B[0:8, 0:256], T.WN[:], T.eqc[:, 256:512], 256)], ["WD", "WN", "eqc"])
-        sign("TCb", T.TC[0:8, :], lambda B: B[0:8, 0:256], 0.0, "Pc%d" % t, ["TCb"])
-        t_("yc%d" % t, lambda B: wrapped(B, False) + [(B[:, 8 * h:8 * h + 8], T.TC[0:8, 128 * h:128 * h + 128], T.IB8[0:8, :], False, h == 1, 64)
-                                                      for h in range(2)], ["A1", "blk1", "TCb", "IB8"])
-        upc = 0 if on_v("TCb") else 1
-        vp(one, lambda B: V.tensor_tensor(T.yc[:], B[:, 0:16], T.dum[:, 32 - 16 * upc:48 - 16 * upc], A.max), "yc%d" % t, ["dum"], ["yc"])
-        lin("dcu", T.dcu[:], T.yc[:], -1.0, 2048.0 + upc * BIG, 16, ["yc"], ["dcu"])
-        banks = [(h, kb) for h in range(2) for kb in sorted(range(4), key=lambda kb: (kb - k0) % 4)]
-        M = sI if VBANKS else "Ib"
-        for b, (h, kb) in enumerate(banks):
-            tn = "d%d_%d" % (t, b)
-            t_(tn, lambda B, h=h, kb=kb: [(B[:], T[M][:], T.xg[:, 2048 * h + kb:2048 * h + 2048:4], True, False, 512)]
-               + [(B[:, j:512:4], T[M][:], T.Z[:, z0 + 128 * h:z0 + 128 * h + 128], False, j == 3, 128) for j in range(4)],
-               [M, Z, "xg_%d" % (2 * h), "xg_%d" % (2 * h + 1)])
-            if b in VBANKS:
-                vp(dv(512), lambda B, b=b: ts(T.th[:, 512 * b:512 * b + 512], B[:], GRID, GRID, A.add, A.not_equal), tn, [], ["tv%d" % b, "th%d" % b])
-            else:
-                sp(sa(512), lambda B, b=b: act(T.ab[:, 512 * b:512 * b + 512], B[:], AF.Abs), tn, [], ["ab%d" % b])
-        for run in RUNS:
-            a, e = 512 * run[0], 512 * run[-1] + 512
-            if run[0] not in VBANKS:
-                v(dh(e - a), lambda a=a, e=e: ts(T.th[:, a:e], T.ab[:, a:e], 0.0 if VBANKS else T[lim][:], 16.0 if VBANKS else 6160.0, A.subtract, A.is_gt),
-                  ["ab%d" % b for b in run] + ([] if VBANKS else [lim]), ["th%d" % b for b in run])
-            t_("cnt%d" % t, lambda B, run=run: [(B[:, 128 * banks[b][0] + banks[b][1] + 4 * j:128 * banks[b][0] + 128:16], T.th[:, 512 * b + j:512 * b + 512:4],
-                                                 T.blkb[:], True, True, 64) for b in run for j in range(4)], ["th%d" % b for b in run] + ["blkb"])
-        sign("sg", T.sg[:], lambda B: B[:, 0:256], 8.5, "cnt%d" % t, ["sg"], half=True)
-        t_("sk%d" % t, lambda B: [(B[32:40, 128 * h:128 * h + 128], T.blkb[:], T.th[:, 2048 * h + k0 // 4:2048 * h + 512:4], True, True, 128) for h in range(2)],
-           ["th0", "th4", "blkb"])
-        sp(sa(256) + 0.02, lambda B: act(T[TW][32:40, 0:256], B[32:40, 0:256], AF.Sign, bias=-8.5, accum_out=T.acc[32:40, :]), "sk%d" % t, [], [TW + "c", "acc"])
+            op("g", [lambda: g.remote_dma(T.Z[:, z0 + 1024:z0 + 1280], T.ZS[:, 256 * t:256 * t + 256], T.sem[arr], T.sem[snt], pid=pid, routing_id=rid,
+                                          dma_engine_mask=topo.mask(core, dst))], ["zs%d" % t], ["way%d" % t], sem=snt, cnt=ne)
+            op("x", [], ["way%d" % t], ["Z%d" % (t + 1)], sem=arr, cnt=ne)
+        t_("D%d" % t, lambda B: [(B[:, 0:384], T.I16[:], T.tri[:], True, False)], ["I16", "tri", "triz", Z], ["Dt"])
+        parts("D", t, lambda B: [(B[:, j:384:16], T.In16[:], T.Lx[:, 0:24]) for j in range(16)], ["In16", "Lx", "Dt"],
+              lambda B: [(B[:, 0:256], T.BLK[:, 0:128], T.A1[:])]
+              + [(B[:, 256:384], T.BLK[:, 128 * h + 128:128 * h + 256], T.A1[:, 128 * h:128 * h + 128]) for h in range(2)],
+              ["A1", "BLKa", "BLKb", "BLKc"], start=False)
+        vp(lambda B: ts(T.eqc[:], B[:, 0:384], 0.0, None, A.is_equal), "D%d" % t, [], ["eqc"])
+        t_("yc%d" % t, lambda B: group(wrapped(B, 16) + [(B[:, 16 + 8 * h:24 + 8 * h], T.eqc[:, a:a + 128], T.WN[:, o:o + 8])
+                                                         for h in range(2) for a, o in ((128 * h, 16), (256, 8 * h))], True, True),
+           ["A1", "blk1", "eqc", "WN", "WNb"])
+        vp(lambda B: V.tensor_tensor(T.yc[:], B[:, 16:32], T.dum[:, 32:48], A.max), "yc%d" % t, ["dumc"], ["yc"])
+        lin("dcu", T.dcu[:], T.yc[:], -1.0, 2048.0, ["yc"], ["dcu"])
+        for j, c in enumerate(quads[:4 - ADDED]):
+            pairs = sorted((2 * c, 2 * c + 1), key=lambda b: b != k0 // 2)
+            for b in pairs:
+                tn = "d%d_%d" % (t, b)
+                t_(tn, lambda B, b=b: group([(B[:], T[sI][:], T.xg[:, 512 * b:512 * b + 512])] + [(B[:, o:o + 256], T[sI][:], zz) for o in (0, 256)],
+                                            True, True), [sI, Z, "xg_%d" % b])
+                sp(lambda B, b=b: act(T.ab[:, 512 * b:512 * b + 512], B[:], AF.Abs), tn, [], ["ab%d" % b])
+            for run in ([pairs] if j else [[b] for b in pairs]):
+                a, e = 512 * min(run), 512 * max(run) + 512
+                v(lambda a=a, e=e: ts(T.th[:, a:e], T.ab[:, a:e], 16.0, None, A.is_gt), ["ab%d" % b for b in run], ["th%d" % b for b in run])
+        lin("zq", T.zq[:, 0:256], zz, T[sv][:, 0:1], T[sv][:, 1:2], [Z, sv], ["zq"])
+        for nm, n, src in (("zqb", 256, "zq"), ("zqc", 512, "zqb")):
+            copy(nm, T.zq[:, n:2 * n], T.zq[:, 0:n], ["zq", src], n)
+        for j, c in enumerate(quads[4 - ADDED:]):
+            a, xs = 1024 * c, ["xg_%d" % (2 * c), "xg_%d" % (2 * c + 1)]
+            op("g", [lambda a=a: g.dma_start(T.xg[:, a:a + 1024], T.zq[:], accum_op=A.add)], ["zq", "zqb", "zqc"], ["dd%d" % j] + xs,
+               sem="dd%d" % j, cnt=16 * (t + 1))
+            v(lambda a=a: ts(T.th[:, a:a + 1024], T.xg[:, a:a + 1024], GRID, GRID, A.add, A.not_equal), xs, ["td", "th%d" % (2 * c), "th%d" % (2 * c + 1)])
+        for h in range(2):
+            tn, o = "cn%s%d" % ("ab"[h], t), 256 + 128 * h
+            for c in quads:
+                t_(tn, lambda B, c=c, o=o: [(B[:, o + k:o + 128:16], T.th[:, 256 * k + o - 256:256 * k + o - 128], T.blkb[:, 32:40], True, True)
+                                            for k in range(4 * c, 4 * c + 4)], ["th%d" % (2 * c), "th%d" % (2 * c + 1), "blkb"])
+            sp(lambda B, h=h, o=o: act(T.sg[:, 128 * h:128 * h + 128], B[:, o:o + 128], AF.Sign, bias=-8.5), tn, [], ["sg_%d" % h])
+        tn = "Pw%d" % t
+        t_(tn, lambda B: [(B[0:40, 256:512], T.blkb[:], T.th[:, 256 * k0:256 * k0 + 256], False, True)], ["th%d" % (k0 // 2), "blkb", "blkz", tn], ["sk", tn])
+        sp(lambda B: act(TW[0:40, 0:256], B[0:40, 256:512], AF.Sign, bias=bar, accum_out=T.acc[0:40, :]), tn, ["bar", "barb"], ["TW", "acc"])
+        copy("TWd", TW[0:8, 256:512], TW[0:8, 0:256], ["TW"], 256)
         if not last:
-            t_("S%d" % t, lambda B: [(B[:, 0:1], T.c32[32:40, :], T.acc[32:40, :], True, True, 256)], ["c32", "acc"])
-            if VBANKS:
-                vp(one, lambda B: ts(T.si[:], B[:, 0:1], -5.0, 1535.625, A.mult, A.add), "S%d" % t, [], ["si"])
-                vp(one, lambda B: ts(T.s0[:], T.si[:], 0.2, B[:, 0:1], A.mult, A.add), "S%d" % t, ["si"], ["s0"])
-                lin("sI", T[sI1][:], T.Ioff[:], 1.0, T.s0[:], 128, ["Ioff", "s0"], [sI1], relu=True)
-            else:
-                vp(one, lambda B: ts(T.si[:], B[:, 0:1], 0.25, 1535.625, A.mult, A.add), "S%d" % t, [], ["si"])
-                vp(one, lambda B: ts(T[lim1][:], T.si[:], -4.0, B[:, 0:1], A.mult, A.add), "S%d" % t, ["si"], [lim1])
-        t_("yw%d" % t, lambda B: [(B[:, c0:c0 + 16], T.I16[:], T[wW][:], c0 == 0, False, 64) for c0 in (0, 16)]
-           + [(B[:, 0:32], T.WB[0:40, 15 - b:143 - b], T[TW][0:40, b:512:16], False, b == 15, 64) for b in range(16)],
-           [wW, "I16", TW + "b", TW + "c", TW + "d", "WB"])
-        up = 0 if on_v("TWb") else 1
-        vp(one, lambda B: V.tensor_tensor(T.yw[:], B[:, 0:32], T.dum[:, 16 - 16 * up:48 - 16 * up], A.max), "yw%d" % t, ["dum"], ["yw"])
-        lin("dwu", T.dwu[:], T.yw[:, 16:32], -1.0, 2048.0 + up * BIG, 16, ["yw"], ["dwu"])
-        lin("dwl", T.dwl[:], T.yw[:, 0:16], -0.25, 511.625 + (up + 1) * BIG / 4, 16, ["yw"], ["dwl"])
-
-        def signed(B):
-            return [(B[:, o + 128 * h:o + 128 * h + 128], T.sg[:, 128 * h:128 * h + 128], T[m][:], 128) for o, m in ((0, "IBp"), (256, "IBn")) for h in range(2)]
-        parts("G", t, lambda B: [(B[:, 0:256], T[It][:], Kn, 256), (B[:, 256:512], T[It][:], T[Gn][:], 256), (B[:, 256:512], T.krow[32:33, :], T.ones[32:33, :], 256)],
-              [It, "Kn", Gn, "kB", "ones"],
-              lambda B: [(B[:, o + 128 * h:o + 128 * h + 128], T.At[:, 128 * h:128 * h + 128], T.I16[:], 128) for o in (0, 256) for h in range(2)]
-              + signed(B), ["At", "I16", "sg", "IBp", "IBn"])
-        lin("ga", T.ga[:], lambda B: B[:, 0:256], 1.0, -BIG, 256, [], ["ga"], "G%d" % t)
-        vp(dv(256), lambda B: V.tensor_tensor(T[Gn1][:], T.ga[:], B[:, 256:512], A.max), "G%d" % t, ["ga"], [Gn1])
-        if not last:
-            lin("Gu", T[Gu1][:], T[Gn1][:], -1.0, 2048.0, 256, [Gn1], [Gu1], how="half")
-        parts("N", t, lambda B: [(B[:, 0:256], T.I16[:], T.cw[:], 256), (B[:, 256:512], T.I16[:], T[Gn][:], 256)], ["I16", "cw", Gn], signed, ["sg", "IBp", "IBn"])
-        lin("cf", T.cf[:], lambda B: B[:], 1.0, -BIG, 512, [], ["cf"], "N%d" % t)
-        v(ds(256), lambda: V.tensor_tensor(T.CAN[:].indirect(T.dwl[:]), T.cf[:, 0:256], T.cf[:, 256:512], A.max), ["cf", "dwl"], ["CAN"])
-        xw = T.xg[:, k0:4096:16]
-        XG = ["xg_%d" % c for c in range(4)]
-        lin("r", T.r1[:], xw, 1.0, BIAS + 59.0, 256, XG, ["r1"], how="half", relu=True)
-        parts("R", t, lambda B: [(B[:, 256:512], T.Ihn[:], xw, 256), (B[:, 256:512], T.Ih[:], zz, 256), (B[:, 0:256], T.Ibn[:], T.r1[:], 256)],
-              XG + ["Ihn", "Ih", "Ibn", Z, "r1"],
-              lambda B: [(B[:, 256:512], T.E8[32:40, :], T[TW][32:40, 0:256], 256), (B[:, 0:256], T.RA[0:40, :], T[TW][0:40, 0:256], 256)],
-              ["E8", "RA", "RAb", TW + "b", TW + "c"])
-        lin("rf", T.rf[:], lambda B: B[:], 1.0, -512.25, 512, [], ["rf"], "R%d" % t, relu=True)
-        v(ds(256), lambda: V.tensor_tensor(T.X[:].indirect(T.dwu[:]), T.rf[:, 0:256], T.rf[:, 256:512], A.add), ["rf", "dwu"], XC)
+            tn = "S%d" % t
+            t_(tn, lambda B: [(B[:, 64:65], T.c32[0:40, :], T.acc[0:40, :], True, True)], ["c32", "c32b", "acc"])
+            lin("si", T.si[:], lambda B: B[:, 64:65], -5.0, 1535.625 + 5 * (0.97 - 307.2), [], ["si"], tn)
+            vp(lambda B: ts(T.s0[:], T.si[:], 0.2, B[:, 64:65], A.mult, A.add), tn, ["si"], ["s0"])
+            lin("sI", T[sI1][:], T.Ib[:], T.s0[:], 0.0, ["Ib", "s0"], [sI1])
+            lin("sv", T[sv1][:], T.cc[:], T.s0[:], 0.0, CC + ["s0"], [sv1])
+        t_("yw%d" % t, lambda B: group([(B[:, 32:64], T.I16[:], T[wW][:])]
+                                       + [(B[:, 32:64], T.WB[0:40, 15 - b:143 - b], TW[0:40, b:512:16]) for b in range(16)], True, True),
+           ["wU%d" % p, wW, "I16", "TW", "TWd", "WB", "WBb"])
+        vp(lambda B: V.tensor_tensor(T.yw[:], B[:, 32:64], T.dum[:, 0:32], A.max), "yw%d" % t, ["dum"], ["yw"])
+        lin("dwl", T.dwl[:], T.yw[:], -1.0, 2048.0 + 2 * BIG, ["yw"], ["dwl"])
+        for h in range(2):
+            tn, a, b = "G%s%d" % ("ab"[h], t), 128 * h, 128 * h + 128
+            t_(tn, lambda B, a=a, b=b: group([(B[:, 0:128], T[It][:], T.Kn[:, 16 + a:16 + b]), (B[:, 128:256], T[It][:], T[Gn][:, 16 + a:16 + b]),
+                                              (B[:, 128:256], T.krow[32:33, :], T.ones[32:33, 0:128]),
+                                              (B[:, 384:512], T.I16[:], T[Gn][:, 16 + a:16 + b])], True, False),
+               [It, "Kn", "%s_%d" % (Gn, h), "kB", "ones", "I16"], ["Ge_%d" % h])
+            t_(tn, lambda B, a=a, b=b: [(B[:, 256:384], T.I16[:], T.cw[:, a:b], False, False)], ["I16", "cw", "Ge_%d" % h], ["Ne_%d" % h])
+            t_(tn, lambda B, a=a, b=b: [(B[:, o:o + 128], T.At[:, a:b], T.I16[:], False, False) for o in (0, 128)], ["At", "I16", "Ge_%d" % h], ["Gt_%d" % h])
+            t_(tn, lambda B, a=a, b=b: [(B[:, 128 * j:128 * j + 128], T.sg[:, a:b], m[:], False, j == 3) for j, m in enumerate((T.IBp, T.IBn, T.IBn, T.IBp))],
+               ["sg_%d" % h, "IBp", "IBn", "Ne_%d" % h, "Gt_%d" % h], ["G_%d" % h])
+            lin("ga", T.ga[:, a:b], lambda B: B[:, 0:128], 1.0, -BIG, [], ["ga_%d" % h], tn)
+            vp(lambda B, a=a, b=b: V.tensor_tensor(T[Gn1][:, 16 + a:16 + b], T.ga[:, a:b], B[:, 128:256], A.max), tn, ["ga_%d" % h], ["%s_%d" % (Gn1, h)])
+            lin("cf", T.cf[:, 2 * a:2 * b], lambda B: B[:, 256:512], -1.0, 2048.0 - BIG, ["G_%d" % h], ["cf_%d" % h], "N%s%d" % ("ab"[h], t))
+            v(lambda h=h, a=a: V.tensor_tensor(T.CAN[:].indirect(T.dwl[:, 8 * h:8 * h + 8]), T.cf[:, 2 * a:2 * a + 128], T.cf[:, 2 * a + 128:2 * a + 256],
+                                               A.max), ["cf_%d" % h, "dwl"], ["CAN"])
+        xw, XG = T.xg[:, 256 * k0:256 * k0 + 256], "xg_%d" % (k0 // 2)
+        lin("r", T.r1[:], xw, 1.0, BIAS + 59.0, [XG], ["r1"], relu=True)
+        parts("R", t, lambda B: [(B[:, 256:512], T.Ihn[:], xw), (B[:, 256:512], T.Ih[:], zz), (B[:, 0:256], T.Ibn[:], T.r1[:])],
+              [XG, "Ihn", "Ih", "Ibn", Z, "r1"],
+              lambda B: [(B[:, 256:512], T.E8[32:40, :], TW[32:40, 0:256]), (B[:, 0:256], T.RA[0:40, :], TW[0:40, 0:256])], ["E8", "RA", "RAb", "TW"])
+        lin("rf", T.rf[:], lambda B: B[:], 1.0, -512.25, [], ["rf"], "R%d" % t, relu=True)
+        win, names, o = (T.XO, XOC, 32) if last else (T.X, XC, 0)
+        if last:
+            lin("rn", T.rf[:, 0:256], T.rf[:, 0:256], 1.0, -BIAS, ["rf"], ["rn", "rf"])
+        v(lambda: V.tensor_tensor(win[:].indirect(T.dwl[:, 16:32]), T.rf[:, 0:256], T.rf[:, 256:512], A.add), ["rf", "dwl"], ["X"] + names)
         for a in range(8):
-            v(ds(32), lambda a=a: V.tensor_tensor(T.X[:].indirect(T.dcu[:, 2 * a:2 * a + 2]), T.xc[:, 32 * a:32 * a + 32], T.c160[:, 0:32], A.add),
-              ["xc", "dcu", "c160"], ["cut"] + XC)
+            v(lambda a=a: V.tensor_tensor(win[:].indirect(T.dcu[:, 2 * a:2 * a + 2]), T.xc[:, 32 * a:32 * a + 32], T.c160[:, o:o + 32], A.add),
+              ["xc", "dcu", "c160", "c160n"], ["cut"] + names)
         if not last:
             now[0] = t + 1
             firsts(t + 1)
@@ -421,17 +433,13 @@ def rank_program(g, core, T, topo):
     now[0] = None
 
     def store(name, out, src, R):
-        op("y", 0.1, [lambda: Y.dma_start(out, src)], R, ["y" + name], lat=3.0, sem="st_" + name, cnt=16)
+        op("y", [lambda: Y.dma_start(out, src)], R, ["y" + name], sem="st_" + name, cnt=16)
 
-    lin("", T.lo[:], T.CAN[:, 0:1024], -1.0, 2048.0, 1024, ["CAN"], ["lo"], e="s")
-    store("ol", T.yl[:], T.lo[:], ["lo"])
-    lin("", T.go[:], T["Gn%d" % (NT % 2)][:], -1.0, 2048.0, 256, ["Gn%d" % (NT % 2)], ["go"], e="s")
+    store("ox", T.yx[:], T.XO[:, 0:4096], XOC)
+    lin("", T.go[:], T["Gn%d" % (NT % 2)][:, 16:272], -1.0, 2048.0, ["Gn%d_%d" % (NT % 2, h) for h in range(2)], ["go"], e="s")
     store("og", T.yg[:], T.go[:], ["go"])
-    for c in range(4):
-        a, b = 1024 * c, 1024 * c + 1024
-        lin("", T.sc[:, a:b], T.X[:, a:b], 1.0, -BIAS, 1024, ["X%d" % c], ["sc%d" % c], how="half", e="vvvs"[c])
-        store("o%d" % c, T.yx[:, a:b], T.sc[:, a:b], ["sc%d" % c])
-    emit(g, T, ops, schedule(ops))
+    store("ol", T.yl[:], T.CAN[:, 0:1024], ["CAN"])
+    return ops
 
 
 def depend(ops):
@@ -458,113 +466,69 @@ def depend(ops):
         o["d"], o["s"] = d, []
         for j in d:
             ops[j]["s"].append(o["i"])
-        o["n"] = "".join(c for c in (o["W"] or [o["tile"]])[0] if c.isalpha()) + "_" + o["e"]
+        o["n"] = "".join(c for c in (o["W"] or [o["tile"]])[0] if c.isalpha()) + "_" + (o["e"] if o["t"] is not None else o["e"].upper())
+        kind = "".join(c for c in o["tile"] or "" if c.isalpha())
+        o["bank"] = SHARE[kind] + o["tile"][len(kind):] if kind in SHARE and kind != o["tile"] else o["tile"]
 
 
 def dues(ops, phase):
-    n = len(ops)
-    due, seen = [None] * n, {}
-    for o in ops:
-        if o["t"] is not None:
-            key = (o["t"], o["n"])
-            o["k"] = seen.get(key, 0)
-            seen[key] = o["k"] + 1
-            if o["t"] == NT - 1 and o["n"] in LAST:
-                kind, k = LAST[o["n"]][o["k"]]
-                due[o["i"]] = PERIOD * o["t"] + phase[kind][k] + 0.001
-                continue
-            ph = phase[o["n"]]
-            due[o["i"]] = PERIOD * o["t"] + ph[min(o["k"], len(ph) - 1)]
-            if o["e"] == "g":
-                due[o["i"]] = max(due[o["i"]], AHEAD + 1.0 if o["t"] else -1.0)
+    due, seen = [], {}
     first = min(o["i"] for o in ops if o["t"] is not None)
-    for o in ops[first:]:
-        if o["t"] is None:
-            due[o["i"]] = max(due[j] for j in o["d"] if j >= first) + 0.001
-    for o in ops[first - 1::-1]:
-        due[o["i"]] = min(due[j] for j in o["s"]) - o["c"] - SYNC if o["e"] != "y" else o["i"] - 1000.0
-    return due, first
+    for o in ops:
+        t, name = o["t"], o["n"]
+        o["k"] = k = seen.get((t, name), 0)
+        seen[(t, name)] = k + 1
+        o["by"] = 2 if (t == 0 or o["i"] < first) and k in phase[2].get(name, ()) else 1 if t == NT - 1 and k in phase[1].get(name, ()) else 0
+        if t is None and o["by"] == 0:
+            due.append(o["i"] - 1000.0)
+        else:
+            due.append(max(PERIOD * (t or 0) + phase[o["by"]][name][k], AHEAD if t else -PERIOD))
+    return due
 
 
-def place(ops, due, first):
-    n = len(ops)
+def place(ops, due):
     users = {}
     for o in ops:
         if o["tile"]:
-            users.setdefault(o["tile"], []).append(o["i"])
+            users.setdefault(o["bank"], []).append(o["i"])
     left = {k: len(u) for k, u in users.items()}
-    bank, extra = {}, {}
+    bank, extra, last = {}, {}, {}
     free = {k: [] for k in range(8)}
     need = [len(o["d"]) for o in ops]
-    rt, fin, t0 = [0.0] * n, [0.0] * n, [0.0] * n
-    ready = sorted((due[i], i) for i in range(n) if need[i] == 0)
-    et = {"v": 0.0, "s": 0.0, "t": 0.0, "g": 0.0, "y": 0.0, "x": 0.0}
-    order, early, begun = [], first, False
+    ready = sorted((due[i], i) for i in range(len(ops)) if need[i] == 0)
+    order = []
     while ready:
         p = 0
-        while ops[ready[p][1]]["tile"] and ops[ready[p][1]]["tile"] not in bank and not free:
+        while ops[ready[p][1]]["tile"] and ops[ready[p][1]]["bank"] not in bank and not free:
             p += 1
             if p == len(ready):
                 raise ValueError("no bank for any ready op")
-        i = ready[p][1]
-        if not begun:
-            can = [(max(rt[j], et[ops[j]["e"]]), q) for q, (_, j) in enumerate(ready) if q == p or
-                   (j < first or due[j] < AHEAD) and (not ops[j]["tile"] or ops[j]["tile"] in bank or len(free) > 3)]
-            p = min((ops[ready[q][1]]["n"] != "sc_v", q) for x, q in can if x <= min(can)[0] + SOON)[1]
-            i = ready[p][1]
-            begun = ops[i]["n"] == "sc_v"
-        elif early:
-            start = max(rt[i], et[ops[i]["e"]])
-            for q, (_, j) in enumerate(ready):
-                if j < first and j != i and (not ops[j]["tile"] or ops[j]["tile"] in bank) and max(rt[j], et[ops[j]["e"]]) + ops[j]["c"] <= start:
-                    p, i = q, j
-                    break
-        e = ops[i]["e"]
-        del ready[p]
-        o = ops[i]
-        early -= i < first
-        st = rt[i] if e == "x" else max(rt[i], et[e])
-        tl = o["tile"]
+        i = ready.pop(p)[1]
+        tl = ops[i]["bank"]
         if tl:
             if tl not in bank:
-                a, bk = min((max([fin[u] for u in us] or [0.0]), k) for k, us in free.items())
-                st = max(st, a + SYNC)
-                bank[tl] = bk
-                extra[i] = free.pop(bk)
+                bank[tl] = list(free)[0]
+                extra[i] = free.pop(bank[tl])
+            elif ops[last[tl]]["e"] != ops[i]["e"]:
+                extra[i] = [last[tl]]
+            last[tl] = i
             left[tl] -= 1
             if left[tl] == 0:
                 free[bank[tl]] = users[tl]
-        et[e] = st + o["c"]
-        fin[i] = f = st + o["c"] + o["lat"]
-        t0[i] = st
         order.append(i)
-        for j in o["s"]:
+        for j in ops[i]["s"]:
             need[j] -= 1
-            if f + SYNC > rt[j]:
-                rt[j] = f + SYNC
             if need[j] == 0:
                 ready.append((due[j], j))
                 ready.sort()
-    if len(order) != n:
-        raise ValueError("schedule stuck")
-    return order, t0, fin, bank, extra
+    return order, bank, extra
 
 
-def schedule(ops):
-    depend(ops)
-    order, t0, fin, bank, extra = place(ops, *dues(ops, PHASE))
-    for o in ops:
-        o["t0"] = t0[o["i"]]
-        o["d"] = set(o["d"]) | set(extra.get(o["i"], ()))
-        if o["tile"]:
-            o["b"] = bank[o["tile"]]
-    return order
-
-
-def emit(g, T, ops, order):
+def emit(g, T, ops, order, bank, extra):
     Q = {"v": g.vector, "s": g.scalar, "t": g.tensor, "g": g, "y": g.sync}
     known = {e: {} for e in Q}
     count, done = {}, {}
+    at = {i: p for p, i in enumerate(order)}
     for i in order:
         o = ops[i]
         e = o["e"]
@@ -572,7 +536,7 @@ def emit(g, T, ops, order):
             done[i] = (o["sem"], o["cnt"], {})
             continue
         kn = known[e]
-        for _, j in sorted(((ops[j]["t0"], j) for j in o["d"]), reverse=True):
+        for j in sorted(set(o["d"]) | set(extra.get(i, ())), key=lambda j: -at[j]):
             sm, c, snap = done[j]
             if c > kn.get(sm, 0):
                 Q[e].wait_ge(T.sem[sm], c)
@@ -583,8 +547,7 @@ def emit(g, T, ops, order):
         if e == "g" and count.get("qg", 0) > kn.get("qg", 0):
             kn["qg"] = count["qg"]
             g.wait_ge(T.sem["qg"], kn["qg"])
-        calls = o["f"](T["ps%d" % o["b"]]) if o["tile"] else o["f"]
-        for f in calls:
+        for f in (o["f"](T["ps%d" % bank[o["bank"]]]) if o["tile"] else o["f"]):
             r = f()
             if o["sem"] is None:
                 count["q" + e] = count.get("q" + e, 0) + 1

from concourse.mybir import AluOpType, AxisListType, ActivationFunctionType

A = AluOpType
AF = ActivationFunctionType
NT = 8
BIAS = 160.0
MID = BIAS + 31.5
XW = 4464
CW = 1392
BIG = 8192.0
GRID = 402653184.0
ADDED = 2
EQN = [256 - 16 * a for a in range(16)]
EQO = [sum(EQN[:a]) for a in range(17)]

F4, BF, HF, I4, U2 = "float32", "bfloat16", "float16", "int32", "uint16"
SCRATCH = {}
for _n, _s, _d in (
        ("X", XW, BF), ("XO", XW, BF), ("CAN", CW, F4), ("cin", 1024, I4), ("tin", 256, I4), ("vin", 256, I4), ("zin", 256, BF),
        ("xg", 4096, BF), ("ab", 4096, BF), ("th", 4096, BF), ("sc", 4096, BF), ("go", 256, F4), ("zq", 1024, BF),
        ("Kn", 272, HF), ("Ku", 256, U2), ("eqw", EQO[16], BF), ("eqc", 384, BF), ("repw", 256, HF),
        ("uW", 16, F4), ("A1", 256, HF), ("At", 256, HF), ("TC", 256, HF), ("TW", 512, HF), ("yw", 32, F4), ("yc", 16, F4), ("sco", 256, I4),
        ("q2", 24, I4), ("Lc", 16, F4), ("Lx", 32, HF), ("cu", 16, U2), ("vl", 16, U2), ("dwl", 32, U2), ("dcu", 16, U2),
        ("xc", 256, BF), ("r1", 256, BF), ("rf", 512, BF), ("cw", 256, HF), ("cf", 512, F4), ("ga", 256, HF), ("sg", 256, BF),
        ("acc", 1, F4), ("si", 1, HF), ("s0", 1, F4),
        ("Z", 1024 * NT, BF), ("ZS", 256 * NT, BF),
        ("pci", 4, I4), ("col", 3, F4), ("k256", 256, BF), ("I16", 128, HF), ("In16", 128, HF), ("Ib", 128, BF), ("Ibn", 128, BF), ("Ih", 128, BF),
        ("Ihn", 128, BF), ("IBp", 128, BF), ("IBn", 128, BF), ("blk1", 8, HF), ("lx", 2, U2), ("blkb", 40, BF), ("blkS", 8, BF), ("WD", 8, BF),
        ("WO", 8, BF), ("WN", 24, BF), ("tri", 384, HF), ("cc", 4, F4), ("thr", 256, BF), ("BLK", 384, HF), ("dmask", 256, HF), ("WB", 144, HF),
        ("E8", 128, HF), ("RA", 128, HF), ("dum", 48, F4), ("resetv", 256, BF), ("c160", 64, BF), ("krow", 128, HF), ("ones", 256, HF),
        ("neg", 144, HF), ("c32", 128, F4), ("zl", 16, U2), ("tmp", 128, HF)):
    SCRATCH[_n] = ("sbuf", [128, _s], _d)
for _k in range(2):
    for _n, _s, _d in (("Gn", 272, HF), ("Gu", 256, U2), ("sI", 128, BF), ("SEL", 128, HF), ("sv", 4, F4), ("wW", 32, HF), ("It", 128, HF),
                       ("cwl", 16, U2)):
        SCRATCH["%s%d" % (_n, _k)] = ("sbuf", [128, _s], _d)
for _k in range(8):
    SCRATCH["ps%d" % _k] = ("psum", [128, 512], F4)

LOADS = "cut trail x0 x1 x2 canal x3 z".split()
SEMAPHORES = (["qv", "qs", "qt", "qg"] + ["ld_" + n for n in LOADS] + ["st_ox", "st_ol", "st_og", "add0", "add1"]
              + ["dd%d" % k for k in range(ADDED)] + ["arr%d" % k for k in range(1, NT)] + ["snt%d" % k for k in range(1, NT)])

ORDER = """
sc_v0 key_t0 Pw_t1 Ge_t0 Pw_t2 xg_s0 sc_v1 zqb_g Pw_t3 zqc_g Pw_t4 key_t1 d_t0 d_t1 key_t2 dd_g0 dd_g1 xg_s1 XO_g ab_s0 ab_s1 d_t2 ab_s2 r_s
sc_v2 sc_v3 key_t3 d_t3 key_t4 sc_v4 th_v0 key_t5 sco_v ZSe_t sk_t Re_t TW_s q_v Lc_s Lx_s R_t De_t th_v1 ab_s3 A_v cW_t TWd_g At_g It_g++
td_v0 th_v2 cu_s cw_s cna_t0 D_t eqc_v xc_s rf_s yw_t cnb_t0 cnb_t1 cnb_t2 ZS_t yw_v dwl_s td_v1 yc_t yc_v cna_t1 cna_t2 cnb_t3 cna_t3 zs_s
X_v Gt_t0 way_g sg_s0 Ne_t0 S_t sg_s1 si_s Gt_t1 Ne_t1 Az_g+ dcu_s G_t0 ga_s0 G_t1 s_v cut_v0 Gn_v0 Gw_t0+ ga_s1 cut_v1 Gn_v1 rw_t+ SEL_g+++
Gw_t1+ cut_v2 sI_s cf_s0 vl_s sv_v cut_v3 CAN_v0 cf_s1 repw_s+ Pw_t0+ cut_v4 CAN_v1 wU_s+ cut_v5 uW_s+ Kn_s+ Kt_t0+ cwl_v+ Kt_t1+ cut_v6
eqw_v7+ eqw_v12+ cut_v7 eqw_v3+ eqw_v14+ eqw_v10+ eqw_v8+ eqw_v13+ eqw_v0+ eqw_v4+ eqw_v5+ eqw_v9+ eqw_v6+ eqw_v11+ eqw_v15+ Gu_s+ eqw_v1+
wW_s+ Ku_v+ eqw_v2+ xg_s3+ Z_x Dt_t+ Ge_t1+ zq_s+ xg_s2+ Zb_g+
""".split()
LAST = """
Ge_t Pw_t1 Ne_t0 xg_s1 key_t0 Ne_t1 zqb_g Pw_t2 Pw_t3 xg_s0 zqc_g Pw_t4 key_t1 d_t2 ab_s2 dd_g0 dd_g1 d_t3 key_t2 d_t0 d_t1 r_s ab_s0 th_v0
ab_s1 key_t3 ab_s3 key_t4 key_t5 sco_v th_v1 q_v sk_t TW_s Re_t R_t Lx_s Lc_s TWd_g At_g rf_s XO_s De_t yw_t th_v2 A_v D_t cnb_t1 cnb_t0 td_v0
yw_v rn_v cna_t1 cnb_t2 cW_t cna_t0 eqc_v cna_t2 Gt_t0 dwl_s X_v cu_s Gt_t1 yc_t yc_v xc_s td_v1 dcu_s cut_v0 cna_t3 cnb_t3 sg_s1 sg_s0 G_t0
ga_s0 G_t1 ga_s1 cf_s0 cut_v1 cut_v2 cut_v3 add_g0+ cut_v4 cut_v5 XO_v+ cut_v6 cut_v7 Gn_v1 CAN_v0 Gn_v0 cf_s1 CAN_v1 cw_s+ sc_v0+ add_g1+
sc_v1+ sc_v2+ sc_v3+ sc_v4+
""".split()
FIRST = """
ones_V WN_V cn_V Knp_V Gnp_V0 Gnp_V1 dum_G cc_V1 cc_V3 I_G At_V neg_V tmp_G0 WB_V pci_G blk_G WB_G barb_V k_G bar_G SEL_G tmp_G1 triz_V RA_G
cb_S p_V0 k_V kB_V c_V TCb_V TWd_V Ib_S In_S Ibn_S IBp_S Ih_S sI_S blkb_S WNb_S cc_V2 blkz_V Ihn_S cW_T cc_V0 lxa_V Gn_S WN_S0 blkS_S sv_S
Gw_T0 p_V1 pk_V xc_V Gw_T1 rw_T lxb_V r_V zl_V dmask_V thr_V X_V0 yc_V vl_V wcol_V resetv_V X_V1 IBn_S WO_S WN_S1 X_S wU_S repw_S WD_V cwl_V
X_V2 wW_S uW_S eqw_V1 eqw_V3 eqw_V5 eqw_V6 eqw_V7 eqw_V8 eqw_V13 Kn_s Gu_S Pw_T0 Kt_t0 Kt_t1 eqw_V4 eqw_V14 eqw_V9 eqw_V10 Z_V eqw_V12 eqw_V11
eqw_V2 CAN_S xg_s3 eqw_V0 Ku_v BLKa_G eqw_V15 It_g Ge_t0 Ge_t1 tmp_G2 c_G BLKb_G tmp_G3 BLKc_G tmp_G4 Pw_T1 key_t0 zq_s xg_s2 Zb_g zqb_g zqc_g
sc_v0 tri_V Pw_T2 Pw_T3 Pw_T4 Dt_t E_S xg_s0 key_t1 dd_g0 dd_g1 dumc_G qp_G xg_s1 sc_v1 d_t0 key_t2 d_t1 RAb_S WBb_G
""".split()
PERIOD, AHEAD = 15.5, 2.0
SCORES = ((4, 1), (4, 2), (4, 2), (2, 2), (2, 2))
UNBIAS = "aavs"
SHARE = {"cna": "n", "cnb": "n", "cW": "c", "yc": "c", "yw": "c", "S": "c", "Ga": "a", "Na": "a", "Gb": "b", "Nb": "b"}


def phases(words):
    ph = {}
    for p, w in enumerate(words):
        name = w.rstrip("+-")
        kind = name.rstrip("0123456789")
        ph.setdefault(kind, {})[int(name[len(kind):] or 0)] = PERIOD * (p / len(words) - w.count("+") + w.count("-"))
    return ph


def opening(words):
    return {k: {j: x * (1 + AHEAD / PERIOD) - PERIOD for j, x in d.items()} for k, d in phases(words).items()}


PHASE = [phases(ORDER), phases(LAST), opening(FIRST)]


def rank_program(g, core, T, topo):
    if T.rank_of(core) is None:
        return
    ops = calls(g, core, T, topo)
    depend(ops)
    order, bank, extra = place(ops, dues(ops, PHASE))
    emit(g, T, ops, order, bank, extra)


def calls(g, core, T, topo):
    rank = T.rank_of(core)
    V, S, PE, Y = g.vector, g.scalar, g.tensor, g.sync
    mm, act = PE.matmul, S.activation
    ops, now = [], [None]

    def op(eng, calls, R=(), W=(), tile=None, sem=None, cnt=0):
        ops.append({"e": eng, "f": calls, "R": list(R), "W": list(W), "tile": tile, "sem": sem, "cnt": cnt, "i": len(ops), "t": now[0]})

    def v(f, R, W): op("v", [f], R, W)
    def s(f, R, W): op("s", [f], R, W)
    def vp(f, tile, R, W): op("v", lambda B: [lambda: f(B)], R, W, tile=tile)
    def sp(f, tile, R, W): op("s", lambda B: [lambda: f(B)], R, W, tile=tile)

    def t_(tile, prods, R, W=()):
        op("t", lambda B: [lambda p=p: mm(*p) for p in prods(B)], R, W, tile=tile)

    def group(ps, start, stop):
        return [p + (start and j == 0, stop and j == len(ps) - 1) for j, p in enumerate(ps)]

    def parts(name, t, early, R1, late, R2, start=True):
        t_("%s%d" % (name, t), lambda B: group(early(B), start, False), R1, [name + "e"])
        t_("%s%d" % (name, t), lambda B: group(late(B), False, True), R2 + [name + "e"])

    def ts(out, i0, s1, s2, o0, o1=None):
        if o1 is None:
            return V.tensor_scalar(out, i0, s1, None, o0)
        return V.tensor_scalar(out, i0, s1, s2, o0, o1)

    def pick(name, out, src, R, pat, cmp, base, cm, other=0.0):
        op("g", [lambda: g.affine_select(out, src, pat, cmp, other, base, cm)], R, [name])

    def copy(name, out, src, R, n):
        pick(name, out, src, R, [[0, n]], A.is_ge, 0, 0)

    def lin(kind, out, src, scale, bias, R, W, tile=None, relu=False, e=None):
        own = [x for x in "vs" if now[0] == NT - 1 and kind + "_" + x in PHASE[1]]
        e = e or (own or [x for x in "vs" if kind + "_" + x in PHASE[0]] or ["s"])[0]

        def on_vector(x): return ts(out, x, bias, 0.0, A.add, A.max) if relu else ts(out, x, scale, bias, A.mult, A.add)
        def on_scalar(x): return act(out, x, AF.Relu if relu else AF.Identity, bias=bias, scale=scale)
        f = on_vector if e == "v" else on_scalar
        op(e, (lambda B: [lambda: f(src(B))]) if tile else [lambda: f(src)], R, W, tile=tile)

    XC = ["X0", "X1", "X2", "X3"]
    XOC = ["XO0", "XO1", "XO2", "XO3"]
    what = {"cut": (T.vin[0:8, :], T.cut[:], "vin"), "trail": (T.tin[:], T.trail[:], "tin"), "canal": (T.cin[:], T.canal[:], "cin"),
            "z": (T.zin[:], T.z[:], "zin")}
    for q in range(4):
        what["x%d" % q] = (T.X[:, 1024 * q:1024 * q + 1024], T.x[:, 1024 * q:1024 * q + 1024], XC[q])
    for name in LOADS:
        op("y", [lambda w=what[name]: Y.dma_start(w[0], w[1])], [], [what[name][2]], sem="ld_" + name, cnt=16)

    def iota(name, out, pat, base, cm, f=True):
        kw = {"allow_small_or_imprecise_dtypes": True} if f else {}
        op("g", [lambda: g.iota(out, pat, base, cm, **kw)], [], [name])

    def fill(name, ap, val):
        v(lambda: V.memset(ap, val), [], [name])

    def scaled(name, out, src, R, val):
        s(lambda: act(out, src, AF.Identity, bias=0.0, scale=val), R, [name])

    def between(name, out, n, pat, lo, hi):
        pick("tmp", T.tmp[:, 0:n], T.ones[:, 0:n], ["ones"], pat, A.is_ge, -lo, 1)
        pick(name, out, T.tmp[:, 0:n], ["tmp"], [[-a, b] for a, b in pat], A.is_ge, hi, -1)

    fill("ones", T.ones[:], 1.0)
    fill("neg", T.neg[0:40, :], -BIG)
    fill("c160", T.c160[:, 0:32], BIAS)
    fill("c160n", T.c160[:, 32:64], -BIAS)
    fill("At", T.At[:], 0.0)
    fill("WB", T.WB[0:32, :], 0.0)
    for name, p0 in (("WB", 0), ("WBb", 32)):
        pick(name, T.WB[p0:p0 + 8, :], T.neg[p0:p0 + 8, :], ["neg"], [[1, 144]], A.is_equal, -15, -16)
    pick("I16", T.I16[:], T.ones[:, 0:128], ["ones"], [[-1, 128]], A.is_equal, 0, 1)
    for name, val in (("Ib", 1.0), ("Ibn", -1.0), ("In16", -1.0), ("IBn", -BIG), ("IBp", BIG), ("Ih", 0.5), ("Ihn", -0.5), ("sI0", 0.97)):
        scaled(name, T[name][:], T.I16[:], ["I16"], val)
    between("blk1", T.blk1[:], 8, [[-16, 8]], 0, 15)
    fill("blkz", T.blkb[:, 0:32], 0.0)
    for name, out, val in (("blkb", T.blkb[:, 32:40], 1.0), ("blkS", T.blkS[:], 4096.0), ("WO", T.WO[:], 4.0)):
        scaled(name, out, T.blk1[:], ["blk1"], val)
    between("BLKa", T.BLK[:, 0:128], 128, [[-16, 8], [0, 16]], 0, 15)
    between("BLKb", T.BLK[:, 128:256], 128, [[-32, 4], [-200, 2], [0, 16]], 16, 31)
    between("BLKc", T.BLK[:, 256:384], 128, [[-32, 4], [200, 2], [0, 16]], 200, 215)
    fill("WN", T.WN[:, 0:16], 0.0)
    s(lambda: act(T.WN[:, 1:8:2], T.blk1[:, 0:8:2], AF.Copy, scale=-BIG), ["blk1"], ["WN"])
    s(lambda: act(T.WN[:, 8:16:2], T.blk1[:, 1:8:2], AF.Copy, scale=-BIG), ["blk1"], ["WN"])
    scaled("WNb", T.WN[:, 16:24], T.blk1[:], ["blk1"], -BIG)
    pick("tmp", T.tmp[32:40, :], T.ones[32:40, 0:128], ["ones"], [[-1, 8], [0, 16]], A.is_equal, 0, 1)
    scaled("E8", T.E8[32:40, :], T.tmp[32:40, :], ["tmp"], -512.0)
    pick("RA", T.RA[0:32, :], T.At[0:32, 0:128], ["At"], [[0, 128]], A.not_equal, -8, 1, BIAS + 63.25)
    scaled("RAb", T.RA[32:40, :], T.E8[32:40, :], ["E8"], -1.0)
    iota("dum", T.dum[:, 0:32], [[-3072, 2], [-16, 16]], 2 * int(BIG) + 1024, -1)
    iota("dumc", T.dum[:, 32:48], [[-16, 16]], -2048, -1)
    iota("pci", T.pci[:, 0:1], [[0, 1]], 0, 1, False)
    iota("k256", T.k256[:], [[0, 16], [1, 16]], 0, 0)
    pk, wcol, bar = T.col[:, 0:1], T.col[:, 1:2], T.col[0:40, 2:3]
    v(lambda: ts(T.pci[:, 1:2], T.pci[:, 0:1], 15, None, A.bitwise_and), ["pci"], ["p15"])
    v(lambda: V.tensor_copy(pk, T.pci[:, 1:2]), ["p15"], ["pk"])
    v(lambda: ts(T.dmask[:], T.k256[:], pk, None, A.is_equal), ["k256", "pk"], ["dmask"])
    fill("triz", T.tri[:, 256:384], 0.0)
    v(lambda: ts(T.tri[:, 0:256], T.k256[:], pk, BIG, A.is_le, A.mult), ["k256", "pk"], ["tri"])
    v(lambda: V.tensor_copy(T.zl[:], T.k256[:, 0:16]), ["k256"], ["zl"])
    v(lambda: ts(T.pci[:, 2:3], T.pci[:, 0:1], 1, 8, A.arith_shift_right, A.bitwise_and), ["pci"], ["p8"])
    v(lambda: V.tensor_copy(T.lx[:, 0:1], T.pci[:, 1:2]), ["p15"], ["lxa"])
    v(lambda: ts(T.lx[:, 1:2], T.pci[:, 2:3], pk, None, A.add), ["p8", "pk"], ["lxb"])
    iota("q2p", T.q2[:, 16:24], [[0, 8]], 0, 0, False)
    v(lambda: ts(T.r1[:], T.k256[:], 0.0, 0.5, A.not_equal, A.mult), ["k256"], ["r1"])
    v(lambda: ts(T.xc[:], T.k256[:], 0.0, -2.5, A.is_equal, A.mult), ["k256"], ["xc"])
    v(lambda: V.tensor_tensor_scan(T.thr[:], T.r1[:], T.xc[:], 0.0, A.mult, A.add), ["r1", "xc"], ["thr"])
    v(lambda: ts(T.resetv[:], T.xc[:], 8.0e6, None, A.mult), ["xc"], ["resetv"])
    v(lambda: V.tensor_tensor(T.yc[:], T.thr[:, 0:16], T.dmask[:, 0:16], A.mult), ["thr", "dmask"], ["yc"])
    v(lambda: V.tensor_reduce(wcol, T.yc[:], AxisListType.X, A.add), ["yc"], ["wcol"])
    v(lambda: ts(T.WD[:], T.blk1[:], wcol, -0.4, A.mult, A.mult), ["blk1", "wcol"], ["WD"])
    fill("k2047", T.krow[0:1, :], 2047.0)
    pick("bar", T.col[0:32, 2:3], T.ones[0:32, 0:1], ["ones"], [[0, 1]], A.is_ge, -8, 1)
    fill("barb", T.col[32:40, 2:3], -8.5)
    pick("c32", T.c32[0:32, :], T.At[0:32, 0:128], ["At"], [[0, 128]], A.not_equal, -8, 1, (0.97 - 307.2) / 256)
    scaled("c32b", T.c32[32:40, :], T.ones[32:40, 0:128], ["ones"], -0.025)
    fill("kB", T.krow[32:33, :], -BIG)
    for name, rows in (("Knp", T.Kn), ("Gnp0", T.Gn0), ("Gnp1", T.Gn1)):
        fill(name, rows[:, 0:16], 0.0)
    CC = ["cc%d" % j for j in range(4)]
    for j, val in enumerate((1.0, -MID, -1.0, MID)):
        fill(CC[j], T.cc[:, j:j + 1], val)
    scaled("sv0", T.sv0[:], T.cc[:], CC, 0.97)
    fill("TWd", T.TW[0:40, 256:512], -1.0)

    lin("", T.TC[0:8, :], T.vin[0:8, :], -1.0, 2048.0, ["vin"], ["TCb"], e="v")
    lin("", T.Gn0[:, 16:272], T.tin[:], -1.0, 2048.0, ["tin"], ["Gn0_0", "Gn0_1"], e="s")
    lin("", T.Z[:, 0:256], T.zin[:], 1.0, BIAS, ["zin"], ["Z0"], e="v")
    lin("", T.CAN[:, 0:1024], T.cin[:], 1.0, 0.0, ["cin"], ["CAN"], e="s")
    for q in range(4):
        lin("", T.X[:, 1024 * q:1024 * q + 1024], T.X[:, 1024 * q:1024 * q + 1024], 1.0, BIAS, [XC[q]], [XC[q]], e="svvv"[q])

    def turned(B, rows, blocks):
        return ([(B[u:u + 32, a:256:16], rows[u:u + 32, 16 * a:16 * a + 32], T.I16[u:u + 32, u + 16:u + 32], True, True)
                 for a in blocks for u in (0, 32, 64, 96)]
                + [(B[u:u + 16, a:256:16], rows[u:u + 32, 16 * a + 16:16 * a + 32], T.I16[u:u + 32, u:u + 16], True, True)
                   for a in blocks for u in (0, 32, 64, 96)])

    def firsts(t):
        k0 = (t + 12) % 16
        wW, wU, cwl, SEL, Gn, Gu = ["%s%d" % (n, t % 2) for n in ("wW", "wU", "cwl", "SEL", "Gn", "Gu")]
        pick(SEL, T[SEL][:], T.ones[:, 0:128], ["ones"], [[-16, 8], [0, 16]], A.is_equal, -k0, 1)
        t_("rw%d" % t, lambda B: [(B[:, 0:256], T[SEL][:], T[Gn][:, 16:272], True, True)], [Gn + "_0", Gn + "_1", SEL])
        tn = "Gw%d" % t
        for h in range(2):
            t_(tn, lambda B, h=h: turned(B, T[Gn], range(8 * h, 8 * h + 8)), [Gn + "_0", "%s_%d" % (Gn, h), "Gnp%d" % (t % 2), "I16"])
        lin("repw", T.repw[:], lambda B: B[:, 0:256], 0.25, 1536.375, [], ["repw"], "rw%d" % t)
        lin("wU", T[wW][:, 0:16], lambda B: B[:, 16 * k0:16 * k0 + 16], 0.25, 1536.375, [], [wU], tn)
        lin("uW", T.uW[:], T[wW][:, 0:16], 1.0, 0.0, [wU], ["uW"])
        lin("Gu", T[Gu][:], lambda B: B[:, 0:256], -1.0, 2048.0, [], [Gu], tn)
        lin("wW", T[wW][:, 16:32], lambda B: B[:, 16 * k0:16 * k0 + 16], 1.0, 0.0, [], [wW], tn)
        lin("cwl", T[cwl][:], T[wW][:, 0:16], -1.0, 2048.0, [wU], [cwl])
        tn = "Pw%d" % t
        t_(tn, lambda B: [(B[0:40, 256:512], T.Ib[0:8, 0:40], T.thr[0:8, :], True, False)], ["Ib", "thr", "repw"], [tn])
        for blocks in (range(0, 3), range(3, 7), range(7, 11), range(11, 16)):
            for a in blocks:
                v(lambda a=a: ts(T.eqw[:, EQO[a]:EQO[a + 1]], T.repw[:, 16 * a:256], T.uW[:, a:a + 1], None, A.is_equal), ["repw", "uW"], ["eqw_%d" % a])

            def sums(B, blocks=blocks):
                r = []
                for a in blocks:
                    r.append((B[0:8, 256 + 16 * a:272 + 16 * a], T.WD[:], T.eqw[:, EQO[a]:EQO[a] + 16], False, False))
                    if a < 15:
                        r.append((B[0:8, 272 + 16 * a:512], T.WO[:], T.eqw[:, EQO[a] + 16:EQO[a + 1]], False, False))
                return r
            t_(tn, sums, ["eqw_%d" % a for a in blocks] + ["WD", "WO", tn], [tn])

    t_("cW", lambda B: [(B[:, 0:16], T.WB[0:8, 15 - b:143 - b], T.TC[0:8, b:256:16], b == 0, b == 15) for b in range(16)], ["TCb", "WB"])
    vp(lambda B: ts(T.vl[:], B[:, 0:16], 0.25 / BIG, 511.625, A.mult, A.add), "cW", [], ["vl"])
    firsts(0)

    def step(t):
        p, q = t % 2, 1 - t % 2
        last = t == NT - 1
        k0 = (t + 12) % 16
        Z = "Z%d" % t
        Gn, Gu, sI, wW, cwl, It, sv = ["%s%d" % (n, p) for n in ("Gn", "Gu", "sI", "wW", "cwl", "It", "sv")]
        Gn1, sI1, sv1 = ["%s%d" % (n, q) for n in ("Gn", "sI", "sv")]
        z0 = 1024 * t
        zz = T.Z[:, z0:z0 + 256]
        TW = T.TW
        can, CAN = (T.CAN[:, 0:1024], "CAN") if t else (T.cin[:], "cin")
        lin("Kn", T.Kn[:, 16:272], can.indirect(T.vl[:]), -1.0, 2048.0, [CAN, "vl"], ["Kn"])
        tn = "Kt%d" % t
        for h in range(2):
            t_(tn, lambda B, h=h: turned(B, T.Kn, range(8 * h, 8 * h + 8)), ["Kn", "Knp", "I16"])
        lin("Ku", T.Ku[:], lambda B: B[:, 0:256], -1.0, 2048.0, [], ["Ku"], tn)
        quads = [(k0 // 4 + j) % 4 for j in range(4)]
        for j, c in enumerate(quads):
            how = {"scale": -1.0} if j < 4 - ADDED else {"scale": T[sv][:, 2:3], "bias": T[sv][:, 3:4]}
            s(lambda c=c, how=how: act(T.xg[:, 1024 * c:1024 * c + 1024], T.X[:, 0:4096].indirect(T[Gu][:, 64 * c:64 * c + 64]), AF.Identity, **how),
              XC + [Gu, sv], ["xg_%d" % (2 * c), "xg_%d" % (2 * c + 1)])
        if last:
            for c, e in enumerate(UNBIAS):
                a, b = 1024 * c, 1024 * c + 1024
                if e == "a":
                    op("g", [lambda a=a, b=b: g.dma_start(T.XO[:, a:b], T.X[:, a:b], accum_op=A.add)], [XC[c], XOC[c]], ["add%d" % c, XOC[c]],
                       sem="add%d" % c, cnt=16)
                else:
                    lin("", T.XO[:, a:b], T.X[:, a:b], 1.0, -BIAS, [XC[c]], ["XO", XOC[c]], e=e)
        elif t >= 2 and UNBIAS[t - 2:t - 1] == "a":
            iota(XOC[t - 2], T.XO[:, 1024 * (t - 2):1024 * (t - 1)], [[0, 1024]], -int(BIAS), 0)
        pick(It, T[It][:], T.I16[:], ["I16"], [[0, 8], [1, 16]], A.not_equal, -t, 0)
        lin("cw", T.cw[:], can.indirect(T[cwl][:]), -1.0, 2048.0, [CAN, cwl], ["cw"])
        for nm, n, src in (("Zb", 256, Z), ("Zc", 512, "Zb"))[:max(w for _, w in SCORES) - 1]:
            copy(nm, T.Z[:, z0 + n:z0 + 2 * n], T.Z[:, z0:z0 + n], [Z, src], n)
        tn = "key%d" % t
        t_(tn, lambda B: [(B[:, 0:256], T.krow[0:1, :], T.ones[0:1, :], True, False)]
           + [(B[:, 128 * h:128 * h + 128], T.Kn[:, 16 + 128 * h:144 + 128 * h], T.I16[:], False, False) for h in range(2)],
           ["k2047", "ones", "Kn", "I16", "Ku"], [tn])
        k1 = 0
        for c, (n, w) in enumerate(SCORES):
            op("v", [lambda k=k, w=w: V.tensor_tensor(T.sc[:, 256 * k:256 * (k + w)], T.X[:, 0:4096].indirect(T.Ku[:, 16 * k:16 * (k + w)]),
                                                      T.Z[:, z0:z0 + 256 * w], A.max) for k in range(k1, k1 + n, w)],
               XC + ["Ku", Z] + ["Zb", "Zc", "Zc"][:w - 1], ["sc%d" % c])
            t_(tn, lambda B, ks=range(k1, k1 + n): [(B[:, 128 * h + k:128 * h + 128:16], T.sc[:, 256 * k + 128 * h:256 * k + 128 * h + 128], T.blkS[:],
                                                     False, k == 15 and h == 1) for k in ks for h in range(2)], ["sc%d" % c, "blkS", tn], [tn])
            k1 += n
        vp(lambda B: V.tensor_tensor_scan(T.sco[:], T.resetv[:], B[:, 0:256], 0.0, A.add, A.max), tn, ["resetv"], ["sco"])
        v(lambda: ts(T.q2[:, 0:16], T.sco[:, 15:256:16], 4095, None, A.bitwise_and), ["sco"], ["q2"])
        lin("Lc", T.Lc[:], T.q2[:, 0:16], 1.0, -2047.0, ["q2"], ["Lc"])
        lin("Lx", T.Lx[:], T.q2[:].indirect(T.lx[:]), 1.0, -2047.0, ["q2", "q2p", "lxa", "lxb"], ["Lx"])
        v(lambda: V.tensor_tensor(T.A1[:], T.Lc[:].indirect(T.zl[:]), T.dmask[:], A.mult), ["Lc", "zl", "dmask"], ["A1"])

        def wrapped(B, o):
            return [(B[:, o + 8 * h:o + 8 * h + 8], T.A1[:, 128 * h:128 * h + 128], T.blk1[:]) for h in range(2)]
        t_("cW%d" % t, lambda B: group(wrapped(B, 0), True, True), ["A1", "blk1"])
        lin("cu", T.cu[:], lambda B: B[:, 0:16], -1.0, 2048.0, [], ["cu"], "cW%d" % t)
        if not last:
            lin("vl", T.vl[:], lambda B: B[:, 0:16], -0.25, 511.625, [], ["vl"], "cW%d" % t)
        if t:
            op("g", [lambda: g.affine_select(T.At[:, t - 1:256:16], T.ones[:, 0:16], [[0, 16]], A.is_gt, 0.0, 0, 0)], ["ones"], ["Az", "At"])
        copy("At", T.At[:, t:256:16], T.Lc[:], ["Lc", "At"], 16)
        lin("xc", T.xc[:], T.X[:, 0:4096].indirect(T.cu[:]), 0.5, (BIAS if last else -BIAS) / 2 - 0.25, XC + ["cu"], ["xc"])
        if not last:
            snt, arr = "snt%d" % (t + 1), "arr%d" % (t + 1)
            parts("ZS", t, lambda B: [(B[:, 0:256], T.Ih[:], zz)], ["Ih", Z], lambda B: [(B[:, 0:256], T.Ib[:], T.xc[:])], ["Ib", "xc"])
            lin("zs", T.ZS[:, 256 * t:256 * t + 256], lambda B: B[:, 0:256], 1.0, BIAS / 2, [], ["zs%d" % t], "ZS%d" % t)
            dst = T.cores[(rank + 1 + t % 3) % len(T.cores)]
            rid, pid = topo.addr(dst)[0], topo.addr(dst)[1]
            ne = len(topo.engines(core, dst))
            op("g", [lambda: g.remote_dma(T.Z[:, z0 + 1024:z0 + 1280], T.ZS[:, 256 * t:256 * t + 256], T.sem[arr], T.sem[snt], pid=pid, routing_id=rid,
                                          dma_engine_mask=topo.mask(core, dst))], ["zs%d" % t], ["way%d" % t], sem=snt, cnt=ne)
            op("x", [], ["way%d" % t], ["Z%d" % (t + 1)], sem=arr, cnt=ne)
        t_("D%d" % t, lambda B: [(B[:, 0:384], T.I16[:], T.tri[:], True, False)], ["I16", "tri", "triz", Z], ["Dt"])
        parts("D", t, lambda B: [(B[:, j:384:16], T.In16[:], T.Lx[:, 0:24]) for j in range(16)], ["In16", "Lx", "Dt"],
              lambda B: [(B[:, 0:256], T.BLK[:, 0:128], T.A1[:])]
              + [(B[:, 256:384], T.BLK[:, 128 * h + 128:128 * h + 256], T.A1[:, 128 * h:128 * h + 128]) for h in range(2)],
              ["A1", "BLKa", "BLKb", "BLKc"], start=False)
        vp(lambda B: ts(T.eqc[:], B[:, 0:384], 0.0, None, A.is_equal), "D%d" % t, [], ["eqc"])
        t_("yc%d" % t, lambda B: group(wrapped(B, 16) + [(B[:, 16 + 8 * h:24 + 8 * h], T.eqc[:, a:a + 128], T.WN[:, o:o + 8])
                                                         for h in range(2) for a, o in ((128 * h, 16), (256, 8 * h))], True, True),
           ["A1", "blk1", "eqc", "WN", "WNb"])
        vp(lambda B: V.tensor_tensor(T.yc[:], B[:, 16:32], T.dum[:, 32:48], A.max), "yc%d" % t, ["dumc"], ["yc"])
        lin("dcu", T.dcu[:], T.yc[:], -1.0, 2048.0, ["yc"], ["dcu"])
        for j, c in enumerate(quads[:4 - ADDED]):
            pairs = sorted((2 * c, 2 * c + 1), key=lambda b: b != k0 // 2)
            for b in pairs:
                tn = "d%d_%d" % (t, b)
                t_(tn, lambda B, b=b: group([(B[:], T[sI][:], T.xg[:, 512 * b:512 * b + 512])] + [(B[:, o:o + 256], T[sI][:], zz) for o in (0, 256)],
                                            True, True), [sI, Z, "xg_%d" % b])
                sp(lambda B, b=b: act(T.ab[:, 512 * b:512 * b + 512], B[:], AF.Abs), tn, [], ["ab%d" % b])
            for run in ([pairs] if j else [[b] for b in pairs]):
                a, e = 512 * min(run), 512 * max(run) + 512
                v(lambda a=a, e=e: ts(T.th[:, a:e], T.ab[:, a:e], 16.0, None, A.is_gt), ["ab%d" % b for b in run], ["th%d" % b for b in run])
        lin("zq", T.zq[:, 0:256], zz, T[sv][:, 0:1], T[sv][:, 1:2], [Z, sv], ["zq"])
        for nm, n, src in (("zqb", 256, "zq"), ("zqc", 512, "zqb")):
            copy(nm, T.zq[:, n:2 * n], T.zq[:, 0:n], ["zq", src], n)
        for j, c in enumerate(quads[4 - ADDED:]):
            a, xs = 1024 * c, ["xg_%d" % (2 * c), "xg_%d" % (2 * c + 1)]
            op("g", [lambda a=a: g.dma_start(T.xg[:, a:a + 1024], T.zq[:], accum_op=A.add)], ["zq", "zqb", "zqc"], ["dd%d" % j] + xs,
               sem="dd%d" % j, cnt=16 * (t + 1))
            v(lambda a=a: ts(T.th[:, a:a + 1024], T.xg[:, a:a + 1024], GRID, GRID, A.add, A.not_equal), xs, ["td", "th%d" % (2 * c), "th%d" % (2 * c + 1)])
        for h in range(2):
            tn, o = "cn%s%d" % ("ab"[h], t), 256 + 128 * h
            for c in quads:
                t_(tn, lambda B, c=c, o=o: [(B[:, o + k:o + 128:16], T.th[:, 256 * k + o - 256:256 * k + o - 128], T.blkb[:, 32:40], True, True)
                                            for k in range(4 * c, 4 * c + 4)], ["th%d" % (2 * c), "th%d" % (2 * c + 1), "blkb"])
            sp(lambda B, h=h, o=o: act(T.sg[:, 128 * h:128 * h + 128], B[:, o:o + 128], AF.Sign, bias=-8.5), tn, [], ["sg_%d" % h])
        tn = "Pw%d" % t
        t_(tn, lambda B: [(B[0:40, 256:512], T.blkb[:], T.th[:, 256 * k0:256 * k0 + 256], False, True)], ["th%d" % (k0 // 2), "blkb", "blkz", tn], ["sk", tn])
        sp(lambda B: act(TW[0:40, 0:256], B[0:40, 256:512], AF.Sign, bias=bar, accum_out=T.acc[0:40, :]), tn, ["bar", "barb"], ["TW", "acc"])
        copy("TWd", TW[0:8, 256:512], TW[0:8, 0:256], ["TW"], 256)
        if not last:
            tn = "S%d" % t
            t_(tn, lambda B: [(B[:, 64:65], T.c32[0:40, :], T.acc[0:40, :], True, True)], ["c32", "c32b", "acc"])
            lin("si", T.si[:], lambda B: B[:, 64:65], -5.0, 1535.625 + 5 * (0.97 - 307.2), [], ["si"], tn)
            vp(lambda B: ts(T.s0[:], T.si[:], 0.2, B[:, 64:65], A.mult, A.add), tn, ["si"], ["s0"])
            lin("sI", T[sI1][:], T.Ib[:], T.s0[:], 0.0, ["Ib", "s0"], [sI1])
            lin("sv", T[sv1][:], T.cc[:], T.s0[:], 0.0, CC + ["s0"], [sv1])
        t_("yw%d" % t, lambda B: group([(B[:, 32:64], T.I16[:], T[wW][:])]
                                       + [(B[:, 32:64], T.WB[0:40, 15 - b:143 - b], TW[0:40, b:512:16]) for b in range(16)], True, True),
           ["wU%d" % p, wW, "I16", "TW", "TWd", "WB", "WBb"])
        vp(lambda B: V.tensor_tensor(T.yw[:], B[:, 32:64], T.dum[:, 0:32], A.max), "yw%d" % t, ["dum"], ["yw"])
        lin("dwl", T.dwl[:], T.yw[:], -1.0, 2048.0 + 2 * BIG, ["yw"], ["dwl"])
        for h in range(2):
            tn, a, b = "G%s%d" % ("ab"[h], t), 128 * h, 128 * h + 128
            t_(tn, lambda B, a=a, b=b: group([(B[:, 0:128], T[It][:], T.Kn[:, 16 + a:16 + b]), (B[:, 128:256], T[It][:], T[Gn][:, 16 + a:16 + b]),
                                              (B[:, 128:256], T.krow[32:33, :], T.ones[32:33, 0:128]),
                                              (B[:, 384:512], T.I16[:], T[Gn][:, 16 + a:16 + b])], True, False),
               [It, "Kn", "%s_%d" % (Gn, h), "kB", "ones", "I16"], ["Ge_%d" % h])
            t_(tn, lambda B, a=a, b=b: [(B[:, 256:384], T.I16[:], T.cw[:, a:b], False, False)], ["I16", "cw", "Ge_%d" % h], ["Ne_%d" % h])
            t_(tn, lambda B, a=a, b=b: [(B[:, o:o + 128], T.At[:, a:b], T.I16[:], False, False) for o in (0, 128)], ["At", "I16", "Ge_%d" % h], ["Gt_%d" % h])
            t_(tn, lambda B, a=a, b=b: [(B[:, 128 * j:128 * j + 128], T.sg[:, a:b], m[:], False, j == 3) for j, m in enumerate((T.IBp, T.IBn, T.IBn, T.IBp))],
               ["sg_%d" % h, "IBp", "IBn", "Ne_%d" % h, "Gt_%d" % h], ["G_%d" % h])
            lin("ga", T.ga[:, a:b], lambda B: B[:, 0:128], 1.0, -BIG, [], ["ga_%d" % h], tn)
            vp(lambda B, a=a, b=b: V.tensor_tensor(T[Gn1][:, 16 + a:16 + b], T.ga[:, a:b], B[:, 128:256], A.max), tn, ["ga_%d" % h], ["%s_%d" % (Gn1, h)])
            lin("cf", T.cf[:, 2 * a:2 * b], lambda B: B[:, 256:512], -1.0, 2048.0 - BIG, ["G_%d" % h], ["cf_%d" % h], "N%s%d" % ("ab"[h], t))
            v(lambda h=h, a=a: V.tensor_tensor(T.CAN[:].indirect(T.dwl[:, 8 * h:8 * h + 8]), T.cf[:, 2 * a:2 * a + 128], T.cf[:, 2 * a + 128:2 * a + 256],
                                               A.max), ["cf_%d" % h, "dwl"], ["CAN"])
        xw, XG = T.xg[:, 256 * k0:256 * k0 + 256], "xg_%d" % (k0 // 2)
        lin("r", T.r1[:], xw, 1.0, BIAS + 59.0, [XG], ["r1"], relu=True)
        parts("R", t, lambda B: [(B[:, 256:512], T.Ihn[:], xw), (B[:, 256:512], T.Ih[:], zz), (B[:, 0:256], T.Ibn[:], T.r1[:])],
              [XG, "Ihn", "Ih", "Ibn", Z, "r1"],
              lambda B: [(B[:, 256:512], T.E8[32:40, :], TW[32:40, 0:256]), (B[:, 0:256], T.RA[0:40, :], TW[0:40, 0:256])], ["E8", "RA", "RAb", "TW"])
        lin("rf", T.rf[:], lambda B: B[:], 1.0, -512.25, [], ["rf"], "R%d" % t, relu=True)
        win, names, o = (T.XO, XOC, 32) if last else (T.X, XC, 0)
        if last:
            lin("rn", T.rf[:, 0:256], T.rf[:, 0:256], 1.0, -BIAS, ["rf"], ["rn", "rf"])
        v(lambda: V.tensor_tensor(win[:].indirect(T.dwl[:, 16:32]), T.rf[:, 0:256], T.rf[:, 256:512], A.add), ["rf", "dwl"], ["X"] + names)
        for a in range(8):
            v(lambda a=a: V.tensor_tensor(win[:].indirect(T.dcu[:, 2 * a:2 * a + 2]), T.xc[:, 32 * a:32 * a + 32], T.c160[:, o:o + 32], A.add),
              ["xc", "dcu", "c160", "c160n"], ["cut"] + names)
        if not last:
            now[0] = t + 1
            firsts(t + 1)

    for t in range(NT):
        now[0] = t
        step(t)
    now[0] = None

    def store(name, out, src, R):
        op("y", [lambda: Y.dma_start(out, src)], R, ["y" + name], sem="st_" + name, cnt=16)

    store("ox", T.yx[:], T.XO[:, 0:4096], XOC)
    lin("", T.go[:], T["Gn%d" % (NT % 2)][:, 16:272], -1.0, 2048.0, ["Gn%d_%d" % (NT % 2, h) for h in range(2)], ["go"], e="s")
    store("og", T.yg[:], T.go[:], ["go"])
    store("ol", T.yl[:], T.CAN[:, 0:1024], ["CAN"])
    return ops


def depend(ops):
    last, readers, tiles = {}, {}, {}
    for o in ops:
        d = set()
        for r in o["R"]:
            d.update(last.get(r, ()))
        for w in o["W"]:
            d.update(last.get(w, ()))
            d.update(readers.get(w, ()))
        for r in o["R"]:
            readers.setdefault(r, []).append(o["i"])
        for w in o["W"]:
            last[w] = [o["i"]]
            readers[w] = []
        if o["tile"]:
            tl = tiles.setdefault(o["tile"], [None, [], []])
            if tl[0] != o["e"]:
                tl[0], tl[1], tl[2] = o["e"], tl[2], []
            d.update(tl[1])
            tl[2].append(o["i"])
        d.discard(o["i"])
        o["d"], o["s"] = d, []
        for j in d:
            ops[j]["s"].append(o["i"])
        o["n"] = "".join(c for c in (o["W"] or [o["tile"]])[0] if c.isalpha()) + "_" + (o["e"] if o["t"] is not None else o["e"].upper())
        kind = "".join(c for c in o["tile"] or "" if c.isalpha())
        o["bank"] = SHARE[kind] + o["tile"][len(kind):] if kind in SHARE and kind != o["tile"] else o["tile"]


def dues(ops, phase):
    due, seen = [], {}
    first = min(o["i"] for o in ops if o["t"] is not None)
    for o in ops:
        t, name = o["t"], o["n"]
        o["k"] = k = seen.get((t, name), 0)
        seen[(t, name)] = k + 1
        o["by"] = 2 if (t == 0 or o["i"] < first) and k in phase[2].get(name, ()) else 1 if t == NT - 1 and k in phase[1].get(name, ()) else 0
        if t is None and o["by"] == 0:
            due.append(o["i"] - 1000.0)
        else:
            due.append(max(PERIOD * (t or 0) + phase[o["by"]][name][k], AHEAD if t else -PERIOD))
    return due


def place(ops, due):
    users = {}
    for o in ops:
        if o["tile"]:
            users.setdefault(o["bank"], []).append(o["i"])
    left = {k: len(u) for k, u in users.items()}
    bank, extra, last = {}, {}, {}
    free = {k: [] for k in range(8)}
    need = [len(o["d"]) for o in ops]
    ready = sorted((due[i], i) for i in range(len(ops)) if need[i] == 0)
    order = []
    while ready:
        p = 0
        while ops[ready[p][1]]["tile"] and ops[ready[p][1]]["bank"] not in bank and not free:
            p += 1
            if p == len(ready):
                raise ValueError("no bank for any ready op")
        i = ready.pop(p)[1]
        tl = ops[i]["bank"]
        if tl:
            if tl not in bank:
                bank[tl] = list(free)[0]
                extra[i] = free.pop(bank[tl])
            elif ops[last[tl]]["e"] != ops[i]["e"]:
                extra[i] = [last[tl]]
            last[tl] = i
            left[tl] -= 1
            if left[tl] == 0:
                free[bank[tl]] = users[tl]
        order.append(i)
        for j in ops[i]["s"]:
            need[j] -= 1
            if need[j] == 0:
                ready.append((due[j], j))
                ready.sort()
    return order, bank, extra


def emit(g, T, ops, order, bank, extra):
    Q = {"v": g.vector, "s": g.scalar, "t": g.tensor, "g": g, "y": g.sync}
    known = {e: {} for e in Q}
    count, done = {}, {}
    at = {i: p for p, i in enumerate(order)}
    for i in order:
        o = ops[i]
        e = o["e"]
        if e == "x":
            done[i] = (o["sem"], o["cnt"], {})
            continue
        kn = known[e]
        for j in sorted(set(o["d"]) | set(extra.get(i, ())), key=lambda j: -at[j]):
            sm, c, snap = done[j]
            if c > kn.get(sm, 0):
                Q[e].wait_ge(T.sem[sm], c)
                kn[sm] = c
                for a, b in snap.items():
                    if b > kn.get(a, 0):
                        kn[a] = b
        if e == "g" and count.get("qg", 0) > kn.get("qg", 0):
            kn["qg"] = count["qg"]
            g.wait_ge(T.sem["qg"], kn["qg"])
        for f in (o["f"](T["ps%d" % bank[o["bank"]]]) if o["tile"] else o["f"]):
            r = f()
            if o["sem"] is None:
                count["q" + e] = count.get("q" + e, 0) + 1
                r.then_inc(T.sem["q" + e], 1)
            elif not o["sem"].startswith("snt"):
                r.then_inc(T.sem[o["sem"]], 16)
        done[i] = (o["sem"] or "q" + e, o["cnt"] or count.get("q" + e, 0), dict(kn))
    for sm in sorted(count):
        g.wait_ge(T.sem[sm], count[sm])
    for o in ops:
        if o["sem"] is not None:
            g.wait_ge(T.sem[o["sem"]], o["cnt"])
